import numpy as np, ml_dtypes
CORES = [16,18,20,22]
N = 4
BF = ml_dtypes.bfloat16
def gentries(a):
    return np.ascontiguousarray(a.reshape(8, 16, -1).transpose(0, 2, 1)).reshape(8, -1)
def gtable(e):
    e = np.asarray(e); return np.ascontiguousarray(e.reshape(8, -1, 16).transpose(0, 2, 1)).reshape(128, -1).astype(np.int32)
E, G, M, S, R = 2048, 256, 256, 2, 5
V, W = S * M, E + (N - 1) * G
def pick(rng, shape, lo, hi):
    return np.where(rng.random(shape) < 0.5, lo, hi)
def parts(rng):
    a = np.minimum((16 * (0.25 + 0.75 * rng.random((N, 8, 1, E))) * rng.random((N, 8, 16, E))).astype(np.int64), 15)
    hot = rng.integers(0, W, (N, 8, 128)); hot[..., :64] = rng.integers(0, V, (N, 8, 64))
    h = np.take_along_axis(hot, rng.integers(0, 128, (N, 8, V * 16)), 2).reshape(N, 8, V, 16)
    return {"a": a, "k": rng.integers(0, 8, (N, 8, 16, 2048)), "be": np.exp2(-10 + 3 * rng.random((N, 8, 16))),
            "ti": rng.integers(0, 1024, (N, 8, E)), "kd": rng.integers(0, 8, (N, 8, E)), "cl": rng.integers(0, 16, (N, 8, V)), "bg": rng.integers(0, 4096, (N, 8, V)), "us": rng.integers(0, 256, (N, 8, R * M)),
            "lp": np.where(rng.random((N, 8, E)) < 0.25, -1, rng.integers(0, W, (N, 8, E))),
            "ca": np.where(rng.random((N, 8, V, 16)) < 0.4, h, rng.integers(0, W, (N, 8, V, 16))),
            "snd": np.ascontiguousarray(np.argsort(rng.random((N, 8, N - 1, E)), axis=-1)[..., :G])}
def pack(p):
    d = {"a0": p["a"].reshape(N, 128, E).astype(np.float32).astype(BF), "k0": p["k"].reshape(N, 128, 2048).astype(np.float32).astype(BF), "be": p["be"].reshape(N, 128, 1).astype(np.float32)}
    for k in ("ti", "kd", "cl", "bg", "us", "lp"): d[k] = p[k].astype(np.int32)
    d["ca"] = np.stack([gtable(x.reshape(8, -1)) for x in p["ca"]]); d["snd"] = np.stack([gtable(x.reshape(8, -1)) for x in p["snd"]])
    return d
def setup_inputs(rng):
    return pack(parts(rng))
def setup_inputs_spread(rng):
    p = parts(rng)
    p["a"] = np.minimum((16 * np.exp2(-3 * rng.random((N, 8, 1, E))) * rng.random((N, 8, 16, E))).astype(np.int64), 15)
    p["k"] = np.minimum((8 * np.exp2(-2 * rng.random((N, 8, 1, 2048))) * rng.random((N, 8, 16, 2048))).astype(np.int64), 7)
    for k, n, e in (("ti", 1024, 3.0), ("bg", 4096, 4.0), ("us", 256, 0.5), ("cl", 16, 2.0), ("ca", W, 2.0)):
        p[k] = np.minimum((n * rng.random(p[k].shape) ** e).astype(np.int64), n - 1)
    p["lp"] = np.where(rng.random((N, 8, E)) < 0.5, -1, rng.integers(0, W, (N, 8, E)))
    r = int(rng.integers(0, N)); p["be"][r] = 2.0 ** -7
    p["ti"][r, :, :V] = rng.integers(0, 48, (8, V)); p["ti"][r, :, V:] = rng.integers(976, 1024, (8, E - V))
    tw = ghosts(p["ti"][:, :, None], p["snd"])[r, :, 0]
    for g in range(8):
        far = np.flatnonzero(tw[g] >= 976)
        p["ca"][r, g] = rng.choice(far, (V, 16)); p["lp"][r, g] = np.where(p["lp"][r, g] < 0, -1, rng.choice(far, E))
    return pack(p)
def setup_inputs_ends(rng):
    p = parts(rng)
    s = rng.random((N, 8, 1, E)); p["a"] = np.where(s < 0.25, 0, np.where(s < 0.5, 15, pick(rng, (N, 8, 16, E), 0, 15)))
    s = rng.random((N, 8, 1, 2048)); p["k"] = np.where(s < 0.25, 0, np.where(s < 0.5, 7, pick(rng, (N, 8, 16, 2048), 0, 7)))
    p["a"][:, ::2, :, 0] = 15; p["a"][..., 2] = 0; p["a"][..., E - 1] = 15
    for j in (0, 63, 1984, 2047): p["k"][..., j] = 7
    p["k"][..., 1991] = 0
    p["be"] = pick(rng, (N, 8, 16), 2.0 ** -10, 2.0 ** -7)
    for k, lo, hi in (("ti", 0, 1023), ("kd", 0, 7), ("us", 0, 255), ("lp", -1, W - 1)):
        p[k] = np.where(rng.random(p[k].shape) < 0.8, pick(rng, p[k].shape, lo, hi), p[k])
    p["cl"] = pick(rng, (N, 8, V), 0, 15); p["bg"] = pick(rng, (N, 8, V), 0, 4095)
    for j in (0, V - 1, E - 1): p["kd"][..., j] = 7
    p["ti"][..., 0] = 1023; p["ti"][..., V - 1] = 0; p["ti"][..., E - 1] = 1023
    p["bg"][..., V - 1] = 4095 * ((np.arange(N)[:, None] + np.arange(8)[None, :]) % 2)
    at = (rng.random((N, 8, V, 1)) < 0.45) | (rng.random((N, 8, V, 16)) < 0.4)
    p["ca"] = np.where(at, pick(rng, (N, 8, V, 16), 0, W - 1), rng.integers(0, W, (N, 8, V, 16)))
    p["ca"][:, :, 0] = W - 1; p["ca"][:, :, V - 1] = W - 1; p["ca"][:, :, 1] = 2
    both = np.concatenate([np.arange(G // 2), np.arange(E - (G - G // 2), E)])
    s = both[np.argsort(rng.random((N, 8, N - 1, G)), axis=-1)]; j = np.argmax(s == E - 1, axis=-1)[..., None]
    np.put_along_axis(s, j, s[..., -1:].copy(), -1); s[..., -1] = E - 1
    p["snd"] = s
    return pack(p)
def setup_inputs_corners(rng):
    p = parts(rng)
    for r in range(N):
        for g in range(8):
            x = (g + r) % 8
            for k, cap, n, kind in (("a", 15, E, x % 4), ("k", 7, 2048, (x // 2) % 4)):
                if kind == 0: p[k][r, g] = cap - rng.integers(0, 2, (16, n))
                elif kind == 1: p[k][r, g] = rng.integers(0, 2, (16, n))
                elif kind == 2: p[k][r, g] = np.broadcast_to(pick(rng, (1, n), 0, cap), (16, n))
    e = np.broadcast_to(np.arange(E), (N, 8, E)); o = rng.integers(0, 8, (N, 8, E))
    p["lp"] = np.choose(o, [np.full_like(e, -1), e, (e + 1) % E, np.zeros_like(e), np.full_like(e, E - 1), np.full_like(e, E), np.full_like(e, W - 1), p["lp"]])
    v = np.broadcast_to(np.arange(V)[:, None], (N, 8, V, 16)); o = rng.integers(0, 10, (N, 8, V, 16))
    for i, c in enumerate((0, V - 1, E - 1, E, W - 1)): p["ca"] = np.where(o == i, c, p["ca"])
    p["ca"] = np.where(o == 5, v, p["ca"])
    p["us"] = rng.choice(np.array([0, 1, 127, 128, 254, 255]), (N, 8, R * M)); p["bg"] = rng.choice(np.array([0, 0, 0, 1, 4094, 4095]), (N, 8, V))
    return pack(p)
def setup_inputs_crowd(rng):
    p = parts(rng); h = int(rng.integers(0, N)); x = rng.integers(V, E, 8); x[0] = E - 1; x[1] -= x[1] % 2; x[3] = 0
    tv = rng.integers(100, 900, 8); kv = rng.integers(0, 8, 8); cv = rng.integers(0, 16, 8)
    for g in range(8):
        p["a"][h, g, :, x[g]] = np.maximum(p["a"][h, g, :, x[g]], 1); p["a"][h, g, cv[g], x[g]] = 1
        for d in range(1, N):
            row = p["snd"][h, g, d - 1]; j = np.flatnonzero(row == x[g])
            if j.size: row[j[0]] = row[G - 1]
            row[G - 1] = x[g]
    for r in range(N):
        for g in range(8):
            w = g if r == h else (g - 1) % 8
            if w == 7: continue
            c = int(x[w]) if r == h else E + ((r - h) % N - 1) * G + G - 1
            p["ti"][r, g, :V] = tv[w]; p["kd"][r, g, :V] = kv[w]; p["bg"][r, g] = 0; p["k"][r, g] = np.maximum(p["k"][r, g], 1)
            if w % 2 == 0: p["cl"][r, g] = cv[w]
            if w == 6: p["ca"][r, g] = rng.choice(np.array([0, c, E, W - 1]), (V, 16)); continue
            p["ca"][r, g] = c
            if w >= 3:
                for s in range(S):
                    i = (0, M - 1, int(rng.integers(0, M)))[w - 3]; p["ca"][r, g, s * M + i] = rng.integers(0, W, 16)
    for g in range(7):
        if x[g] >= V: p["ti"][h, g, x[g]] = tv[g] + rng.integers(0, 65)
    p["cl"][h, 1, ::M] = cv[1]
    q = (h + 1) % N; i = np.arange(M); n = min(G, M); ev = p["snd"][h, 7, 0, :n]; o = V + i[n:]
    tc = 400 + 32 * (i >> 6) + rng.integers(0, 32, M); kc = (i >> 3) % 8
    p["ti"][q, 0, :V] = 400; p["kd"][q, 0, :V] = np.tile(i % 8, S); p["bg"][q, 0] = 0; p["k"][q, 0] = rng.integers(1, 3, (16, 2048))
    p["ca"][q, 0] = np.tile(np.where(i < n, E + i, V + i), S)[:, None]; p["lp"][q, 0, o] = -1
    for b, g, c, lo, hi in ((h, 7, ev, 0, n), (q, 0, o, n, M)):
        p["a"][b, g][:, c] = rng.integers(1, 3, (16, hi - lo)); p["ti"][b, g, c] = tc[lo:hi]; p["kd"][b, g, c] = kc[lo:hi]
    return pack(p)
def setup_inputs_calm(rng):
    p = parts(rng)
    for r in range(N):
        for g in range(8):
            kind = (g + r) % 4
            if kind == 0: p["a"][r, g] = (np.arange(16)[:, None] == rng.integers(0, 16, (1, E))) & (rng.random((1, E)) < 0.5)
            elif kind == 3: p["a"][r, g] = rng.integers(0, 4, (16, E))
            else: p["a"][r, g] = kind
            p["k"][r, g] = (1, 1, 0, 3)[kind]
            if kind == 2: p["k"][r, g] = rng.integers(0, 3, (16, 2048))
    p["ca"] = rng.integers(0, W, (N, 8, V, 16)); p["us"] = 16 * rng.integers(0, 16, (N, 8, R * M)); p["bg"] = rng.choice(np.array([0, 0, 0, 1, 16, 256]), (N, 8, V))
    r = int(rng.integers(0, N)); p["k"][r, (1 - r) % 4] = 0
    g = 4 + (2 - r) % 4; p["us"][r, g] = 255; p["bg"][r, g] = 4095
    return pack(p)
def check_ranges(d):
    bad = []
    for k, lo, hi in (("a0", 0, 15), ("k0", 0, 7), ("be", 2.0 ** -10, 2.0 ** -7), ("ti", 0, 1023), ("kd", 0, 7), ("cl", 0, 15), ("bg", 0, 4095), ("us", 0, 255), ("lp", -1, W - 1), ("ca", 0, W - 1), ("snd", 0, E - 1)):
        v = np.asarray(d[k]).astype(np.float64)
        if not np.all((v >= lo) & (v <= hi)): bad.append("range of " + k)
        elif k in ("a0", "k0") and np.any(v != np.floor(v)): bad.append("whole numbers of " + k)
    s = np.sort(np.stack([gentries(x) for x in np.asarray(d["snd"])]).reshape(N, 8, N - 1, G), axis=-1)
    if np.any(s[..., 1:] == s[..., :-1]): bad.append("repeated event in a block of snd")
    return bad
def ghosts(x, sl):
    out = []
    for r in range(N):
        w = [x[r]]
        for d in range(1, N):
            q = (r - d) % N
            w.append(np.roll(np.take_along_axis(x[q], sl[q, :, d - 1][:, None, :], 2), 1, axis=0))
        out.append(np.concatenate(w, axis=2))
    return np.stack(out)
def reference(a0, k0, be, ti, kd, cl, bg, us, lp, ca, snd):
    A = a0.astype(np.float32).astype(np.int64).reshape(N, 8, 16, E); K = k0.astype(np.float32).astype(np.int64).reshape(N, 8, 16, 2048)
    beta = be.astype(np.float64).reshape(N, 8, 16, 1); T, D, cls, B, U, L = [v.astype(np.int64) for v in (ti, kd, cl, bg, us, lp)]
    C = np.stack([gentries(x) for x in ca]).astype(np.int64); sl = np.stack([gentries(x) for x in snd]).astype(np.int64).reshape(N, 8, N - 1, G)
    TW = ghosts(T[:, :, None], sl)[:, :, 0]; DW = ghosts(D[:, :, None], sl)[:, :, 0]
    lam = []
    for t in range(R):
        lo = (t % S) * M; AW = ghosts(A, sl)
        c = C[:, :, 16 * lo:16 * (lo + M)]
        lag = np.abs(np.repeat(T[:, :, lo:lo + M], 16, axis=2) - np.take_along_axis(TW, c, 2))
        bn = 64 * (lag >> 5) + 8 * np.repeat(D[:, :, lo:lo + M], 16, axis=2) + np.take_along_axis(DW, c, 2)
        pr = np.take_along_axis(AW, c[:, :, None], 3) * np.take_along_axis(K, bn[:, :, None], 3)
        lam.append(np.add.reduce((np.exp(-beta * lag[:, :, None]) * pr).reshape(N, 8, 16, M, 16), axis=4))
        w = np.add.reduce(pr, axis=2).reshape(N, 8, M, 16); cum = np.add.accumulate(w, axis=3)
        hit = 256 * cum > (U[:, :, t * M:(t + 1) * M] * (B[:, :, lo:lo + M] + cum[..., 15]))[..., None]
        el = np.any(hit, axis=3); first = np.argmax(hit, axis=3)[..., None]
        cc = c.reshape(N, 8, M, 16); par = np.take_along_axis(cc, first, 3)[..., 0]; pb = np.take_along_axis(bn.reshape(N, 8, M, 16), first, 3)[..., 0]
        add = np.zeros_like(A)
        for r in range(N):
            for g in range(8):
                i = np.flatnonzero(el[r, g]); cg = cls[r, g, lo:lo + M]
                col, j = np.unique(par[r, g, i], return_index=True); z = cg[i[j]]; own = col < E
                np.add.at(add, (r, g, z[own], col[own]), 1)
                y = col[~own] - E; d = y // G + 1; q = (r - d) % N; h = (g - 1) % 8
                np.add.at(add, (q, h, z[~own], sl[q, h, d - 1, y % G]), 1)
                if t < R - 1:
                    b, j = np.unique(pb[r, g, i], return_index=True); z = cg[i[j]]
                    K[r, g, z, b] = np.minimum(K[r, g, z, b] + 1, 7)
        A = np.minimum(A + add, 15)
        if t < R - S:
            L[:, :, lo:lo + M] = np.where(el, par, L[:, :, lo:lo + M])
            up = np.where(el & (par < E), np.take_along_axis(L, np.minimum(par, E - 1), 2), -1)[..., None]
            least = np.argmin(w, axis=3)[..., None]
            C[:, :, 16 * lo:16 * (lo + M)] = np.where((np.arange(16) == least) & (up >= 0), up, cc).reshape(N, 8, 16 * M)
    return {"yl": np.concatenate(lam, axis=3).reshape(N, 128, R * M).astype(np.float32), "ya": A.reshape(N, 128, E).astype(np.float32)}

def check_inputs(d):
    bad = list(check_ranges(d))
    if not bad:
        for name, y in reference(**d).items():
            for q in range(N):
                v = np.abs(np.asarray(y[q], np.float64)); s = np.sqrt(np.mean(v * v))
                if v.max() > 9 * s or s < 2.0 ** -6: bad.append('%s of rank %d is uneven or too small' % (name, q))
    return bad

@@ -1,0 +1,561 @@
+import math
+from concourse.bass import DstId, RemoteDMATransfer
+from concourse.mybir import AluOpType as O, ActivationFunctionType as AF
+
+E, M, R = 2048, 256, 5
+XB, FB, DA, AWN = 2048, (2816, 3072, 3584), 4352, 4608
+LB, INV, ILN = 2832, 2816, 4880
+LO = (0, 256, 768)
+CD = 3456
+CH = (0, 64, 128, 192, 256)
+KCUT = (0, 16, 32, 64, 96, 128, 160, 192, 224, 256)
+LAM = 256
+GA = 32
+WHO1, XV, GVA, PASSES = "AAAAAAAA", "AAA", True, 4
+CALL1 = ([(2, 0, 768, 0, 16)], [(1, 0, 512, 0, 16)], [(0, 0, 256, 0, 16)])
+CALL2 = ([(0, 0, 256, 0, 16)], [(1, 0, 512, 0, 16)], [(2, 0, 768, 0, 16)])
+CY, PEC, GAT, SCA, FIX, HOP, LDMA, RDMA, ISS, DISS, FIRST = 1.04e-3, 0.55e-3, 1.56, 3.8, 0.05, 0.1, 2.1, 2.4, 0.3, 0.15, 2.0
+
+SCRATCH = {}
+for _n, _w, _d in (
+        ("AW", AWN, "bfloat16"), ("KW", 2304, "bfloat16"), ("IL", ILN, "bfloat16"), ("PH", E, "bfloat16"), ("AUX", E, "bfloat16"), ("KG", 4096, "bfloat16"),
+        ("PR", 8192, "bfloat16"), ("A0", E, "bfloat16"), ("RG", 8192, "float32"), ("ST", 4096, "float32"), ("TE", 2048, "float32"),
+        ("YL", 1280, "float32"), ("YA", 2048, "float32"), ("XR", 768, "bfloat16"), ("LND", 1536, "bfloat16"),
+        ("XD", 768, "bfloat16"), ("G1", 768, "bfloat16"), ("G2", 768, "bfloat16"), ("IM", 768, "bfloat16"),
+        ("U", 1280, "bfloat16"), ("OH", 512, "bfloat16"), ("NOH", 512, "bfloat16"), ("C7", 512, "bfloat16"),
+        ("FX0", 1024, "float16"), ("FX1", 1024, "float16"), ("E15", 512, "float32"), ("W16", 512, "float16"), ("T1", 256, "float32"),
+        ("HIT", 256, "bfloat16"), ("SEL", 768, "float16"), ("REP", 512, "float16"), ("VL", 96, "float32"), ("SD", 768, "float32"),
+        ("TN", 512, "float32"), ("TI", 16, "int32"), ("MB", 16, "bfloat16"), ("M8", 256, "bfloat16"), ("MK", 512, "float32"), ("TT", 512, "float32"),
+        ("GV", 256, "bfloat16"), ("GK", 256, "bfloat16"), ("TMP", 256, "bfloat16"), ("TMQ", 256, "bfloat16"), ("UP", 256, "bfloat16"),
+        ("AB", 768, "float32"), ("HI", 768, "bfloat16"),
+        ("cI", 512, "uint16"), ("cA", 512, "uint16"), ("cB", 512, "uint16"), ("cR", 512, "uint16"), ("uS", 48, "uint16"), ("uT", 192, "uint16"),
+        ("uL", 128, "uint16"), ("uY", 128, "uint16"), ("CA", 512, "int32"), ("CF", 512, "float32"), ("SN", 48, "int32"), ("BE", 2, "float32"),
+        ("DI", 528, "int32"), ("DH", 704, "int32"), ("DB", 816, "bfloat16"), ("Z", 128, "bfloat16"),
+        ("IO", 144, "float32"), ("J", 144, "float32"), ("BK", 128, "bfloat16"), ("B2", 1024, "bfloat16"), ("I32", 128, "float32"),
+        ("KI", 2, "int32"), ("KC", 32, "float32"), ("M16", 16, "float32"), ("M2", 8, "float32"), ("I64", 64, "float32"),
+        ("JJ", 256, "float32"), ("CM", 256, "bfloat16"), ("RS", 256, "float32"), ("RM", 256, "float32"), ("DU", 64, "float32"),
+        ("H0", 264, "float32"), ("H1", 264, "float32"), ("H2", 264, "float32"), ("SQ", 8, "float32"), ("G8", 128, "float32"),
+        ("CT", 1024, "bfloat16"), ("YB", 6 * 144, "bfloat16"), ("Y16", 144, "float16"), ("MBF", 27 * 128, "bfloat16"), ("MF", 6 * 128, "float16")):
+    SCRATCH[_n] = ("sbuf", [128, _w], _d)
+SCRATCH["EQ"] = ("sbuf", [128, 32, 256], "bfloat16")
+for _n in range(8):
+    SCRATCH["P%d" % _n] = ("psum", [128, 512], "float32")
+NDMA = 40
+SEMAPHORES = ["eV", "eA", "eP", "eG"] + ["d%d" % _n for _n in range(NDMA)] + [_a + str(_n) for _a in ("a", "x", "n", "la", "lx", "ln") for _n in range(3)]
+
+
+def S(name, c0=0, c1=None, step=1, p=(0, 128, 1)):
+    return (name, p, c0, SCRATCH[name][1][1] if c1 is None else c1, step)
+
+
+def orders(T, topo):
+    n = len(T.cores)
+    return [sorted([(q + d) % n for d in range(1, n)], key=lambda r: (topo.die(T.cores[r]) == topo.die(T.cores[q]), (r - q) % n != 2, (r - q) % n)) for q in range(n)]
+
+
+def hazards(ops, pe_chain):
+    recs, out = {}, []
+    for i, o in enumerate(ops):
+        dep = set()
+        acc = []
+        for d, wr in [(d, False) for d in o["r"]] + [(d, True) for d in o["w"]]:
+            pm = 0
+            for x in range(*d[1]):
+                pm |= 1 << x
+            acc.append((d, wr, pm))
+            ps = SCRATCH[d[0]][0] == "psum"
+            for (m2, a, b, j, w2) in recs.get(d[0], []):
+                same = ops[j]["q"] == o["q"]
+                if same and o["q"] == "P":
+                    if pe_chain and ps: dep.add(j)
+                elif (ps and not same) or ((wr or w2) and (m2 & pm) and a < d[3] and d[2] < b):
+                    dep.add(j)
+        for d, wr, pm in acc:
+            l = recs.setdefault(d[0], [])
+            if SCRATCH[d[0]][0] == "psum":
+                if l and ops[l[-1][3]]["q"] != o["q"]:
+                    l[:] = [e for e in l if ops[e[3]]["q"] == ops[l[-1][3]]["q"]]
+                elif l and o["q"] == "P":
+                    l.pop()
+            elif wr and d[4] == 1:
+                l[:] = [e for e in l if not ((e[0] & ~pm) == 0 and e[1] >= d[2] and e[2] <= d[3])]
+            l.append((pm, d[2], d[3], i, wr))
+        out.append(dep)
+    return out
+
+
+def arrange(ops):
+    n = len(ops); pre = hazards(ops, True)
+    for i, o in enumerate(ops):
+        pre[i] |= set(o["after"])
+
+    def lat(j, i):
+        a, b = ops[j], ops[i]
+        if a["q"] is None: return HOP
+        if b["q"] is None: return a["lat"]
+        if a["q"] == b["q"] and (a["q"] == "P" or (a["q"] == "G" and j in b["after"])): return 0.0
+        return a["lat"] + HOP
+    edges = [[(j, lat(j, i)) for j in pre[i]] for i in range(n)]
+    back = [[] for _ in range(n)]
+    for i in range(n):
+        for j, l in edges[i]:
+            back[j].append((i, l))
+
+    def place(seq, ed):
+        st, busy = [0.0] * n, {}
+        for i in seq:
+            o = ops[i]; t = max([st[j] + ops[j]["c"] + l for j, l in ed[i]] + [0.0])
+            if o["q"] is not None:
+                l = busy.setdefault(o["q"], []); lo, k = 0, len(l)
+                while lo < k:
+                    mid = (lo + k) // 2
+                    if l[mid][1] <= t: lo = mid + 1
+                    else: k = mid
+                while k < len(l) and l[k][0] < t + o["c"] - 1e-9:
+                    t = max(t, l[k][1]); k += 1
+                l.insert(k, (t, t + o["c"]))
+            st[i] = t
+        return st
+    pr = [o["c"] for o in ops]
+    for i in range(n - 1, -1, -1):
+        for j, l in edges[i]:
+            pr[j] = max(pr[j], ops[j]["c"] + l + pr[i] + 1e-6)
+    st = place(sorted(range(n), key=lambda i: (-pr[i], i)), edges)
+    best = (max(st), st)
+    for _ in range(PASSES):
+        sb = place(sorted(range(n), key=lambda i: (-st[i] - ops[i]["c"], -i)), back)
+        st = place(sorted(range(n), key=lambda i: (-sb[i] - ops[i]["c"], i)), edges)
+        best = min(best, (max(st), st))
+    st = best[1]
+    return [ops[i] for i in sorted(range(n), key=lambda i: (st[i], i))]
+
+
+def emit(g, T, ops):
+    Q = {"V": g.vector, "A": g.scalar, "P": g.tensor, "G": g, "S": g.sync}
+    pre = hazards(ops, False)
+    known, clock, waits, need, cnt, last = {q: {} for q in Q}, {}, [], set(), {}, {}
+    for o, dp in zip(ops, pre):
+        q, tok = o["q"], o["tok"]
+        if tok is None:
+            cnt[q] = cnt.get(q, 0) + 1
+            tok = o["tok"] = ("e" + q, cnt[q])
+            o["eng"] = True
+        dep, ws = {}, []
+        for j in dp:
+            s, v = ops[j]["tok"]
+            dep[s] = max(dep.get(s, 0), v)
+        if q is not None:
+            for s, v in sorted(dep.items()):
+                if known[q].get(s, 0) < v and not any(s2 != s and clock[(s2, v2)].get(s, 0) >= v for s2, v2 in dep.items()):
+                    ws.append((s, v))
+            for s, v in dep.items():
+                for s2, v2 in clock[(s, v)].items():
+                    known[q][s2] = max(known[q].get(s2, 0), v2)
+            need.update(ws)
+            clock[tok] = dict(known[q])
+        else:
+            clock[tok] = {}
+        clock[tok][tok[0]] = tok[1]
+        waits.append(ws)
+        last[tok[0]] = max(tok[1], last.get(tok[0], 0))
+    num, c = {}, {}
+    for o in ops:
+        if o.get("eng") and o["tok"] in need:
+            c[o["tok"][0]] = c.get(o["tok"][0], 0) + 1
+            num[o["tok"]] = c[o["tok"][0]]
+    for o, ws in zip(ops, waits):
+        if o["q"] is None:
+            continue
+        for w in ws:
+            Q[o["q"]].wait_ge(T.sem[w[0]], num.get(w, w[1]))
+        ins = o["f"](Q[o["q"]])
+        if o["tok"] in num:
+            ins.then_inc(T.sem[o["tok"][0]], 1)
+        elif o["dma"]:
+            ins.then_inc(T.sem[o["tok"][0]], 16)
+    for s, v in sorted(last.items()):
+        if s[0] != "e":
+            g.wait_ge(T.sem[s], v)
+
+
+def rank_program(g, core, T, topo):
+    rank = T.rank_of(core)
+    if rank is None:
+        return
+    n = len(T.cores)
+    order = orders(T, topo)
+    to = order[rank]
+    fr = [[q for q in range(n) if q != rank and order[q][i] == rank][0] for i in range(3)]
+    dto = [(r - rank) % n for r in to]
+    ops, nd, rc, sends = [], [0], {}, []
+
+    def ap(d):
+        if not isinstance(d, tuple):
+            return d
+        if d[0] == "ind":
+            return ap(d[1]).indirect(ap(d[2]))
+        if d[0] == "EQ":
+            return T["EQ"][:, d[2] // 256:d[3] // 256, 0:16] if d[4] == 16 else T["EQ"][:, d[2] // 256, d[2] % 256:(d[3] - 1) % 256 + 1]
+        return T[d[0]][d[1][0]:d[1][1]:d[1][2], d[2]:d[3]:d[4]] if (d[4] != 1 or d[1][2] != 1) else T[d[0]][d[1][0]:d[1][1], d[2]:d[3]]
+
+    def I(win, off):
+        return ("ind", win, off)
+
+    def width(d):
+        return 16 * width(d[2]) if d[0] == "ind" else len(range(d[2], d[3], d[4]))
+
+    def cost(q, out, ins, mul=1.0):
+        w = max(width(out), width(ins[0]))
+        if out[0] == "ind": return FIX + w * SCA * CY
+        if ins[0][0] == "ind": return FIX + w * GAT * CY
+        if q == "A": return FIX + max(64, w) * CY
+        if mul == 1.0 and all(SCRATCH[d[0]][2] in ("bfloat16", "float16", "uint16") for d in [out] + ins): mul = 0.5
+        return max(64, w * mul) * CY
+
+    def op(q, f, out, ins, c, tok=None, dma=False, lat=0.0, after=()):
+        r, w = [], []
+        for d in ins:
+            if isinstance(d, tuple):
+                r += [d[1], d[2]] if d[0] == "ind" else [d]
+        if isinstance(out, tuple):
+            if out[0] == "ind":
+                w.append(out[1]); r.append(out[2])
+            else:
+                w.append(out)
+        ops.append({"q": q, "f": f, "r": r, "w": w, "tok": tok, "dma": dma, "c": c, "lat": lat, "after": list(after)})
+
+    def tt(out, a, b, o):
+        ps = a[0] != "ind" and "psum" in (SCRATCH[a[0]][0], SCRATCH[b[0]][0])
+        op("V", lambda q: q.tensor_tensor(ap(out), ap(a), ap(b), o), out, [a, b], cost("V", out, [a], 1.001 if ps else 2.0))
+
+    def ts(out, a, s1, o0, s2=None, o1=None):
+        if o1 is None:
+            op("V", lambda q: q.tensor_scalar(ap(out), ap(a), ap(s1), None, o0), out, [a, s1], cost("V", out, [a]))
+        else:
+            op("V", lambda q: q.tensor_scalar(ap(out), ap(a), ap(s1), ap(s2), o0, o1), out, [a, s1, s2], cost("V", out, [a]))
+
+    def cp(out, a): op("V", lambda q: q.tensor_copy(ap(out), ap(a)), out, [a], cost("V", out, [a]))
+    def ms(out, v): op("V", lambda q: q.memset(ap(out), v), out, [], cost("V", out, [out]))
+    def scan(out, a, b, ini, o0, o1): op("V", lambda q: q.tensor_tensor_scan(ap(out), ap(a), ap(b), ini, o0, o1), out, [a, b], cost("V", out, [a, b]))
+
+    def act(out, a, f=AF.Copy, bias=None, scale=None):
+        k = {}
+        if bias is not None: k["bias"] = ap(bias)
+        if scale is not None: k["scale"] = ap(scale)
+        op("A", lambda q: q.activation(ap(out), ap(a), f, **k), out, [a, bias, scale], cost("A", out, [a]))
+
+    def mm(out, l, r, start, stop, w=None):
+        op("P", lambda q: q.matmul(ap(out), ap(l), ap(r), start, stop), out, [l, r],
+           max(min(64, width(l)), w or width(r)) * PEC * (4 if SCRATCH[l[0]][2] == "float32" else 1))
+
+    def mms(out, terms):
+        for j, (l, r) in enumerate(terms):
+            mm(out, l, r, j == 0, j == len(terms) - 1)
+
+    def iota(out, pat, base, cm):
+        c = 0.13 + 2 * width(out) * CY
+        if SCRATCH[out[0]][2] == "int32":
+            op("G", lambda q: q.iota(ap(out), pat, base, cm), out, [], c)
+        else:
+            op("G", lambda q: q.iota(ap(out), pat, base, cm, allow_small_or_imprecise_dtypes=True), out, [], c)
+
+    def diag(out, a, v, shift):
+        op("G", lambda q: q.affine_select(ap(out), ap(a), [[1, 128]], O.not_equal, v, -shift, -1), out, [a], 0.17 + 256 * CY)
+
+    def dma(q, out, a, more=0.0):
+        nd[0] += 1
+        op(q, lambda e: e.dma_start(ap(out), ap(a)), out, [a], DISS, ("d%d" % (nd[0] - 1), 16), True, LDMA + more)
+
+    def engines(src, dst, e0, e1):
+        el = topo.engines(src, dst)
+        return el[e0 * len(el) // 16:e1 * len(el) // 16]
+
+    def send(trs, ls):
+        l = []
+        for peer, dst, src, rs, e0, e1 in trs:
+            c = T.cores[peer]; rid, pid, _ = topo.addr(c); el = engines(core, c, e0, e1)
+            l.append((dst, src, rs, pid, rid, sum(1 << e for e in el)))
+            rc[ls] = rc.get(ls, 0) + len(el)
+        if len(l) == 1:
+            f = lambda q: q.remote_dma(ap(l[0][0]), ap(l[0][1]), T.sem[l[0][2]], T.sem[ls], l[0][3], l[0][4], l[0][5])
+        else:
+            f = lambda q: q.remote_dma_fused([RemoteDMATransfer(dst_ids=[DstId(rid=x[4], pnc=x[3])], dma_engine_mask=x[5], remote_sem=T.sem[x[2]], src=ap(x[1]), dst=ap(x[0]))
+                                              for x in l], local_sem=T.sem[ls])
+        op("G", f, None, [x[1] for x in l], ISS + (0 if sends else FIRST), (ls, rc[ls]), False, RDMA + sum(width(x[1]) for x in l) * 7e-4, sends[-1:])
+        sends.append(len(ops) - 1)
+
+    def recv(peer, dst, rs, parts):
+        rc[rs] = rc.get(rs, 0) + sum(len(engines(T.cores[peer], core, e0, e1)) for e0, e1 in parts)
+        op(None, None, dst, [], 0.0, (rs, rc[rs]), False, 0.0, sends[-3:])
+
+    def send1(k): send([(fr[i], S("LND", LO[i] + a, LO[i] + z), S("AW", FB[i] + a, FB[i] + z), "a%d" % i, e0, e1) for i, a, z, e0, e1 in CALL1[k]], "la%d" % k)
+    def send2(k): send([(to[i], S("AW", FB[i] + a, FB[i] + z), S("XR", a, z), "x%d" % i, e0, e1) for i, a, z, e0, e1 in CALL2[k]], "lx%d" % k)
+
+    def recv1():
+        for i in range(3):
+            recv(to[i], S("LND", LO[i], LO[i] + 256 * (i + 1)), "a%d" % i, [x[3:] for c in CALL1 for x in c if x[0] == i])
+
+    def recv2():
+        for i in range(3):
+            recv(fr[i], S("AW", FB[i], FB[i] + 256 * (i + 1)), "x%d" % i, [x[3:] for c in CALL2 for x in c if x[0] == i])
+
+    def P(b, c0=0, c1=256, step=1, p=(0, 128, 1)): return S("P%d" % b, c0, c1, step, p)
+    def col(name, j): return S(name, j, j + 1)
+    names = ["I", "ROT", "ROTM", "RINV", "N3", "N2", "N1", "I64", "D01", "DC0", "DC1", "DC2", "R01", "RDL", "R45", "NR45", "R6", "R68", "RIV", "RB", "RC", "RU",
+             "WD", "WF", "DF", "GT", "WE"]
+    def mb(x): return S("MBF", 128 * names.index(x), 128 * names.index(x) + 128)
+    n16 = ["I", "NI", "BK", "TRI", "DM", "B15"]
+    def mf(x): return S("MF", 128 * n16.index(x), 128 * n16.index(x) + 128)
+    ny = ["1", "45", "6", "DL", "PH", "LP"]
+    def Y(x, k): return S("YB", 144 * ny.index(x) + 15 - k, 144 * ny.index(x) + 143 - k)
+    def ct(j): return S("CT", 256 * j, 256 * j + 256)
+    def row(name, r, w): return S(name, 0, w, 1, (r, 128, 16))
+    def b2(j): return S("B2", 128 * j, 128 * j + 128)
+    def blk(name, j): return S(name, 256 * j, 256 * j + 256)
+    def sub(d, c): return d[:2] + (d[2] + c[0], d[2] + c[1], 1)
+    def xp(j): return S("AW", XB + 256 * j, XB + 256 * j + 256)
+    kcol = col("KC", 0); io = S("IO", 0, 128); p8 = (0, 8, 1); Y1 = S("YB", 0, 144)
+    def FX(b, f): return S("FX%d" % b, 256 * f, 256 * f + 256)
+
+    dma("S", S("SN"), T["snd"][:]); dma("S", S("DI", 0, 128), T["ti"][:]); dma("A", S("DI", 288, 416), T["kd"][:]); dma("A", S("A0"), T["a0"][:], 1.0)
+    dma("S", S("CA"), T["ca"][:], 0.5); dma("A", S("BE", 0, 1), T["be"][:]); dma("S", S("KW", 0, E), T["k0"][:], 1.0)
+    dma("S", S("DI", 128, 160), T["bg"][:]); dma("S", S("DI", 416, 448), T["cl"][:]); dma("S", S("DI", 448, 528), T["us"][:]); dma("S", S("DI", 160, 288), T["lp"][:])
+    iota(col("KI", 0), [[1, 1]], 0, 1); iota(S("I64"), [[1, 64]], 0, 0); iota(S("IO"), [[1, 144]], 0, -1)
+    iota(S("JJ"), [[0, 16], [1, 16]], 0, 0); iota(S("H0"), [[1, 33], [0, 8]], 0, 0); iota(S("DU", 0, 16), [[16, 16]], 0, 0)
+    iota(S("G8", 0, 128, 1, p8), [[1, 8], [0, 16]], 0, -1)
+    ms(S("Z"), 0.0)
+    for x, v in (("I", 1.0), ("N3", -3.0), ("N2", -2.0), ("N1", -1.0), ("I64", 64.0)):
+        diag(mb(x), S("Z"), v, 0)
+    diag(mb("ROT"), S("Z"), 1.0, 16); diag(mb("ROT"), mb("ROT"), 1.0, -112); diag(mb("RINV"), S("Z"), 1.0, -16); diag(mb("RINV"), mb("RINV"), 1.0, 112)
+    diag(b2(0), S("Z"), -1.0, 1)
+    ts(col("KI", 1), col("KI", 0), 15, O.bitwise_and); cp(kcol, col("KI", 1))
+    ts(S("M16"), S("I64", 0, 16), kcol, O.is_equal); tt(S("M2"), S("M16", 0, 16, 2), S("M16", 1, 16, 2), O.add)
+    tt(S("KC", 1, 3), S("M16", 0, 2), S("M16", 2, 4), O.add)
+    ts(S("PH", 0, 64), S("I64"), col("KC", 2), O.mult); act(S("IL", 0, 64), S("I64"), scale=col("M16", 1))
+    for j in range(5):
+        ts(col("KC", 16 + j), col("KC", 1), float(64 << j), O.mult); act(col("KC", 24 + j), col("M16", 0), scale=float(64 << j))
+        ts(S("PH", 64 << j, 128 << j), S("PH", 0, 64 << j), col("KC", 16 + j), O.add)
+        act(S("IL", 64 << j, 128 << j), S("IL", 0, 64 << j), AF.Identity, col("KC", 24 + j))
+    ts(col("KC", 3), col("M2", 0), -1.0, O.mult, 1.0, O.add)
+    tt(col("KC", 4), col("M2", 1), col("M2", 0), O.subtract)
+    ts(col("KC", 8), col("M16", 2), float(XB), O.mult); ts(col("KC", 11), col("M16", 0), 2048.0, O.mult)
+    for i in range(3):
+        ts(col("KC", 5 + i), col("M16", 2), float(FB[i] - XB), O.mult, col("KC", 11), O.add)
+    ts(col("KC", 9), col("M16", 0), -1.0, O.mult, 1.0, O.add); ts(col("KC", 10), col("KC", 9), 1024.0, O.mult)
+    ts(col("KC", 12), col("M16", 15), -1.0, O.mult, 1.0, O.add)
+    ts(S("J"), S("IO"), kcol, O.add); ts(Y1, S("J"), 15.0, O.is_equal)
+    ts(b2(4), S("J", 0, 128), 0.0, O.is_ge); ts(b2(5), S("J", 0, 128), 15.0, O.is_le); tt(S("BK"), b2(4), b2(5), O.mult)
+    for j, v in enumerate((1.0, -2048.0, -1408.0, -10240.0)):
+        ms(ct(j), v)
+    ts(mb("ROTM"), mb("ROT"), col("KC", 3), O.mult); ts(mb("D01"), mb("I"), col("M2", 0), O.mult)
+    for i in range(3):
+        ts(mb("DC%d" % i), mb("I"), col("KC", 5 + i), O.mult)
+    for x, c in (("45", col("M2", 2)), ("6", col("M16", 6)), ("DL", col("KC", 4)), ("PH", col("M2", 1)), ("LP", col("M2", 4))):
+        act(S("YB", 144 * ny.index(x), 144 * ny.index(x) + 144), Y1, scale=c)
+    for x, c, v in (("R01", col("M2", 0), 1.0), ("RDL", col("KC", 4), 1.0), ("R45", col("M2", 2), 1.0), ("R6", col("M16", 6), 1.0), ("RB", col("M2", 5), 1.0),
+                    ("RC", col("M16", 12), 1.0), ("RU", col("M16", 13), 1.0), ("RIV", col("M16", 7), 1.0), ("NR45", col("M2", 2), -1.0), ("R68", col("M16", 6), 8.0),
+                    ("WE", col("M16", 15), -16384.0)):
+        ts(mb(x), S("BK"), c, O.mult, v, O.mult) if v != 1.0 else act(mb(x), S("BK"), scale=c)
+    act(mb("WF"), S("BK"), scale=16384.0); act(S("I32"), mb("I"))
+    cp(S("Y16"), Y1); cp(mf("I"), mb("I")); cp(mf("NI"), mb("N1")); cp(mf("BK"), S("BK")); ts(mf("B15"), S("BK"), col("M16", 15), O.mult)
+    ts(b2(6), io, 0.0, O.is_ge, 256.0, O.mult); tt(mf("TRI"), b2(6), S("BK"), O.mult)
+    ts(b2(7), io, 1.0, O.is_ge, 16384.0, O.mult); tt(mb("WD"), b2(7), S("BK"), O.mult)
+    ts(b2(1), b2(0), col("KC", 12), O.mult); diag(mb("DF"), b2(1), 1.0, 0)
+    ts(b2(2), mb("I"), col("KC", 9), O.mult); tt(mf("DM"), b2(2), b2(1), O.add)
+    GT = mb("GT")[:1] + (p8,) + mb("GT")[2:]
+    ts(GT, S("G8", 0, 128, 1, p8), 0.0, O.is_equal)
+    ms(S("IL", INV, LB), 0.0); ts(col("IL", INV), col("M16", 7), 100.0, O.mult); ms(S("AW", DA, AWN), 0.0); ms(S("KW", E, E + 256), 0.0); iota(S("AUX"), [[0, E]], 0, 0)
+    ts(S("JJ"), S("JJ"), kcol, O.is_equal, 2.0 ** 30 + 8192, O.mult); act(S("CM"), S("JJ"), AF.Identity, -2.0 ** 30)
+    ms(S("RS"), 2.0 ** 30); ms(S("RS", 0, 256, 16), -2.0 ** 30); ms(S("RM"), -0.0625); ms(S("RM", 0, 256, 16), 2.0 ** 20)
+    ts(S("DU", 0, 16), S("DU", 0, 16), kcol, O.add, float(DA - CD), O.add)
+    for j, v in ((1, E + 1), (2, LB - 2047), (3, LB - 2047 + 256)):
+        ts(S("DU", 16 * j, 16 * j + 16), S("DU", 0, 16), float(v - DA + CD), O.add)
+    ms(S("H0", 0, 264, 8), 0.0)
+    for j in range(8):
+        ms(S("H1", j, 264, 8), 1.0 / math.factorial(7 - j))
+    act(S("H0"), S("H0"), scale=col("BE", 0)); act(col("BE", 1), col("BE", 0), scale=-1.0)
+    scan(S("H2"), S("H0"), S("H1"), 0.0, O.mult, O.add)
+    act(col("SQ", 0), col("H2", 263))
+    for j in range(5):
+        act(col("SQ", j + 1), col("SQ", j), scale=col("SQ", j))
+    op("V", lambda q: q.reciprocal(ap(col("SQ", 6)), ap(col("SQ", 5))), col("SQ", 6), [col("SQ", 5)], 0.2)
+    act(S("TE", 0, 32), S("H2", 7, 256, 8), scale=col("SQ", 6))
+    for j in range(6):
+        act(S("TE", 32 << j, 64 << j), S("TE", 0, 32 << j), scale=col("SQ", j))
+    ms(col("TE", 0), 0.0)
+    for i in range(3):
+        cp(S("uS", 16 * i, 16 * i + 16), S("SN", 16 * (dto[i] - 1), 16 * dto[i]))
+    ts(S("DH", 576, 704), S("DI", 160, 288), 0.0, O.is_lt, 2817.0, O.mult); tt(S("DI", 160, 288), S("DI", 160, 288), S("DH", 576, 704), O.add)
+    for a, z in ((0, 128), (128, 288)):
+        ts(S("DH", a, z), S("DI", a, z), 8128, O.bitwise_and); ts(S("DH", 288 + a, 288 + z), S("DI", a, z), 63, O.bitwise_and)
+        cp(S("DB", a, z), S("DH", a, z)); cp(S("DB", 288 + a, 288 + z), S("DH", 288 + a, 288 + z))
+    cp(S("DB", 576, 704), S("DI", 288, 416)); cp(S("DB", 704, 816), S("DI", 416, 528))
+    for q, nm, r, c0, w in (("S", "IL", 4, 0, 128), ("A", "IL", 5, 288, 128), ("S", "IL", 6, 576, 128), ("S", "AUX", 10, 128, 32), ("S", "AUX", 11, 416, 32),
+                            ("S", "AUX", 12, 704, 32), ("S", "AUX", 13, 736, 80), ("S", "AUX", 8, 160, 128), ("S", "AUX", 9, 448, 128)):
+        dma(q, row(nm, r, 16 * w), S("DB", c0, c0 + w), 0.3)
+    for b in range(2):
+        ts(blk("CF", b), blk("CA", b), 2048.0, O.is_ge, -2048.0, O.add); cp(blk("cI", b), blk("CA", b))
+        tt(FX(b, 0), blk("CF", b), blk("CA", b), O.add)
+    for j in range(4):
+        act(S("AW", 512 * j, 512 * j + 512), S("A0", 512 * j, 512 * j + 512), AF.Identity, 15.0, -1.0)
+    for j in range(3):
+        act(xp(j), I(S("A0"), S("uS", 16 * j, 16 * j + 16)), AF.Identity, 15.0, -1.0)
+        mm(P(5 + j), mb("ROT"), xp(j), True, True)
+        act(blk("XR", j), P(5 + j))
+    send2(0)
+    ts(S("XD"), S("PH", 0, 768), col("M2", 1), O.mult, col("KC", 8), O.add)
+    for i in (2, 1, 0):
+        cp(I(S("PH"), S("uS", 16 * i, 16 * i + 16)), blk("XD", i))
+    act(S("G1"), I(S("IL", 0, E), S("uS"))); cp(S("G2"), I(S("PH"), S("uS")))
+    for i in range(3):
+        c0 = 256 * (dto[i] - 1)
+        mms(P(i), [(mb("D01"), S("IL", c0 + 1, c0 + 257)), (mb("DC%d" % i), ct(0)), (mb("ROTM"), blk("G1", i)), (mb("ROT"), blk("G2", i))])
+        act(blk("IM", i), P(i)) if i != 1 else cp(blk("IM", i), P(i))
+        send([(to[i], S("IL", E + c0, E + c0 + 256), blk("IM", i), "n%d" % i, 0, 16)], "ln%d" % i)
+    dma("S", row("IL", 2, E), row("PH", 2, E), 0.3); dma("A", row("IL", 3, E), row("PH", 3, E), 0.3)
+    for i in range(3):
+        c0 = E + 256 * ((rank - fr[i]) % n - 1)
+        recv(fr[i], S("IL", c0, c0 + 256), "n%d" % i, [(0, 16)])
+    for k in range(1, len(CALL2)):
+        send2(k)
+    recv2()
+    for j, (c0, w) in enumerate(((0, 512), (512, 512), (1024, 256))):
+        mm(P(3 + j % 2, 0, w), mb("RU"), S("AUX", c0, c0 + w), True, True); act(S("U", c0, c0 + w), P(3 + j % 2, 0, w))
+    mm(P(4, 0, 512), mb("RC"), S("AUX", 0, 512), True, True); ts(S("OH"), P(4, 0, 512), kcol, O.is_equal)
+    act(S("C7"), S("OH"), AF.Identity, 7.0, -1.0)
+    if not GVA: ts(S("NOH"), S("OH"), -1.0, O.mult)
+    mms(P(3, 0, 128), [(Y("LP", a), S("AUX", a, E, 16)) for a in range(16)]); cp(S("uL"), P(3, 0, 128))
+
+    def floor32(ps, j, c=(0, 256)):
+        act(sub(blk("AB", j), c), ps, AF.Abs); act(sub(blk("HI", j), c), sub(blk("AB", j), c), AF.Identity, 159.515625, 0.03125)
+
+    def lists(b, bk, c=(0, 256)):
+        w = c[1] - c[0]
+        ts(sub(blk("cB", b), c), sub(FX(b, 2), c), -1.0, O.add)
+        mms(P(bk[0], 0, w), [(mf("I"), sub(FX(b, 0), c)), (mf("I"), sub(FX(b, 1), c))])
+        mm(P(bk[1], 0, w), mf("DM"), sub(FX(b, 3), c), True, True); mm(P(bk[2], 0, w), mf("B15"), sub(FX(b, 3), c), True, True)
+        ts(sub(blk("cA", b), c), P(bk[0], 0, w), float(CD), O.add); ts(sub(blk("cR", b), c), P(bk[1], 0, w), col("KC", 10), O.add)
+        act(sub(blk("E15", b), c), P(bk[2], 0, w), AF.Exp, None, col("BE", 1))
+        for j in range(c[0], c[1], GA):
+            act(S("RG", 4096 * b + 16 * j, 4096 * b + 16 * (j + GA)), I(S("TE"), S("cR", 256 * b + j, 256 * b + j + GA)))
+
+    def agather(b):
+        for j, z in zip(KCUT[:-1], KCUT[1:]):
+            act(S("KG", 16 * j, 16 * z), I(S("AW", 0, DA), S("cA", 256 * b + j, 256 * b + z)), AF.Identity, 15.0, -1.0)
+
+    def facts(b, who, bk, c):
+        own = sub(blk("IL", b), c); g0 = 4096 * b; w = c[1] - c[0]
+        for j in range(c[0] // 32, c[1] // 32):
+            o, x = S("PR", g0 + 512 * j, g0 + 512 * j + 512), I(S("IL", 0, INV), S("cI", 256 * b + 32 * j, 256 * b + 32 * j + 32))
+            cp(o, x) if who[j] == "V" else act(o, x)
+        mm(P(bk[0], 0, w), mb("NR45"), own, True, False); mm(P(bk[1], 0, w), mb("R68"), own, True, False); mm(P(bk[2], 0, w), mb("I"), sub(ct(2), (0, w)), True, False)
+        for j in range(c[0] // 64, c[1] // 64):
+            for x, z in (("45", bk[0]), ("6", bk[1]), ("DL", bk[2])):
+                for k in range(16):
+                    mm(P(z, 64 * j - c[0], 64 * j + 64 - c[0]), Y(x, k), S("PR", g0 + 1024 * j + k, g0 + 1024 * j + 1024, 16), False, j == c[1] // 64 - 1 and k == 15 and x != "6")
+        floor32(P(bk[0], 0, w), b, c); mm(P(bk[1], 0, w), mb("I64"), sub(blk("HI", b), c), False, True)
+        ts(sub(FX(b, 2), c), P(bk[1], 0, w), -10239.0, O.add); cp(sub(FX(b, 1), c), P(bk[2], 0, w)); cp(sub(FX(b, 3), c), sub(blk("AB", b), c))
+        lists(b, bk, c)
+
+    facts(0, "VAVAVAVA", (5, 6, 7), (0, 128)); facts(0, "VAVAVAVA", (0, 1, 2), (128, 256))
+    agather(0); facts(1, WHO1, (0, 1, 2), (0, 256))
+    for j in range(4):
+        act(S("IL", LB + 512 * j, LB + 512 * j + 512), I(S("IL", 0, LB), S("uL", 32 * j, 32 * j + 32)))
+
+    def dedupe(key, k, bank):
+        mm(P(bank), mb("I"), S("CM"), True, False); mm(P(bank), mb("WE"), S("HIT"), False, False)
+        for b in range(16):
+            w = 256 - 16 * b; off = 4096 * k + 256 * b
+            ts(S("EQ", off, off + w), S("REP", 256 * k + 16 * b, 256 * k + 256), sub(key, (b, b + 1)), O.is_equal)
+            if b < 15: mm(P(bank, 16 * b + 16, 256), mb("WF"), S("EQ", off + 16, off + w), False, False)
+        mm(P(bank), mb("WD"), S("EQ", 4096 * k, 4096 * k + 4096, 16), False, True)
+
+    for t in range(R):
+        b = t % 2; lo = 256 * b; own = blk("IL", b); pr = 4096 * b; W16 = blk("W16", b); v0 = 48 * b
+
+        def tn(j): return S("TN", 256 * b + 16 * j, 256 * b + 16 * j + 16)
+        def ut(j): return S("uT", 96 * b + 16 * j, 96 * b + 16 * j + 16)
+
+        def winners(k, bank, y1, add, u):
+            scan(blk("SD", k), S("RS"), P(bank), 0.0, O.min, O.max)
+            tt(tn(8 + k), y1, S("SD", 256 * k + 15, 256 * k + 256, 16), O.max); tt(tn(10 + k), tn(8 + k), S("DU", 16 * k, 16 * k + 16), O.min); ts(u, tn(10 + k), add, O.add)
+
+        for j, z in zip(CH[:-1], CH[1:]):
+            for c0, c1 in zip(KCUT[:-1], KCUT[1:]):
+                if j <= c0 < z:
+                    tt(S("PR", pr + 16 * c0, pr + 16 * c1), I(S("KW", 0, E), S("cB", lo + c0, lo + c1)), S("KG", 16 * c0, 16 * c1), O.mult)
+            mms(P(5, j, z), [(Y("1", k), S("PR", pr + 16 * j + k, pr + 16 * z, 16)) for k in range(16)])
+        cp(W16, P(5))
+        mms(P(6, 256, 512), [(mb("RB"), blk("AUX", b)), (mf("BK"), W16)]); mm(P(7), mf("TRI"), W16, True, True)
+        tt(S("T1"), P(6, 256, 512), blk("U", t), O.mult); tt(S("HIT"), P(7), S("T1"), O.is_gt)
+        mm(P(6), mb("DF"), S("HIT"), True, True)
+        nf = 3 if t < R - 1 else 2
+        for f in range(nf):
+            tt(blk("SEL", f), P(6), FX(b, f), O.mult)
+        mm(P(3), mf("BK"), blk("SEL", 0), True, True)
+        mms(P(4, 0, 16), [(S("Y16", 15 - a, 143 - a), S("SEL", a, 256, 16)) for a in range(16)])
+        mms(P(7, 0, 16 * nf - 16), [(S("Y16", 15 - a, 143 - a), S("SEL", 256 + a, 256 * nf, 16)) for a in range(16)])
+        cp(blk("REP", 0), P(3)); cp(S("VL", v0, v0 + 16), P(4, 0, 16)); act(S("VL", v0 + 16, v0 + 16 * nf), P(7, 0, 16 * nf - 16))
+        key, dl, bn = S("VL", v0, v0 + 16), S("VL", v0 + 16, v0 + 32), S("VL", v0 + 32, v0 + 48)
+        dedupe(key, 0, 5)
+        tt(tn(0), key, dl, O.add); ts(ut(0), tn(0), float(CD), O.add)
+        if GVA:
+            act(S("TMQ"), I(S("AW"), ut(0))); mms(P(7), [(mb("N1"), blk("OH", b)), (mb("I"), S("TMQ"))]); act(S("GV"), P(7), AF.Relu)
+        else:
+            tt(S("GV"), I(S("AW"), ut(0)), blk("OH", b), O.max)
+        winners(0, 5, tn(0), float(CD), ut(1))
+        cp(I(S("AW"), ut(1)), S("GV")) if GVA else tt(I(S("AW"), ut(1)), S("GV"), blk("NOH", b), O.add)
+        for k in range(len(CALL1)):
+            send1(k)
+        recv1()
+        for j in range(3):
+            mms(P(5 + j), [(mb("N%d" % (3 - j)), blk("XR", j)), (mb("ROT"), xp(j))]
+                + [(mb("I"), S("LND", LO[i] + 256 * j, LO[i] + 256 * j + 256)) for i in (2, 1, 0) if i >= j])
+            act(blk("XR", j), P(5 + j), AF.Relu) if XV[j] == "A" else ts(blk("XR", j), P(5 + j), 0.0, O.max)
+        if t < R - 1:
+            for k in range(len(CALL2)):
+                send2(k)
+        for j in range(3):
+            mm(P(5 + j, 256, 512), mb("RINV"), blk("XR", j), True, True)
+            act(xp(j), P(5 + j, 256, 512))
+        if t < R - 1:
+            recv2(); agather(1 - b)
+            mm(P(3), mf("BK"), blk("SEL", 2), True, True); cp(blk("REP", 1), P(3)); dedupe(bn, 1, 4)
+            ts(ut(2), bn, -1.0, O.add)
+            tt(S("GK"), I(S("KW"), ut(2)), blk("C7", b), O.min)
+            winners(1, 4, bn, -1.0, ut(3))
+            tt(I(S("KW"), ut(3)), S("GK"), blk("OH", b), O.add)
+        for a in range(0, 4096, LAM):
+            scan(S("ST", a, a + LAM), S("RG", pr + a, pr + a + LAM), S("PR", pr + a, pr + a + LAM), 0.0, O.mult, O.add)
+        tt(blk("YL", t), S("ST", 15, 4096, 16), blk("E15", b), O.mult)
+        dma("S", T["yl"][:, 256 * t:256 * t + 256], blk("YL", t))
+        if t < R - 2:
+            ts(tn(1), key, 0.0, O.is_equal, 8192.0, O.mult); ts(tn(4), key, 0.0, O.is_lt); tt(tn(5), key, tn(4), O.add); ts(tn(6), key, 2064.0, O.add)
+            tt(tn(5), tn(5), tn(1), O.add); tt(tn(6), tn(6), tn(4), O.mult); tt(tn(5), tn(5), S("DU", 32 + 16 * b, 48 + 16 * b), O.min)
+            ts(ut(5), tn(6), float(INV), O.add); ts(ut(4), tn(5), 2047.0, O.add)
+            act(S("TMP"), I(S("IL"), ut(4))); act(S("IL", LB + lo, LB + lo + 256), S("TMP")); act(S("UP"), I(S("IL"), ut(5)))
+            for h in range(2):
+                mm(P(0, 128 * h, 128 * h + 128), S("W16", lo + 128 * h, lo + 128 * h + 128), mf("I"), True, True)
+            scan(blk("SD", 2), S("RM"), P(0), 0.0, O.add, O.min)
+            ts(S("TI"), S("SD", 527, 768, 16), 16.0, O.mult, 15.0, O.add); ts(S("TI"), S("TI"), 15, O.bitwise_and); cp(S("MB"), S("TI"))
+            for h in range(2):
+                mm(P(0, 128 * h, 128 * h + 128, 1, p8), S("MB", 8 * h, 8 * h + 8), mb("I"), True, True)
+            act(S("M8", 0, 256, 1, p8), P(0, 0, 256, 1, p8))
+            mms(P(1), [(mb("R45"), S("UP")), (mb("NR45"), own)]); floor32(P(1), 2)
+            mms(P(0), [(GT, S("M8", 0, 256, 1, p8)), (mb("RIV"), S("UP"))])
+            act(blk("MK", 1), P(0), AF.Abs, kcol, -1.0); act(blk("MK", 0), blk("MK", 1), AF.Relu, 1.0, -1.0)
+            new = ([(mb("R01"), S("UP")), (mb("I"), ct(1))], [(mb("RDL"), S("UP")), (mb("I"), ct(2))],
+                   [(mb("R6"), S("UP")), (mb("R68"), own), (mb("I64"), blk("HI", 2)), (mb("I"), ct(3)), (mb("I"), ct(0))], [(S("I32"), blk("AB", 2))])
+            for f in range(4):
+                z = (f + 1) % 3
+                mms(P(z), new[f] + [(mf("NI"), FX(b, f))]); mm(P(z, 256, 512), mf("I"), FX(b, f), True, True)
+                tt(blk("TT", f % 2), P(z), blk("MK", 0), O.mult); tt(FX(b, f), P(z, 256, 512), blk("TT", f % 2), O.add)
+            lists(b, (0, 1, 2))
+    mms(P(0, 0, 128), [(Y("PH", a), S("PH", a, E, 16)) for a in range(16)]); cp(S("uY"), P(0, 0, 128))
+    for j in range(4):
+        o, w = S("YA", 512 * j, 512 * j + 512), I(S("AW", 0, FB[0]), S("uY", 32 * j, 32 * j + 32))
+        ts(o, w, -1.0, O.mult, 15.0, O.add) if j % 2 == 0 else act(o, w, AF.Identity, 15.0, -1.0)
+        dma("SA"[j % 2], T["ya"][:, 512 * j:512 * j + 512], o)
+    op("S", None, None, [], 0.0, ("end", 0), False, 0.0, [i for i, o in enumerate(ops) if o["dma"]])
+    ops = [o for o in arrange(ops) if o["f"] is not None or o["q"] is None]
+    emit(g, T, ops)

@@ -1,47 +1,54 @@
-import math
+import numpy
 from concourse.bass import DstId, RemoteDMATransfer
 from concourse.mybir import AluOpType as O, ActivationFunctionType as AF
 
 E, M, R = 2048, 256, 5
-XB, FB, DA, AWN = 2048, (2816, 3072, 3584), 4352, 4608
-LB, INV, ILN = 2832, 2816, 4880
+CD, XB, FB, AWN = 3072, 3136, (3904, 2560, 4160), 5392
+I0, LB, ILN = 16, 2832, 4896
 LO = (0, 256, 768)
-CD = 3456
+BIG = 16384.0
 CH = (0, 64, 128, 192, 256)
 KCUT = (0, 16, 32, 64, 96, 128, 160, 192, 224, 256)
+MODE = ("aaaaaaaaa",) + ("bbbbbbbbb",) * 4
 LAM = 256
-GA = 32
-WHO1, XV, GVA, PASSES = "AAAAAAAA", "AAA", True, 4
-CALL1 = ([(2, 0, 768, 0, 16)], [(1, 0, 512, 0, 16)], [(0, 0, 256, 0, 16)])
-CALL2 = ([(0, 0, 256, 0, 16)], [(1, 0, 512, 0, 16)], [(2, 0, 768, 0, 16)])
-CY, PEC, GAT, SCA, FIX, HOP, LDMA, RDMA, ISS, DISS, FIRST = 1.04e-3, 0.55e-3, 1.56, 3.8, 0.05, 0.1, 2.1, 2.4, 0.3, 0.15, 2.0
+WHO0, WHO1, XV, GKA, FXA, PROD, PASSES, PSK = "VAVAVAVA", "AAAAAAAA", "VVV", True, True, "scan", 200, True
+CY, PEC, GAT, SCA, FIX, HOP, LDMA, RDMA, ISS, DISS, FIRST = 0.95e-3, 0.485e-3, 1.56, 3.8, 0.05, 0.22, 2.1, 2.6, 0.3, 0.15, 2.0
 
 SCRATCH = {}
 for _n, _w, _d in (
-        ("AW", AWN, "bfloat16"), ("KW", 2304, "bfloat16"), ("IL", ILN, "bfloat16"), ("PH", E, "bfloat16"), ("AUX", E, "bfloat16"), ("KG", 4096, "bfloat16"),
-        ("PR", 8192, "bfloat16"), ("A0", E, "bfloat16"), ("RG", 8192, "float32"), ("ST", 4096, "float32"), ("TE", 2048, "float32"),
-        ("YL", 1280, "float32"), ("YA", 2048, "float32"), ("XR", 768, "bfloat16"), ("LND", 1536, "bfloat16"),
+        ("AW", AWN, "bfloat16"), ("KW", 2304, "bfloat16"), ("IL", ILN, "bfloat16"), ("PH", E, "bfloat16"), ("AG", 4096, "bfloat16"), ("KG", 4096, "bfloat16"),
+        ("PR", 4 * 4096, "bfloat16"), ("A0", 2816, "bfloat16"), ("RG", 8192, "float32"), ("ST", 4096, "float32"),
+        ("YL", 1280, "float32"), ("XR", 768, "bfloat16"), ("XT", 768, "bfloat16"), ("LND", 1536, "bfloat16"),
         ("XD", 768, "bfloat16"), ("G1", 768, "bfloat16"), ("G2", 768, "bfloat16"), ("IM", 768, "bfloat16"),
-        ("U", 1280, "bfloat16"), ("OH", 512, "bfloat16"), ("NOH", 512, "bfloat16"), ("C7", 512, "bfloat16"),
-        ("FX0", 1024, "float16"), ("FX1", 1024, "float16"), ("E15", 512, "float32"), ("W16", 512, "float16"), ("T1", 256, "float32"),
+        ("U", 1280, "bfloat16"), ("AUX", 1280, "bfloat16"), ("OH", 512, "bfloat16"), ("C7", 512, "bfloat16"),
+        ("FX0", 768, "float16"), ("FX1", 768, "float16"), ("CUM", 256, "float32"), ("D32", 128, "float32"), ("L32", 128, "float32"), ("KD", 512, "bfloat16"), ("TK", 2048, "bfloat16"), ("T1", 256, "float32"),
         ("HIT", 256, "bfloat16"), ("SEL", 768, "float16"), ("REP", 512, "float16"), ("VL", 96, "float32"), ("SD", 768, "float32"),
-        ("TN", 512, "float32"), ("TI", 16, "int32"), ("MB", 16, "bfloat16"), ("M8", 256, "bfloat16"), ("MK", 512, "float32"), ("TT", 512, "float32"),
-        ("GV", 256, "bfloat16"), ("GK", 256, "bfloat16"), ("TMP", 256, "bfloat16"), ("TMQ", 256, "bfloat16"), ("UP", 256, "bfloat16"),
+        ("TN", 128, "float32"), ("TI", 16, "int32"), ("MB", 16, "bfloat16"), ("M8", 256, "bfloat16"), ("MK", 512, "bfloat16"), ("TT", 1024, "float32"),
+        ("GV", 768, "bfloat16"), ("GK", 768, "bfloat16"), ("TMP", 256, "bfloat16"), ("UC", 256, "bfloat16"), ("UP", 256, "bfloat16"),
         ("AB", 768, "float32"), ("HI", 768, "bfloat16"),
-        ("cI", 512, "uint16"), ("cA", 512, "uint16"), ("cB", 512, "uint16"), ("cR", 512, "uint16"), ("uS", 48, "uint16"), ("uT", 192, "uint16"),
-        ("uL", 128, "uint16"), ("uY", 128, "uint16"), ("CA", 512, "int32"), ("CF", 512, "float32"), ("SN", 48, "int32"), ("BE", 2, "float32"),
-        ("DI", 528, "int32"), ("DH", 704, "int32"), ("DB", 816, "bfloat16"), ("Z", 128, "bfloat16"),
-        ("IO", 144, "float32"), ("J", 144, "float32"), ("BK", 128, "bfloat16"), ("B2", 1024, "bfloat16"), ("I32", 128, "float32"),
-        ("KI", 2, "int32"), ("KC", 32, "float32"), ("M16", 16, "float32"), ("M2", 8, "float32"), ("I64", 64, "float32"),
-        ("JJ", 256, "float32"), ("CM", 256, "bfloat16"), ("RS", 256, "float32"), ("RM", 256, "float32"), ("DU", 64, "float32"),
-        ("H0", 264, "float32"), ("H1", 264, "float32"), ("H2", 264, "float32"), ("SQ", 8, "float32"), ("G8", 128, "float32"),
-        ("CT", 1024, "bfloat16"), ("YB", 6 * 144, "bfloat16"), ("Y16", 144, "float16"), ("MBF", 27 * 128, "bfloat16"), ("MF", 6 * 128, "float16")):
+        ("cI", 512, "uint16"), ("cA", 512, "uint16"), ("cB", 512, "uint16"), ("uS", 48, "uint16"), ("uT", 256, "uint16"),
+        ("uY", 128, "uint16"), ("CA", 512, "int32"), ("SN", 48, "int32"), ("BE", 2, "float32"),
+        ("DI", 528, "int32"), ("DB", 1072, "bfloat16"), ("Z", 128, "bfloat16"),
+        ("IO", 144, "float32"), ("J", 144, "float32"), ("BK", 128, "bfloat16"), ("B2", 768, "bfloat16"), ("I32", 128, "float32"),
+        ("KI", 2, "int32"), ("KC", 32, "float32"), ("KH", 48, "float32"), ("M16", 16, "float32"), ("M2", 8, "float32"), ("I256", 256, "float32"),
+        ("B256", 256, "bfloat16"), ("LG", 1280, "float16"), ("DC", 16, "float32"),
+        ("CM", 256, "bfloat16"), ("RS", 256, "float32"), ("RM", 256, "float32"), ("DU", 32, "float32"), ("G8", 128, "float32"),
+        ("YB", 5 * 144, "bfloat16"), ("Y16", 144, "float16"), ("MBF", 29 * 128, "bfloat16"), ("MF", 3 * 128, "float16"), ("DK", 16 * 128, "float16")):
     SCRATCH[_n] = ("sbuf", [128, _w], _d)
 SCRATCH["EQ"] = ("sbuf", [128, 32, 256], "bfloat16")
 for _n in range(8):
     SCRATCH["P%d" % _n] = ("psum", [128, 512], "float32")
 NDMA = 40
-SEMAPHORES = ["eV", "eA", "eP", "eG"] + ["d%d" % _n for _n in range(NDMA)] + [_a + str(_n) for _a in ("a", "x", "n", "la", "lx", "ln") for _n in range(3)]
+DBG = []
+ORDER = []
+DBG2 = []
+SEED, SWAPS, HEAT, BYTE, JOGS, WARM = 5, 1500, 0.3, 6e-4, 2000, 0.5
+GUESS = ((1.0, 1.0, 0.24, 0.0), (0.95, 1.2, 0.16, 0.0), (1.35, 0.75, 0.2, 0.0), (1.3, 1.6, 0.25, 0.0))
+SEQ = ("PR", "AG", "KG", "EQ")
+XPW = "VVV"
+LEAD = {}
+KB, EB, KVL, TOT = 1, (6, 7), "V", 192
+SEMAPHORES = ["eV", "eA", "eP", "eG"] + ["d%d" % _n for _n in range(NDMA)] + [_a + str(_n) for _a in ("a", "x", "n", "m", "la", "lx", "ln", "lm") for _n in range(3)]
 
 
 def S(name, c0=0, c1=None, step=1, p=(0, 128, 1)):
@@ -64,11 +71,11 @@ def hazards(ops, pe_chain):
                 pm |= 1 << x
             acc.append((d, wr, pm))
             ps = SCRATCH[d[0]][0] == "psum"
-            for (m2, a, b, j, w2) in recs.get(d[0], []):
+            for (m2, a, b, j, w2, s2) in recs.get(d[0], []):
                 same = ops[j]["q"] == o["q"]
                 if same and o["q"] == "P":
                     if pe_chain and ps: dep.add(j)
-                elif (ps and not same) or ((wr or w2) and (m2 & pm) and a < d[3] and d[2] < b):
+                elif (ps and not same) or ((wr or w2) and (m2 & pm) and a < d[3] and d[2] < b and not (s2 == d[4] > 1 and (a - d[2]) % s2 and d[0] == "RG")):
                     dep.add(j)
         for d, wr, pm in acc:
             l = recs.setdefault(d[0], [])
@@ -77,57 +84,148 @@ def hazards(ops, pe_chain):
                     l[:] = [e for e in l if ops[e[3]]["q"] == ops[l[-1][3]]["q"]]
                 elif l and o["q"] == "P":
                     l.pop()
-            elif wr and d[4] == 1:
-                l[:] = [e for e in l if not ((e[0] & ~pm) == 0 and e[1] >= d[2] and e[2] <= d[3])]
-            l.append((pm, d[2], d[3], i, wr))
+            elif wr:
+                l[:] = [e for e in l if not ((e[0] & ~pm) == 0 and e[1] >= d[2] and e[2] <= d[3] and (d[4] == 1 or (e[5] == d[4] and (e[1] - d[2]) % d[4] == 0)))]
+            l.append((pm, d[2], d[3], i, wr, d[4]))
         out.append(dep)
     return out
 
 
 def arrange(ops):
-    n = len(ops); pre = hazards(ops, True)
-    for i, o in enumerate(ops):
-        pre[i] |= set(o["after"])
+    n = len(ops); pre = hazards(ops, True); qs = [o["q"] for o in ops]
+    if ORDER:
+        at = {i: k for k, i in enumerate(ORDER)}
+        assert len(ORDER) == n and all(at[j] < at[i] for i in range(n) for j in pre[i])
+        return [ops[i] for i in ORDER]
 
-    def lat(j, i):
-        a, b = ops[j], ops[i]
-        if a["q"] is None: return HOP
-        if b["q"] is None: return a["lat"]
-        if a["q"] == b["q"] and (a["q"] == "P" or (a["q"] == "G" and j in b["after"])): return 0.0
-        return a["lat"] + HOP
-    edges = [[(j, lat(j, i)) for j in pre[i]] for i in range(n)]
+    def graph(fc, fg, hop, far):
+        c = [o["c"] * (1.0 if o["dma"] or o["lat"] else fg if o["ind"] else fc) for o in ops]
+        lt = [o["lat"] + (far if o["lat"] and not o["dma"] else 0.0) for o in ops]
+        ed = []
+        for i in range(n):
+            e = {j: c[j] + (lt[j] if qs[i] is None else 0.0) for j in ops[i]["after"]}
+            for j in pre[i]:
+                e[j] = c[j] + (0.0 if qs[i] == qs[j] == "P" else lt[j] + hop)
+            ed.append(list(e.items()))
+        return c, ed
+    guess = [graph(*x) for x in GUESS]
+    c, edges = guess[0]
     back = [[] for _ in range(n)]
     for i in range(n):
         for j, l in edges[i]:
-            back[j].append((i, l))
+            back[j].append((i, l - c[j] + c[i]))
 
-    def place(seq, ed):
-        st, busy = [0.0] * n, {}
-        for i in seq:
-            o = ops[i]; t = max([st[j] + ops[j]["c"] + l for j, l in ed[i]] + [0.0])
-            if o["q"] is not None:
-                l = busy.setdefault(o["q"], []); lo, k = 0, len(l)
+    def place(key, ed, to):
+        left = [len(e) for e in ed]; st, busy = [0.0] * n, {q: ([], []) for q in "VAPGS"}
+        ready = sorted(((key[i], i) for i in range(n) if not left[i]), reverse=True)
+        while ready:
+            i = ready.pop()[1]; t = 0.0
+            for j, l in ed[i]:
+                if st[j] + l > t: t = st[j] + l
+            if qs[i] is not None:
+                a, z = busy[qs[i]]; lo, k, d = 0, len(a), c[i] - 1e-9
                 while lo < k:
                     mid = (lo + k) // 2
-                    if l[mid][1] <= t: lo = mid + 1
+                    if z[mid] <= t: lo = mid + 1
                     else: k = mid
-                while k < len(l) and l[k][0] < t + o["c"] - 1e-9:
-                    t = max(t, l[k][1]); k += 1
-                l.insert(k, (t, t + o["c"]))
+                while k < len(a) and a[k] < t + d:
+                    if z[k] > t: t = z[k]
+                    k += 1
+                a.insert(k, t); z.insert(k, t + c[i])
             st[i] = t
+            for j, _ in to[i]:
+                left[j] -= 1
+                if not left[j]:
+                    x = (key[j], j); lo, k = 0, len(ready)
+                    while lo < k:
+                        mid = (lo + k) // 2
+                        if ready[mid] > x: lo = mid + 1
+                        else: k = mid
+                    ready.insert(lo, x)
         return st
-    pr = [o["c"] for o in ops]
+
+    def worth(st):
+        seq = sorted(range(n), key=lambda i: (st[i], i)); tot = 0.0
+        for (cc, ed), x in zip(guess, GUESS):
+            s, free = [0.0] * n, {}
+            for i in seq:
+                t = free.get(qs[i], 0.0)
+                for j, l in ed[i]:
+                    if s[j] + l > t: t = s[j] + l
+                s[i] = t
+                if qs[i] is not None: free[qs[i]] = t + cc[i]
+            tot += max(s) / (x[0] + x[1])
+        return tot, seq
+    pr = list(c)
     for i in range(n - 1, -1, -1):
         for j, l in edges[i]:
-            pr[j] = max(pr[j], ops[j]["c"] + l + pr[i] + 1e-6)
-    st = place(sorted(range(n), key=lambda i: (-pr[i], i)), edges)
-    best = (max(st), st)
-    for _ in range(PASSES):
-        sb = place(sorted(range(n), key=lambda i: (-st[i] - ops[i]["c"], -i)), back)
-        st = place(sorted(range(n), key=lambda i: (-sb[i] - ops[i]["c"], i)), edges)
-        best = min(best, (max(st), st))
-    st = best[1]
-    return [ops[i] for i in sorted(range(n), key=lambda i: (st[i], i))]
+            pr[j] = max(pr[j], l + pr[i])
+    tags = sorted(set(o["tag"] for o in ops)); tg = [tags.index(o["tag"]) for o in ops]
+    rng = numpy.random.default_rng(SEED); best = None; lead = (0.0, [LEAD.get(x[:-1], 0.0) for x in tags])
+    for k in range(PASSES):
+        x = list(lead[1])
+        for _ in range(k and 2):
+            x[int(rng.integers(len(x)))] += float(rng.normal()) * (1.0, 4.0, 10.0)[k % 3]
+        st = place([-pr[i] - x[tg[i]] for i in range(n)], edges, back)
+        w = worth(st) + (st,)
+        if k == 0 or w[0] < lead[0] + 0.1: lead = (w[0], x)
+        best = min(best or w, w)
+    cur = best
+    for k in range(JOGS):
+        st = cur[2]; t0 = rng.random() * max(st); t1 = t0 + 3.0 + 12.0 * rng.random()
+        near = [i for i in range(n) if t0 <= st[i] < t1]; key = list(st)
+        if k % 2:
+            x = tg[near[int(rng.integers(len(near)))]]; d = float(rng.normal()) * (1.0, 3.0)[k // 2 % 2]
+            for i in near:
+                if tg[i] == x: key[i] += d
+        else:
+            for i, d in zip(near, (rng.random(len(near)) * (0.3, 1.0)[k // 2 % 2]).tolist()):
+                key[i] += d
+        if k % 16 == 0:
+            sb = place([-key[i] - c[i] for i in range(n)], back, edges); key = [-sb[i] - c[i] for i in range(n)]
+        st = place(key, edges, back); w = worth(st) + (st,)
+        if w[0] < cur[0] + WARM * (1 - k / JOGS) * rng.random(): cur = w
+        best = min(best, w)
+    ps = [set(j for j, _ in e) for e in edges]
+
+    def replay(seq):
+        tot, why = 0.0, []
+        for (cc, ed), x in zip(guess, GUESS):
+            s, by, free = [0.0] * n, [-1] * n, {}
+            for i in seq:
+                t, y = free.get(qs[i], (0.0, -1))
+                for j, l in ed[i]:
+                    if s[j] + l >= t: t = s[j] + l; y = j
+                s[i] = t; by[i] = y
+                if qs[i] is not None: free[qs[i]] = (t + cc[i], i)
+            tot += s[n - 1] / (x[0] + x[1]); why.append(by)
+        return tot, why, seq
+    cur = top = replay(best[1])
+    for k in range(SWAPS):
+        by = cur[1][k % len(GUESS)]; v = n - 1; pairs = []
+        while by[v] >= 0:
+            if by[v] not in ps[v]: pairs.append((by[v], v))
+            v = by[v]
+        u, v = pairs[int(rng.integers(len(pairs)))]
+        seq = cur[2]; a, z = seq.index(u), seq.index(v); need, held, head, rest = set(ps[v]), set(), [], []
+        for x in seq[z - 1:a:-1]:
+            if x in need or qs[x] in held:
+                head.append(x); need |= ps[x]; held.add(qs[x] or x)
+            else:
+                rest.append(x)
+        if u in need or qs[u] in held: continue
+        new = replay(seq[:a] + head[::-1] + [v, u] + rest[::-1] + seq[z + 1:])
+        if new[0] < cur[0] + HEAT * (1 - k / SWAPS) * rng.random():
+            cur = new
+            if cur[0] < top[0]: top = cur
+    st, free = [0.0] * n, {}
+    for i in top[2]:
+        st[i] = max([free.get(qs[i], 0.0)] + [st[j] + l for j, l in edges[i]])
+        if qs[i] is not None: free[qs[i]] = st[i] + c[i]
+    DBG2[:] = [dict(zip(tags, lead[1])), best[0]]
+    DBG[:] = [max(st), st, ops, [[(j, l - c[j]) for j, l in e] for e in edges], top[0]]
+    ORDER.extend(top[2])
+    return [ops[i] for i in ORDER]
 
 
 def emit(g, T, ops):
@@ -187,7 +285,7 @@ def rank_program(g, core, T, topo):
     to = order[rank]
     fr = [[q for q in range(n) if q != rank and order[q][i] == rank][0] for i in range(3)]
     dto = [(r - rank) % n for r in to]
-    ops, nd, rc, sends = [], [0], {}, []
+    ops, nd, rc, sends, sent, prev, tag = [], [0], {}, [], {}, {}, ["load"]
 
     def ap(d):
         if not isinstance(d, tuple):
@@ -222,7 +320,12 @@ def rank_program(g, core, T, topo):
                 w.append(out[1]); r.append(out[2])
             else:
                 w.append(out)
-        ops.append({"q": q, "f": f, "r": r, "w": w, "tok": tok, "dma": dma, "c": c, "lat": lat, "after": list(after)})
+        ops.append({"q": q, "f": f, "r": r, "w": w, "tok": tok, "dma": dma, "c": c, "lat": lat, "after": list(after), "tag": tag[0],
+                    "ind": any(isinstance(d, tuple) and d[0] == "ind" for d in [out] + ins)})
+        if w and q in ("V", "A") and w[0][0] in SEQ:
+            k = (q, w[0][0])
+            if k in prev: ops[-1]["after"].append(prev[k])
+            prev[k] = len(ops) - 1
 
     def tt(out, a, b, o):
         ps = a[0] != "ind" and "psum" in (SCRATCH[a[0]][0], SCRATCH[b[0]][0])
@@ -248,9 +351,14 @@ def rank_program(g, core, T, topo):
         op("P", lambda q: q.matmul(ap(out), ap(l), ap(r), start, stop), out, [l, r],
            max(min(64, width(l)), w or width(r)) * PEC * (4 if SCRATCH[l[0]][2] == "float32" else 1))
 
-    def mms(out, terms):
+    def mms(out, terms, whole=True):
         for j, (l, r) in enumerate(terms):
             mm(out, l, r, j == 0, j == len(terms) - 1)
+        if whole: unit(len(terms))
+
+    def unit(k):
+        l = ops[-k:]; del ops[-k:]
+        op("P", lambda q: [o["f"](q) for o in l][-1], l[0]["w"][0], [d for o in l for d in o["r"]], sum(o["c"] for o in l))
 
     def iota(out, pat, base, cm):
         c = 0.13 + 2 * width(out) * CY
@@ -259,303 +367,321 @@ def rank_program(g, core, T, topo):
         else:
             op("G", lambda q: q.iota(ap(out), pat, base, cm, allow_small_or_imprecise_dtypes=True), out, [], c)
 
+    def fill(out, v): iota(out, [[0, width(out)]], v, 0)
+
     def diag(out, a, v, shift):
         op("G", lambda q: q.affine_select(ap(out), ap(a), [[1, 128]], O.not_equal, v, -shift, -1), out, [a], 0.17 + 256 * CY)
 
-    def dma(q, out, a, more=0.0):
+    def rowsel(out, a, v, r):
+        op("G", lambda q: q.affine_select(ap(out), ap(a), [[-16, 8], [0, 16]], O.not_equal, v, -r, 1), out, [a], 0.17 + 256 * CY)
+
+    def dma(q, out, a, more=0.0, wait=()):
         nd[0] += 1
-        op(q, lambda e: e.dma_start(ap(out), ap(a)), out, [a], DISS, ("d%d" % (nd[0] - 1), 16), True, LDMA + more)
+        op(q, lambda e: e.dma_start(ap(out), ap(a)), out, [a] + list(wait), DISS, ("d%d" % (nd[0] - 1), 16), True, LDMA + more)
 
-    def engines(src, dst, e0, e1):
-        el = topo.engines(src, dst)
-        return el[e0 * len(el) // 16:e1 * len(el) // 16]
+    def send(peer, dst, src, rs, ls, more=0.0):
+        c = T.cores[peer]; rid, pid, _ = topo.addr(c)
+        rc[ls] = rc.get(ls, 0) + len(topo.engines(core, c))
+        op("G", lambda q: q.remote_dma(ap(dst), ap(src), T.sem[rs], T.sem[ls], pid, rid, topo.mask(core, c)), None, [src],
+           ISS + (0 if sends else FIRST), (ls, rc[ls]), False, RDMA + width(src) * BYTE + more, sends[-1:])
+        sends.append(len(ops) - 1); sent[rs] = len(ops) - 1
 
-    def send(trs, ls):
-        l = []
-        for peer, dst, src, rs, e0, e1 in trs:
-            c = T.cores[peer]; rid, pid, _ = topo.addr(c); el = engines(core, c, e0, e1)
-            l.append((dst, src, rs, pid, rid, sum(1 << e for e in el)))
-            rc[ls] = rc.get(ls, 0) + len(el)
-        if len(l) == 1:
-            f = lambda q: q.remote_dma(ap(l[0][0]), ap(l[0][1]), T.sem[l[0][2]], T.sem[ls], l[0][3], l[0][4], l[0][5])
-        else:
-            f = lambda q: q.remote_dma_fused([RemoteDMATransfer(dst_ids=[DstId(rid=x[4], pnc=x[3])], dma_engine_mask=x[5], remote_sem=T.sem[x[2]], src=ap(x[1]), dst=ap(x[0]))
-                                              for x in l], local_sem=T.sem[ls])
-        op("G", f, None, [x[1] for x in l], ISS + (0 if sends else FIRST), (ls, rc[ls]), False, RDMA + sum(width(x[1]) for x in l) * 7e-4, sends[-1:])
-        sends.append(len(ops) - 1)
-
-    def recv(peer, dst, rs, parts):
-        rc[rs] = rc.get(rs, 0) + sum(len(engines(T.cores[peer], core, e0, e1)) for e0, e1 in parts)
-        op(None, None, dst, [], 0.0, (rs, rc[rs]), False, 0.0, sends[-3:])
-
-    def send1(k): send([(fr[i], S("LND", LO[i] + a, LO[i] + z), S("AW", FB[i] + a, FB[i] + z), "a%d" % i, e0, e1) for i, a, z, e0, e1 in CALL1[k]], "la%d" % k)
-    def send2(k): send([(to[i], S("AW", FB[i] + a, FB[i] + z), S("XR", a, z), "x%d" % i, e0, e1) for i, a, z, e0, e1 in CALL2[k]], "lx%d" % k)
-
-    def recv1():
-        for i in range(3):
-            recv(to[i], S("LND", LO[i], LO[i] + 256 * (i + 1)), "a%d" % i, [x[3:] for c in CALL1 for x in c if x[0] == i])
-
-    def recv2():
-        for i in range(3):
-            recv(fr[i], S("AW", FB[i], FB[i] + 256 * (i + 1)), "x%d" % i, [x[3:] for c in CALL2 for x in c if x[0] == i])
+    def recv(peer, dst, rs):
+        rc[rs] = rc.get(rs, 0) + len(topo.engines(T.cores[peer], core))
+        op(None, None, dst, [], 0.0, (rs, rc[rs]), False, 0.0, [sent[rs]])
 
     def P(b, c0=0, c1=256, step=1, p=(0, 128, 1)): return S("P%d" % b, c0, c1, step, p)
     def col(name, j): return S(name, j, j + 1)
-    names = ["I", "ROT", "ROTM", "RINV", "N3", "N2", "N1", "I64", "D01", "DC0", "DC1", "DC2", "R01", "RDL", "R45", "NR45", "R6", "R68", "RIV", "RB", "RC", "RU",
-             "WD", "WF", "DF", "GT", "WE"]
+    names = ["I", "ROT", "ROTM", "ROT23", "RINV", "NRI", "N3", "N2", "N1", "I64", "NB", "D01", "R01", "R23", "R45", "NR45", "R6", "RKB", "RIV", "RB", "RC", "RU",
+             "WD", "WF", "DF", "GT", "WE", "RZ", "I16"]
     def mb(x): return S("MBF", 128 * names.index(x), 128 * names.index(x) + 128)
-    n16 = ["I", "NI", "BK", "TRI", "DM", "B15"]
+    n16 = ["I", "BK", "B15"]
     def mf(x): return S("MF", 128 * n16.index(x), 128 * n16.index(x) + 128)
-    ny = ["1", "45", "6", "DL", "PH", "LP"]
+    ny = ["1", "45", "236", "23", "01"]
     def Y(x, k): return S("YB", 144 * ny.index(x) + 15 - k, 144 * ny.index(x) + 143 - k)
-    def ct(j): return S("CT", 256 * j, 256 * j + 256)
-    def row(name, r, w): return S(name, 0, w, 1, (r, 128, 16))
+    def row(name, r, c0, w): return S(name, c0, c0 + w, 1, (r, 128, 16))
     def b2(j): return S("B2", 128 * j, 128 * j + 128)
     def blk(name, j): return S(name, 256 * j, 256 * j + 256)
     def sub(d, c): return d[:2] + (d[2] + c[0], d[2] + c[1], 1)
     def xp(j): return S("AW", XB + 256 * j, XB + 256 * j + 256)
-    kcol = col("KC", 0); io = S("IO", 0, 128); p8 = (0, 8, 1); Y1 = S("YB", 0, 144)
+    def fw(i): return S("AW", FB[i], FB[i] + 256 * (i + 1))
+    def il(c0, w): return S("IL", I0 + c0, I0 + c0 + w)
+    def kc(j): return col("KC", j)
+    def m16(j): return col("M16", j)
+    def m2(j): return col("M2", j)
+    kcol = kc(0); io = S("IO", 0, 128); p8 = (0, 8, 1); Y1 = S("YB", 0, 144)
     def FX(b, f): return S("FX%d" % b, 256 * f, 256 * f + 256)
 
-    dma("S", S("SN"), T["snd"][:]); dma("S", S("DI", 0, 128), T["ti"][:]); dma("A", S("DI", 288, 416), T["kd"][:]); dma("A", S("A0"), T["a0"][:], 1.0)
-    dma("S", S("CA"), T["ca"][:], 0.5); dma("A", S("BE", 0, 1), T["be"][:]); dma("S", S("KW", 0, E), T["k0"][:], 1.0)
-    dma("S", S("DI", 128, 160), T["bg"][:]); dma("S", S("DI", 416, 448), T["cl"][:]); dma("S", S("DI", 448, 528), T["us"][:]); dma("S", S("DI", 160, 288), T["lp"][:])
-    iota(col("KI", 0), [[1, 1]], 0, 1); iota(S("I64"), [[1, 64]], 0, 0); iota(S("IO"), [[1, 144]], 0, -1)
-    iota(S("JJ"), [[0, 16], [1, 16]], 0, 0); iota(S("H0"), [[1, 33], [0, 8]], 0, 0); iota(S("DU", 0, 16), [[16, 16]], 0, 0)
-    iota(S("G8", 0, 128, 1, p8), [[1, 8], [0, 16]], 0, -1)
+    dma("S", S("SN"), T["snd"][:], -0.5); dma("A", S("DI", 0, 128), T["ti"][:], -0.4); dma("S", S("DI", 288, 416), T["kd"][:], -0.3); dma("S", S("A0", 0, E), T["a0"][:], 1.3)
+    ops[2]["after"], ops[3]["after"] = [0], [2]
+    dma("S", S("KW", 0, E), T["k0"][:], 2.0, [S("SN")]); dma("S", S("CA"), T["ca"][:], 0.5, [S("A0", 0, E)]); dma("S", S("BE", 0, 1), T["be"][:], 0.0, [S("CA")])
+    for c0, c1, x in ((128, 160, "bg"), (416, 448, "cl"), (448, 528, "us"), (160, 288, "lp")):
+        dma("S", S("DI", c0, c1), T[x][:], 0.0, [S("CA")])
+    iota(col("KI", 0), [[1, 1]], 0, 1); iota(S("I256"), [[1, 256]], 0, 0); iota(S("IO"), [[1, 144]], 0, -1)
     ms(S("Z"), 0.0)
-    for x, v in (("I", 1.0), ("N3", -3.0), ("N2", -2.0), ("N1", -1.0), ("I64", 64.0)):
+    diag(mb("ROT"), S("Z"), 1.0, 16); diag(mb("ROT"), mb("ROT"), 1.0, -112)
+    for x, v in (("I", 1.0), ("I64", 64.0), ("I16", 16.0), ("N3", -3.0), ("N2", -2.0), ("N1", -1.0), ("NB", -BIG)):
         diag(mb(x), S("Z"), v, 0)
-    diag(mb("ROT"), S("Z"), 1.0, 16); diag(mb("ROT"), mb("ROT"), 1.0, -112); diag(mb("RINV"), S("Z"), 1.0, -16); diag(mb("RINV"), mb("RINV"), 1.0, 112)
+    diag(mb("RINV"), S("Z"), 1.0, -16); diag(mb("RINV"), mb("RINV"), 1.0, 112); diag(mb("NRI"), S("Z"), -1.0, -16); diag(mb("NRI"), mb("NRI"), -1.0, 112)
     diag(b2(0), S("Z"), -1.0, 1)
     ts(col("KI", 1), col("KI", 0), 15, O.bitwise_and); cp(kcol, col("KI", 1))
-    ts(S("M16"), S("I64", 0, 16), kcol, O.is_equal); tt(S("M2"), S("M16", 0, 16, 2), S("M16", 1, 16, 2), O.add)
-    tt(S("KC", 1, 3), S("M16", 0, 2), S("M16", 2, 4), O.add)
-    ts(S("PH", 0, 64), S("I64"), col("KC", 2), O.mult); act(S("IL", 0, 64), S("I64"), scale=col("M16", 1))
-    for j in range(5):
-        ts(col("KC", 16 + j), col("KC", 1), float(64 << j), O.mult); act(col("KC", 24 + j), col("M16", 0), scale=float(64 << j))
-        ts(S("PH", 64 << j, 128 << j), S("PH", 0, 64 << j), col("KC", 16 + j), O.add)
-        act(S("IL", 64 << j, 128 << j), S("IL", 0, 64 << j), AF.Identity, col("KC", 24 + j))
-    ts(col("KC", 3), col("M2", 0), -1.0, O.mult, 1.0, O.add)
-    tt(col("KC", 4), col("M2", 1), col("M2", 0), O.subtract)
-    ts(col("KC", 8), col("M16", 2), float(XB), O.mult); ts(col("KC", 11), col("M16", 0), 2048.0, O.mult)
+    ts(S("M16"), S("I256", 0, 16), kcol, O.is_equal); tt(S("M2"), S("M16", 0, 16, 2), S("M16", 1, 16, 2), O.add)
+    iota(S("KH", 0, 16), [[256, 16]], -CD, 0); ts(S("KH", 16, 32), S("KH", 0, 16), m16(2), O.mult)
+    ts(S("KH", 32, 48), S("KH", 0, 16), float(XB), O.add, m16(2), O.mult)
+    tt(kc(1), m16(1), m16(3), O.add); ts(S("B256"), S("I256"), kc(1), O.mult)
+    for j in range(3):
+        ts(blk("XD", j), S("B256"), col("KH", 32 + j), O.add)
+    for j in range(4):
+        ts(S("PH", 128 * j, 128 * j + 128), S("B256", 0, 256, 2), col("KH", 16 + j), O.add)
+    for j in range(2, 8):
+        ts(blk("PH", j), S("B256"), col("KH", 18 + j), O.add)
+    ms(S("IL", 0, I0 + E), 1.0)
+    ts(S("DB", 816, 944), S("Z"), kcol, O.add, 128.0, O.mult); cp(S("DB", 944, 1072), S("I256", 0, 128))
+    tt(kc(2), m2(0), m2(1), O.add); ts(kc(4), kc(2), -1.0, O.mult, 1.0, O.add)
     for i in range(3):
-        ts(col("KC", 5 + i), col("M16", 2), float(FB[i] - XB), O.mult, col("KC", 11), O.add)
-    ts(col("KC", 9), col("M16", 0), -1.0, O.mult, 1.0, O.add); ts(col("KC", 10), col("KC", 9), 1024.0, O.mult)
-    ts(col("KC", 12), col("M16", 15), -1.0, O.mult, 1.0, O.add)
+        ts(kc(16 + i), m16(0), float(E + 256 * (dto[i] - 1)), O.mult); ts(kc(5 + i), m16(2), float(FB[i] - XB), O.mult, kc(16 + i), O.add)
     ts(S("J"), S("IO"), kcol, O.add); ts(Y1, S("J"), 15.0, O.is_equal)
-    ts(b2(4), S("J", 0, 128), 0.0, O.is_ge); ts(b2(5), S("J", 0, 128), 15.0, O.is_le); tt(S("BK"), b2(4), b2(5), O.mult)
-    for j, v in enumerate((1.0, -2048.0, -1408.0, -10240.0)):
-        ms(ct(j), v)
-    ts(mb("ROTM"), mb("ROT"), col("KC", 3), O.mult); ts(mb("D01"), mb("I"), col("M2", 0), O.mult)
-    for i in range(3):
-        ts(mb("DC%d" % i), mb("I"), col("KC", 5 + i), O.mult)
-    for x, c in (("45", col("M2", 2)), ("6", col("M16", 6)), ("DL", col("KC", 4)), ("PH", col("M2", 1)), ("LP", col("M2", 4))):
+    act(b2(4), S("J", 0, 128), AF.Abs, -7.5); ts(S("BK"), b2(4), 8.0, O.is_lt)
+    act(mb("ROTM"), mb("ROT"), scale=kc(4)); act(mb("D01"), mb("I"), scale=m2(0)); act(mb("ROT23"), mb("ROT"), scale=m2(1))
+    ts(kc(3), m16(6), 0.0625, O.mult, m2(1), O.add)
+    for x, c in (("45", m2(2)), ("236", kc(3)), ("23", m2(1)), ("01", m2(0))):
         act(S("YB", 144 * ny.index(x), 144 * ny.index(x) + 144), Y1, scale=c)
-    for x, c, v in (("R01", col("M2", 0), 1.0), ("RDL", col("KC", 4), 1.0), ("R45", col("M2", 2), 1.0), ("R6", col("M16", 6), 1.0), ("RB", col("M2", 5), 1.0),
-                    ("RC", col("M16", 12), 1.0), ("RU", col("M16", 13), 1.0), ("RIV", col("M16", 7), 1.0), ("NR45", col("M2", 2), -1.0), ("R68", col("M16", 6), 8.0),
-                    ("WE", col("M16", 15), -16384.0)):
-        ts(mb(x), S("BK"), c, O.mult, v, O.mult) if v != 1.0 else act(mb(x), S("BK"), scale=c)
-    act(mb("WF"), S("BK"), scale=16384.0); act(S("I32"), mb("I"))
-    cp(S("Y16"), Y1); cp(mf("I"), mb("I")); cp(mf("NI"), mb("N1")); cp(mf("BK"), S("BK")); ts(mf("B15"), S("BK"), col("M16", 15), O.mult)
-    ts(b2(6), io, 0.0, O.is_ge, 256.0, O.mult); tt(mf("TRI"), b2(6), S("BK"), O.mult)
-    ts(b2(7), io, 1.0, O.is_ge, 16384.0, O.mult); tt(mb("WD"), b2(7), S("BK"), O.mult)
-    ts(b2(1), b2(0), col("KC", 12), O.mult); diag(mb("DF"), b2(1), 1.0, 0)
-    ts(b2(2), mb("I"), col("KC", 9), O.mult); tt(mf("DM"), b2(2), b2(1), O.add)
+    ts(kc(8), m16(8), -10240.0, O.mult, m16(9), O.add); ts(kc(9), m16(6), 8.0, O.mult, kc(8), O.add)
+    ts(kc(10), m16(8), -1408.0, O.mult, m2(0), O.add); ts(kc(13), m2(2), -1.0, O.mult)
+    for x, c in (("RKB", kc(9)), ("NR45", kc(13)), ("R01", kc(10))):
+        act(mb(x), S("BK"), scale=c)
+    for x, v, rows in (("R23", 1.0, (2, 3)), ("R45", 1.0, (4, 5)), ("R6", 1.0, (6,)), ("RB", 1.0, (10, 11)), ("RC", 1.0, (12,)),
+                       ("RU", 1.0, (13,)), ("WE", -BIG, (15,)), ("RZ", -2.0 ** 17, (8,))):
+        for j, r in enumerate(rows):
+            rowsel(mb(x), mb(x) if j else S("Z"), v, r)
+    rowsel(mb("RIV"), S("Z"), -100.0, 7); rowsel(mb("RIV"), mb("RIV"), 100.0, 8)
+    act(mb("WF"), S("BK"), scale=BIG); act(S("I32"), mb("I"))
+    cp(S("Y16"), Y1); cp(mf("I"), mb("I")); cp(mf("BK"), S("BK")); ts(mf("B15"), S("BK"), m16(15), O.mult)
+    iota(b2(5), [[0, 8], [1, 16]], 1, 0); tt(b2(2), b2(5), S("BK"), O.mult)
+    for k in range(16):
+        ts(S("TK", 128 * k, 128 * k + 128), b2(2), k + 0.5, O.is_gt)
+    ts(b2(3), io, 1.0, O.is_ge, BIG, O.mult); tt(mb("WD"), b2(3), S("BK"), O.mult)
+    ts(kc(12), m16(15), -1.0, O.mult, 1.0, O.add); act(b2(1), b2(0), scale=kc(12)); diag(mb("DF"), b2(1), 1.0, 0)
+    act(S("D32"), mb("DF")); act(S("L32"), S("BK"), scale=m16(15))
+    tt(S("DC", 1, 16), S("M16", 1, 16), S("M16", 0, 15), O.subtract)
+    for k in range(1, 16):
+        ts(S("DK", 128 * k, 128 * k + 128), S("BK"), col("DC", k), O.mult)
+    iota(S("G8", 0, 128, 1, p8), [[1, 8], [0, 16]], 0, -1)
     GT = mb("GT")[:1] + (p8,) + mb("GT")[2:]
     ts(GT, S("G8", 0, 128, 1, p8), 0.0, O.is_equal)
-    ms(S("IL", INV, LB), 0.0); ts(col("IL", INV), col("M16", 7), 100.0, O.mult); ms(S("AW", DA, AWN), 0.0); ms(S("KW", E, E + 256), 0.0); iota(S("AUX"), [[0, E]], 0, 0)
-    ts(S("JJ"), S("JJ"), kcol, O.is_equal, 2.0 ** 30 + 8192, O.mult); act(S("CM"), S("JJ"), AF.Identity, -2.0 ** 30)
-    ms(S("RS"), 2.0 ** 30); ms(S("RS", 0, 256, 16), -2.0 ** 30); ms(S("RM"), -0.0625); ms(S("RM", 0, 256, 16), 2.0 ** 20)
-    ts(S("DU", 0, 16), S("DU", 0, 16), kcol, O.add, float(DA - CD), O.add)
-    for j, v in ((1, E + 1), (2, LB - 2047), (3, LB - 2047 + 256)):
-        ts(S("DU", 16 * j, 16 * j + 16), S("DU", 0, 16), float(v - DA + CD), O.add)
-    ms(S("H0", 0, 264, 8), 0.0)
-    for j in range(8):
-        ms(S("H1", j, 264, 8), 1.0 / math.factorial(7 - j))
-    act(S("H0"), S("H0"), scale=col("BE", 0)); act(col("BE", 1), col("BE", 0), scale=-1.0)
-    scan(S("H2"), S("H0"), S("H1"), 0.0, O.mult, O.add)
-    act(col("SQ", 0), col("H2", 263))
-    for j in range(5):
-        act(col("SQ", j + 1), col("SQ", j), scale=col("SQ", j))
-    op("V", lambda q: q.reciprocal(ap(col("SQ", 6)), ap(col("SQ", 5))), col("SQ", 6), [col("SQ", 5)], 0.2)
-    act(S("TE", 0, 32), S("H2", 7, 256, 8), scale=col("SQ", 6))
-    for j in range(6):
-        act(S("TE", 32 << j, 64 << j), S("TE", 0, 32 << j), scale=col("SQ", j))
-    ms(col("TE", 0), 0.0)
+    tt(kc(14), m16(8), m16(0), O.subtract); cp(col("IL", I0 - 1), kc(14))
+    fill(S("IL", LB, ILN), 0); cp(col("IL", LB + E), kc(14))
+    fill(S("AW", 0, 1024), 0); fill(S("AW", 2560, XB), 0); fill(S("AW", FB[0], AWN), 0); fill(S("KW", E, E + 256), 0)
+    iota(blk("TT", 0), [[0, 16], [1, 16]], 0, 0); iota(blk("TT", 1), [[1, 256]], E + 1 - int(BIG), 0); iota(S("DU"), [[16, 32]], 1408, 0)
+    ts(S("CM"), blk("TT", 0), kcol, O.subtract, 2.0 ** 26, O.mult); act(blk("TT", 2), S("CM"), AF.Abs); tt(S("RS"), blk("TT", 1), blk("TT", 2), O.subtract)
+    ms(S("RM"), -0.0625); ms(S("RM", 0, 256, 16), 2.0 ** 20); ts(S("DU"), S("DU"), kcol, O.add)
+    act(col("BE", 1), col("BE", 0), scale=-1.0)
     for i in range(3):
         cp(S("uS", 16 * i, 16 * i + 16), S("SN", 16 * (dto[i] - 1), 16 * dto[i]))
-    ts(S("DH", 576, 704), S("DI", 160, 288), 0.0, O.is_lt, 2817.0, O.mult); tt(S("DI", 160, 288), S("DI", 160, 288), S("DH", 576, 704), O.add)
     for a, z in ((0, 128), (128, 288)):
-        ts(S("DH", a, z), S("DI", a, z), 8128, O.bitwise_and); ts(S("DH", 288 + a, 288 + z), S("DI", a, z), 63, O.bitwise_and)
-        cp(S("DB", a, z), S("DH", a, z)); cp(S("DB", 288 + a, 288 + z), S("DH", 288 + a, 288 + z))
+        cp(S("DB", a, z), S("DI", a, z)); tt(S("DB", 288 + a, 288 + z), S("DI", a, z), S("DB", a, z), O.subtract)
     cp(S("DB", 576, 704), S("DI", 288, 416)); cp(S("DB", 704, 816), S("DI", 416, 528))
-    for q, nm, r, c0, w in (("S", "IL", 4, 0, 128), ("A", "IL", 5, 288, 128), ("S", "IL", 6, 576, 128), ("S", "AUX", 10, 128, 32), ("S", "AUX", 11, 416, 32),
-                            ("S", "AUX", 12, 704, 32), ("S", "AUX", 13, 736, 80), ("S", "AUX", 8, 160, 128), ("S", "AUX", 9, 448, 128)):
-        dma(q, row(nm, r, 16 * w), S("DB", c0, c0 + w), 0.3)
+    ms(S("AUX"), 0.0)
+    for q, x, r, at, c0, w in (("A", "IL", 0, I0, 816, 128), ("A", "IL", 1, I0, 944, 128), ("S", "IL", 4, I0, 0, 128), ("A", "IL", 5, I0, 288, 128), ("S", "IL", 6, I0, 576, 128), ("S", "AUX", 10, 0, 128, 32), ("S", "AUX", 11, 0, 416, 32),
+                               ("S", "AUX", 12, 0, 704, 32), ("S", "AUX", 13, 0, 736, 80), ("S", "IL", 0, LB, 160, 128), ("S", "IL", 1, LB, 448, 128)):
+        dma(q, row(x, r, at, 16 * w), S("DB", c0, c0 + w), 0.3 if w == 128 else 0.0)
+    for i in range(3):
+        act(blk("G1", i), I(il(0, E), S("uS", 16 * i, 16 * i + 16)))
     for b in range(2):
-        ts(blk("CF", b), blk("CA", b), 2048.0, O.is_ge, -2048.0, O.add); cp(blk("cI", b), blk("CA", b))
-        tt(FX(b, 0), blk("CF", b), blk("CA", b), O.add)
-    for j in range(4):
-        act(S("AW", 512 * j, 512 * j + 512), S("A0", 512 * j, 512 * j + 512), AF.Identity, 15.0, -1.0)
-    for j in range(3):
-        act(xp(j), I(S("A0"), S("uS", 16 * j, 16 * j + 16)), AF.Identity, 15.0, -1.0)
-        mm(P(5 + j), mb("ROT"), xp(j), True, True)
-        act(blk("XR", j), P(5 + j))
-    send2(0)
-    ts(S("XD"), S("PH", 0, 768), col("M2", 1), O.mult, col("KC", 8), O.add)
+        cp(blk("cI", b), blk("CA", b)); ts(FX(b, 2), blk("cI", b), -1408.0, O.add)
+    for i in range(3):
+        act(xp(i), I(S("A0", 0, E), S("uS", 16 * i, 16 * i + 16)))
+        mm(P(i), mb("ROT"), xp(i), True, True)
+        act(blk("XR", i), P(i))
+        send(to[i], blk("A0", 7 + dto[i]), blk("XR", i), "m%d" % i, "lm%d" % i)
+    act(S("AW", 0, 1024, 2), S("A0", 0, 512))
     for i in (2, 1, 0):
         cp(I(S("PH"), S("uS", 16 * i, 16 * i + 16)), blk("XD", i))
-    act(S("G1"), I(S("IL", 0, E), S("uS"))); cp(S("G2"), I(S("PH"), S("uS")))
     for i in range(3):
+        if i: cp(blk("G2", i), I(S("PH"), S("uS", 16 * i, 16 * i + 16)))
         c0 = 256 * (dto[i] - 1)
-        mms(P(i), [(mb("D01"), S("IL", c0 + 1, c0 + 257)), (mb("DC%d" % i), ct(0)), (mb("ROTM"), blk("G1", i)), (mb("ROT"), blk("G2", i))])
-        act(blk("IM", i), P(i)) if i != 1 else cp(blk("IM", i), P(i))
-        send([(to[i], S("IL", E + c0, E + c0 + 256), blk("IM", i), "n%d" % i, 0, 16)], "ln%d" % i)
-    dma("S", row("IL", 2, E), row("PH", 2, E), 0.3); dma("A", row("IL", 3, E), row("PH", 3, E), 0.3)
+        mms(P(5 + i), [(mb("D01"), blk("XD", 0)), (mb("ROTM"), blk("G1", i)), (mb("ROT23"), blk("G2" if i else "XD", i))], False)
+        act(blk("IM", i), P(5 + i), AF.Identity, kc(5 + i))
+        send(to[i], il(E + c0, 256), blk("IM", i), "n%d" % i, "ln%d" % i)
+    dma("S", row("IL", 2, I0, E), row("PH", 2, 0, E), 0.3); dma("A", row("IL", 3, I0, E), row("PH", 3, 0, E), 0.3)
     for i in range(3):
-        c0 = E + 256 * ((rank - fr[i]) % n - 1)
-        recv(fr[i], S("IL", c0, c0 + 256), "n%d" % i, [(0, 16)])
-    for k in range(1, len(CALL2)):
-        send2(k)
-    recv2()
-    for j, (c0, w) in enumerate(((0, 512), (512, 512), (1024, 256))):
-        mm(P(3 + j % 2, 0, w), mb("RU"), S("AUX", c0, c0 + w), True, True); act(S("U", c0, c0 + w), P(3 + j % 2, 0, w))
+        d = (rank - fr[i]) % n
+        recv(fr[i], blk("A0", 7 + d), "m%d" % i); recv(fr[i], il(E + 256 * (d - 1), 256), "n%d" % i)
+    dma("S", S("AW", 1024, 2560), T["a0"][:, 512:E], 1.0, [il(E, 768)])
+    for c0, w in ((0, 512), (512, 512), (1024, 256)):
+        mm(P(3, 0, w), mb("RU"), S("AUX", c0, c0 + w), True, True); act(S("U", c0, c0 + w), P(3, 0, w), scale=2.0 ** -8)
     mm(P(4, 0, 512), mb("RC"), S("AUX", 0, 512), True, True); ts(S("OH"), P(4, 0, 512), kcol, O.is_equal)
-    act(S("C7"), S("OH"), AF.Identity, 7.0, -1.0)
-    if not GVA: ts(S("NOH"), S("OH"), -1.0, O.mult)
-    mms(P(3, 0, 128), [(Y("LP", a), S("AUX", a, E, 16)) for a in range(16)]); cp(S("uL"), P(3, 0, 128))
+    if not GKA: act(S("C7"), S("OH"), AF.Identity, 7.0, -1.0)
 
     def floor32(ps, j, c=(0, 256)):
         act(sub(blk("AB", j), c), ps, AF.Abs); act(sub(blk("HI", j), c), sub(blk("AB", j), c), AF.Identity, 159.515625, 0.03125)
 
-    def lists(b, bk, c=(0, 256)):
-        w = c[1] - c[0]
-        ts(sub(blk("cB", b), c), sub(FX(b, 2), c), -1.0, O.add)
-        mms(P(bk[0], 0, w), [(mf("I"), sub(FX(b, 0), c)), (mf("I"), sub(FX(b, 1), c))])
-        mm(P(bk[1], 0, w), mf("DM"), sub(FX(b, 3), c), True, True); mm(P(bk[2], 0, w), mf("B15"), sub(FX(b, 3), c), True, True)
-        ts(sub(blk("cA", b), c), P(bk[0], 0, w), float(CD), O.add); ts(sub(blk("cR", b), c), P(bk[1], 0, w), col("KC", 10), O.add)
-        act(sub(blk("E15", b), c), P(bk[2], 0, w), AF.Exp, None, col("BE", 1))
-        for j in range(c[0], c[1], GA):
-            act(S("RG", 4096 * b + 16 * j, 4096 * b + 16 * (j + GA)), I(S("TE"), S("cR", 256 * b + j, 256 * b + j + GA)))
-
-    def agather(b):
-        for j, z in zip(KCUT[:-1], KCUT[1:]):
-            act(S("KG", 16 * j, 16 * z), I(S("AW", 0, DA), S("cA", 256 * b + j, 256 * b + z)), AF.Identity, 15.0, -1.0)
-
     def facts(b, who, bk, c):
-        own = sub(blk("IL", b), c); g0 = 4096 * b; w = c[1] - c[0]
+        own = il(256 * b + c[0], c[1] - c[0]); g0 = 4096 * b; w = c[1] - c[0]
         for j in range(c[0] // 32, c[1] // 32):
-            o, x = S("PR", g0 + 512 * j, g0 + 512 * j + 512), I(S("IL", 0, INV), S("cI", 256 * b + 32 * j, 256 * b + 32 * j + 32))
+            o, x = S("PR", g0 + 512 * j, g0 + 512 * j + 512), I(il(0, 2816), S("cI", 256 * b + 32 * j, 256 * b + 32 * j + 32))
             cp(o, x) if who[j] == "V" else act(o, x)
-        mm(P(bk[0], 0, w), mb("NR45"), own, True, False); mm(P(bk[1], 0, w), mb("R68"), own, True, False); mm(P(bk[2], 0, w), mb("I"), sub(ct(2), (0, w)), True, False)
-        for j in range(c[0] // 64, c[1] // 64):
-            for x, z in (("45", bk[0]), ("6", bk[1]), ("DL", bk[2])):
+        mm(P(bk[0], 0, w), mb("NR45"), own, True, False); mm(P(bk[1], 0, w), mb("RKB"), own, True, False)
+        for x, z in (("45", bk[0]), ("236", bk[2])):
+            for j in range(c[0] // 64, c[1] // 64):
                 for k in range(16):
-                    mm(P(z, 64 * j - c[0], 64 * j + 64 - c[0]), Y(x, k), S("PR", g0 + 1024 * j + k, g0 + 1024 * j + 1024, 16), False, j == c[1] // 64 - 1 and k == 15 and x != "6")
+                    mm(P(z, 64 * j - c[0], 64 * j + 64 - c[0]), Y(x, k), S("PR", g0 + 1024 * j + k, g0 + 1024 * j + 1024, 16),
+                       x == "236" and k == 0, k == 15 and (x == "236" or j == c[1] // 64 - 1))
+                unit(16)
+        ts(sub(FX(b, 0), c), P(bk[2], 0, w), 1.5 * 2 ** 23, O.add, 1.5 * 2 ** 23, O.subtract)
+        tt(sub(blk("KD", b), c), P(bk[2], 0, w), sub(FX(b, 0), c), O.subtract); mm(P(bk[1], 0, w), mb("I16"), sub(blk("KD", b), c), False, False)
         floor32(P(bk[0], 0, w), b, c); mm(P(bk[1], 0, w), mb("I64"), sub(blk("HI", b), c), False, True)
-        ts(sub(FX(b, 2), c), P(bk[1], 0, w), -10239.0, O.add); cp(sub(FX(b, 1), c), P(bk[2], 0, w)); cp(sub(FX(b, 3), c), sub(blk("AB", b), c))
-        lists(b, bk, c)
+        cp(sub(FX(b, 1), c), P(bk[1], 0, w)); cp(sub(blk("LG", b), c), sub(blk("AB", b), c))
+        ts(sub(blk("cB", b), c), sub(FX(b, 1), c), -1.0, O.add)
 
-    facts(0, "VAVAVAVA", (5, 6, 7), (0, 128)); facts(0, "VAVAVAVA", (0, 1, 2), (128, 256))
-    agather(0); facts(1, WHO1, (0, 1, 2), (0, 256))
-    for j in range(4):
-        act(S("IL", LB + 512 * j, LB + 512 * j + 512), I(S("IL", 0, LB), S("uL", 32 * j, 32 * j + 32)))
+    facts(0, WHO0, (0, 1, 2), (0, 128)); facts(0, WHO0, (5, 6, 7), (128, 256))
+    tag[0] = "facts"; facts(1, WHO1, (5, 6, 7), (0, 256))
+    ts(blk("cA", 1), FX(1, 0), float(CD), O.add)
 
-    def dedupe(key, k, bank):
-        mm(P(bank), mb("I"), S("CM"), True, False); mm(P(bank), mb("WE"), S("HIT"), False, False)
+    def first_wins(k, key, bank, u, add):
+        mm(P(bank), mb("I"), S("CM"), True, False); mm(P(bank), mb("WE"), S("HIT"), False, False); mm(P(bank), mf("BK"), blk("SEL", k), False, False)
         for b in range(16):
             w = 256 - 16 * b; off = 4096 * k + 256 * b
             ts(S("EQ", off, off + w), S("REP", 256 * k + 16 * b, 256 * k + 256), sub(key, (b, b + 1)), O.is_equal)
             if b < 15: mm(P(bank, 16 * b + 16, 256), mb("WF"), S("EQ", off + 16, off + w), False, False)
         mm(P(bank), mb("WD"), S("EQ", 4096 * k, 4096 * k + 4096, 16), False, True)
+        scan(blk("SD", k), S("RS"), P(bank), -2.0 ** 26, O.max, O.min)
+        ts(u, S("SD", 256 * k + 15, 256 * k + 256, 16), add + BIG, O.add)
+
+    def raised(name, win, u, b, cap, ps):
+        act(blk(name, 0), I(win, u)); mms(ps, [(mb("I"), blk("OH", b)), (mb("I"), blk(name, 0))])
+        act(blk(name, 1), ps, AF.Relu, cap, -1.0); act(blk(name, 2), blk(name, 1), AF.Identity, cap, -1.0)
+
+    def capped(out, ps, j, who):
+        if who == "V":
+            ts(out, ps, 15.0, O.min)
+        else:
+            act(blk("XT", j), ps, AF.Relu, 15.0, -1.0); act(out, blk("XT", j), AF.Identity, 15.0, -1.0)
+
+    def last_factor(t):
+        mm(P(EB[1]), mf("B15"), blk("LG", t), True, True); act(P(EB[1]), P(EB[1]), AF.Exp, None, col("BE", 1))
+        tt(blk("YL", t), S("ST", 15, 4096, 16), P(EB[1]), O.mult)
+        dma("S", T["yl"][:, 256 * t:256 * t + 256], blk("YL", t))
 
     for t in range(R):
-        b = t % 2; lo = 256 * b; own = blk("IL", b); pr = 4096 * b; W16 = blk("W16", b); v0 = 48 * b
+        b = t % 2; lo = 256 * b; own = il(lo, 256); pr = 4096 * (t % 4); rg = 4096 * b; v0 = 48 * b
 
-        def tn(j): return S("TN", 256 * b + 16 * j, 256 * b + 16 * j + 16)
-        def ut(j): return S("uT", 96 * b + 16 * j, 96 * b + 16 * j + 16)
+        def tn(j): return S("TN", 64 * b + 16 * j, 64 * b + 16 * j + 16)
+        def ut(j): return S("uT", 128 * b + 16 * j, 128 * b + 16 * j + 16)
 
-        def winners(k, bank, y1, add, u):
-            scan(blk("SD", k), S("RS"), P(bank), 0.0, O.min, O.max)
-            tt(tn(8 + k), y1, S("SD", 256 * k + 15, 256 * k + 256, 16), O.max); tt(tn(10 + k), tn(8 + k), S("DU", 16 * k, 16 * k + 16), O.min); ts(u, tn(10 + k), add, O.add)
-
-        for j, z in zip(CH[:-1], CH[1:]):
-            for c0, c1 in zip(KCUT[:-1], KCUT[1:]):
-                if j <= c0 < z:
-                    tt(S("PR", pr + 16 * c0, pr + 16 * c1), I(S("KW", 0, E), S("cB", lo + c0, lo + c1)), S("KG", 16 * c0, 16 * c1), O.mult)
-            mms(P(5, j, z), [(Y("1", k), S("PR", pr + 16 * j + k, pr + 16 * z, 16)) for k in range(16)])
-        cp(W16, P(5))
-        mms(P(6, 256, 512), [(mb("RB"), blk("AUX", b)), (mf("BK"), W16)]); mm(P(7), mf("TRI"), W16, True, True)
-        tt(S("T1"), P(6, 256, 512), blk("U", t), O.mult); tt(S("HIT"), P(7), S("T1"), O.is_gt)
-        mm(P(6), mb("DF"), S("HIT"), True, True)
-        nf = 3 if t < R - 1 else 2
-        for f in range(nf):
-            tt(blk("SEL", f), P(6), FX(b, f), O.mult)
-        mm(P(3), mf("BK"), blk("SEL", 0), True, True)
-        mms(P(4, 0, 16), [(S("Y16", 15 - a, 143 - a), S("SEL", a, 256, 16)) for a in range(16)])
-        mms(P(7, 0, 16 * nf - 16), [(S("Y16", 15 - a, 143 - a), S("SEL", 256 + a, 256 * nf, 16)) for a in range(16)])
-        cp(blk("REP", 0), P(3)); cp(S("VL", v0, v0 + 16), P(4, 0, 16)); act(S("VL", v0 + 16, v0 + 16 * nf), P(7, 0, 16 * nf - 16))
-        key, dl, bn = S("VL", v0, v0 + 16), S("VL", v0 + 16, v0 + 32), S("VL", v0 + 32, v0 + 48)
-        dedupe(key, 0, 5)
-        tt(tn(0), key, dl, O.add); ts(ut(0), tn(0), float(CD), O.add)
-        if GVA:
-            act(S("TMQ"), I(S("AW"), ut(0))); mms(P(7), [(mb("N1"), blk("OH", b)), (mb("I"), S("TMQ"))]); act(S("GV"), P(7), AF.Relu)
-        else:
-            tt(S("GV"), I(S("AW"), ut(0)), blk("OH", b), O.max)
-        winners(0, 5, tn(0), float(CD), ut(1))
-        cp(I(S("AW"), ut(1)), S("GV")) if GVA else tt(I(S("AW"), ut(1)), S("GV"), blk("NOH", b), O.add)
-        for k in range(len(CALL1)):
-            send1(k)
-        recv1()
-        for j in range(3):
-            mms(P(5 + j), [(mb("N%d" % (3 - j)), blk("XR", j)), (mb("ROT"), xp(j))]
-                + [(mb("I"), S("LND", LO[i] + 256 * j, LO[i] + 256 * j + 256)) for i in (2, 1, 0) if i >= j])
-            act(blk("XR", j), P(5 + j), AF.Relu) if XV[j] == "A" else ts(blk("XR", j), P(5 + j), 0.0, O.max)
-        if t < R - 1:
-            for k in range(len(CALL2)):
-                send2(k)
-        for j in range(3):
-            mm(P(5 + j, 256, 512), mb("RINV"), blk("XR", j), True, True)
-            act(xp(j), P(5 + j, 256, 512))
-        if t < R - 1:
-            recv2(); agather(1 - b)
-            mm(P(3), mf("BK"), blk("SEL", 2), True, True); cp(blk("REP", 1), P(3)); dedupe(bn, 1, 4)
-            ts(ut(2), bn, -1.0, O.add)
-            tt(S("GK"), I(S("KW"), ut(2)), blk("C7", b), O.min)
-            winners(1, 4, bn, -1.0, ut(3))
-            tt(I(S("KW"), ut(3)), S("GK"), blk("OH", b), O.add)
-        for a in range(0, 4096, LAM):
-            scan(S("ST", a, a + LAM), S("RG", pr + a, pr + a + LAM), S("PR", pr + a, pr + a + LAM), 0.0, O.mult, O.add)
-        tt(blk("YL", t), S("ST", 15, 4096, 16), blk("E15", b), O.mult)
-        dma("S", T["yl"][:, 256 * t:256 * t + 256], blk("YL", t))
-        if t < R - 2:
-            ts(tn(1), key, 0.0, O.is_equal, 8192.0, O.mult); ts(tn(4), key, 0.0, O.is_lt); tt(tn(5), key, tn(4), O.add); ts(tn(6), key, 2064.0, O.add)
-            tt(tn(5), tn(5), tn(1), O.add); tt(tn(6), tn(6), tn(4), O.mult); tt(tn(5), tn(5), S("DU", 32 + 16 * b, 48 + 16 * b), O.min)
-            ts(ut(5), tn(6), float(INV), O.add); ts(ut(4), tn(5), 2047.0, O.add)
-            act(S("TMP"), I(S("IL"), ut(4))); act(S("IL", LB + lo, LB + lo + 256), S("TMP")); act(S("UP"), I(S("IL"), ut(5)))
+        tag[0] = "exp%d" % t
+        for k in range(8):
             for h in range(2):
-                mm(P(0, 128 * h, 128 * h + 128), S("W16", lo + 128 * h, lo + 128 * h + 128), mf("I"), True, True)
-            scan(blk("SD", 2), S("RM"), P(0), 0.0, O.add, O.min)
+                mm(P(EB[k % 2], h, 512, 2), *((S("DK", 128 * (k + 8 * h), 128 * (k + 8 * h + 1)), blk("LG", t)) if k + h else (mb("RZ"), il(0, 256))), True, True)
+            act(S("RG", rg + k, rg + 4096, 8), P(EB[k % 2], 0, 512), AF.Exp, None, col("BE", 0))
+        if t: last_factor(t - 1)
+        tag[0] = "chain%d" % t
+        for j, z in zip(CH[:-1], CH[1:]):
+            for md, c0, c1 in zip(MODE[t], KCUT[:-1], KCUT[1:]):
+                if j <= c0 < z:
+                    ia = I(S("AW", 0, FB[2] + 768), S("cA", lo + c0, lo + c1)) if t else I(S("A0"), S("cI", c0, c1))
+                    ik = I(S("KW", 0, E), S("cB", lo + c0, lo + c1))
+                    o, ag, kg = S("PR", pr + 16 * c0, pr + 16 * c1), S("AG", 16 * c0, 16 * c1), S("KG", 16 * c0, 16 * c1)
+                    if md == "a":
+                        act(ag, ia); tt(o, ik, ag, O.mult)
+                    elif md == "b":
+                        act(kg, ik); tt(o, ia, kg, O.mult)
+                    elif PROD == "tt":
+                        act(kg, ik); act(ag, ia); tt(o, ag, kg, O.mult)
+                    else:
+                        act(kg, ik, scale=-1.0); act(ag, ia, scale=-1.0); scan(o, ag, kg, 0.0, O.min, O.mult)
+            if z > TOT:
+                mms(P(0, j, z), [(mb("RB"), S("AUX", lo + j, lo + z))] + [(S("BK"), S("PR", pr + 16 * j + k, pr + 16 * z, 16)) for k in range(16)])
+            mms(P(1, j, z), [(S("TK", 128 * k, 128 * k + 128), S("PR", pr + 16 * j + k, pr + 16 * z, 16)) for k in range(16)])
+            if z == TOT:
+                act(S("CUM", 0, z), P(1, 0, z)); mms(P(0, 0, z), [(mb("RB"), S("AUX", lo, lo + z)), (S("L32"), S("CUM", 0, z))])
+        tt(S("T1"), P(0), blk("U", t), O.mult); tt(S("HIT"), P(1), S("T1"), O.is_gt)
+        if t < R - 2: act(S("CUM", TOT, 256), P(1, TOT, 256))
+        mm(P(2), mb("DF"), S("HIT"), True, True)
+        nf = (3, 3, 3, 2, 1)[t]
+        tt(blk("SEL", 0), P(2), FX(b, 0), O.mult)
+        key, bn, cn = S("VL", v0, v0 + 16), S("VL", v0 + 16, v0 + 32), S("VL", v0 + 32, v0 + 48)
+        mm(P(2, 256, 512), mf("BK"), blk("SEL", 0), True, True); cp(blk("REP", 0), P(2, 256, 512))
+        for f in range(1, nf):
+            tt(blk("SEL", f), P(2), FX(b, f), O.mult)
+        mms(P(3, 0, 16), [(S("Y16", 15 - a, 143 - a), S("SEL", a, 256, 16)) for a in range(16)])
+        if not PSK: cp(key, P(3, 0, 16))
+        ts(ut(0), P(3, 0, 16) if PSK else key, float(CD), O.add)
+        raised("GV", S("AW"), ut(0), b, 15.0, P(2, 256, 512))
+        first_wins(0, P(3, 0, 16) if PSK else key, 0, ut(1), float(CD))
+        if PSK and t < R - 2: cp(key, P(3, 0, 16))
+        cp(I(S("AW"), ut(1)), blk("GV", 2))
+        if t < R - 1:
+            tag[0] = "k%d" % t
+            mm(P(KB, 256, 512), mf("BK"), blk("SEL", 1), True, True)
+            mms(P(KB, 0, 16 * nf - 16), [(S("Y16", 15 - a, 143 - a), S("SEL", 256 + a, 256 * nf, 16)) for a in range(16)])
+            cp(blk("REP", 1), P(KB, 256, 512))
+            (cp if KVL == "V" else act)(S("VL", v0 + 16, v0 + 16 * nf), P(KB, 0, 16 * nf - 16))
+            ts(ut(2), bn, -1.0, O.add)
+            if GKA:
+                raised("GK", S("KW"), ut(2), b, 7.0, P(2, 256, 512))
+            else:
+                tt(blk("GK", 0), I(S("KW"), ut(2)), blk("C7", b), O.min)
+        tag[0] = "chain%d" % t
+        for i in (2, 1, 0):
+            send(fr[i], S("LND", LO[i], LO[i] + 256 * (i + 1)), fw(i), "a%d" % i, "la%d" % i, (0.15, 0.15, 0.0)[i])
+        for i in range(3):
+            recv(to[i], S("LND", LO[i], LO[i] + 256 * (i + 1)), "a%d" % i)
+        for j in (2, 1, 0):
+            lnd = [S("LND", LO[i] + 256 * j, LO[i] + 256 * j + 256) for i in (2, 1, 0) if i >= j]
+            if t < R - 1:
+                mms(P(j), [(mb("N%d" % (3 - j)), blk("XR", j))] * (t > 0) + [(mb("ROT"), xp(j))] + [(mb("I"), x) for x in lnd], False)
+                capped(blk("XR", j), P(j), j, XV[j])
+            else:
+                mms(P(j), [(mb("NRI"), blk("XR", j))] * (3 - j) + [(mb("I"), xp(j))] + [(mb("RINV"), x) for x in lnd], False)
+                capped(xp(j), P(j), j, XV[j])
+        if t < R - 1:
+            for j in (2, 1, 0):
+                send(to[j], fw(j), S("XR", 0, 256 * j + 256), "x%d" % j, "lx%d" % j, (0.15, 0.15, 0.0)[j])
+            for j in (2, 1, 0):
+                mm(P(j, 256, 512), mb("RINV"), blk("XR", j), True, True)
+                act(xp(j), P(j, 256, 512)) if XPW[j] == "A" else cp(xp(j), P(j, 256, 512))
+            for i in range(3):
+                recv(fr[i], fw(i), "x%d" % i)
+            tag[0] = "k%d" % t
+            first_wins(1, bn, 3, ut(3), -1.0)
+            cp(I(S("KW"), ut(3)), blk("GK", 2)) if GKA else tt(I(S("KW"), ut(3)), blk("GK", 0), blk("OH", b), O.add)
+        tag[0] = "lam%d" % t
+        for a in range(0, 4096, LAM):
+            scan(S("ST", a, a + LAM), S("RG", rg + a, rg + a + LAM), S("PR", pr + a, pr + a + LAM), 0.0, O.mult, O.add)
+        if t == R - 1: last_factor(t)
+        if t < R - 2:
+            tag[0] = "cand%d" % t
+            ts(tn(0), key, 0.0, O.is_equal, 8192.0, O.mult); tt(tn(1), cn, tn(0), O.add); tt(tn(2), tn(1), S("DU", 16 * b, 16 * b + 16), O.min)
+            ts(ut(4), tn(2), 1408.0, O.add); ts(ut(5), tn(1), 640.0, O.min, float(LB - I0 + 1408), O.add)
+            act(S("TMP"), I(il(0, ILN - I0), ut(4))); act(S("IL", LB + lo, LB + lo + 256), S("TMP")); act(S("UC"), I(il(0, ILN - I0), ut(5)))
+            mms(P(4, 0, 16), [(Y("01", a), S("UC", a, 256, 16)) for a in range(16)]); ts(ut(6), P(4, 0, 16), float(I0), O.add)
+            act(S("UP"), I(S("IL", 0, LB), ut(6)))
+            for h in range(2):
+                mm(P(5, 128 * h, 128 * h + 128), S("CUM", 128 * h, 128 * h + 128), S("D32"), True, True)
+            scan(blk("SD", 2), S("RM"), P(5), 0.0, O.add, O.min)
             ts(S("TI"), S("SD", 527, 768, 16), 16.0, O.mult, 15.0, O.add); ts(S("TI"), S("TI"), 15, O.bitwise_and); cp(S("MB"), S("TI"))
             for h in range(2):
-                mm(P(0, 128 * h, 128 * h + 128, 1, p8), S("MB", 8 * h, 8 * h + 8), mb("I"), True, True)
-            act(S("M8", 0, 256, 1, p8), P(0, 0, 256, 1, p8))
-            mms(P(1), [(mb("R45"), S("UP")), (mb("NR45"), own)]); floor32(P(1), 2)
-            mms(P(0), [(GT, S("M8", 0, 256, 1, p8)), (mb("RIV"), S("UP"))])
-            act(blk("MK", 1), P(0), AF.Abs, kcol, -1.0); act(blk("MK", 0), blk("MK", 1), AF.Relu, 1.0, -1.0)
-            new = ([(mb("R01"), S("UP")), (mb("I"), ct(1))], [(mb("RDL"), S("UP")), (mb("I"), ct(2))],
-                   [(mb("R6"), S("UP")), (mb("R68"), own), (mb("I64"), blk("HI", 2)), (mb("I"), ct(3)), (mb("I"), ct(0))], [(S("I32"), blk("AB", 2))])
-            for f in range(4):
-                z = (f + 1) % 3
-                mms(P(z), new[f] + [(mf("NI"), FX(b, f))]); mm(P(z, 256, 512), mf("I"), FX(b, f), True, True)
-                tt(blk("TT", f % 2), P(z), blk("MK", 0), O.mult); tt(FX(b, f), P(z, 256, 512), blk("TT", f % 2), O.add)
-            lists(b, (0, 1, 2))
-    mms(P(0, 0, 128), [(Y("PH", a), S("PH", a, E, 16)) for a in range(16)]); cp(S("uY"), P(0, 0, 128))
+                mm(P(5, 128 * h, 128 * h + 128, 1, p8), S("MB", 8 * h, 8 * h + 8), mb("I"), True, True)
+            act(S("M8", 0, 256, 1, p8), P(5, 0, 256, 1, p8))
+            mms(P(4), [(mb("R45"), S("UP")), (mb("NR45"), own)]); floor32(P(4), 2)
+            mms(P(5), [(GT, S("M8", 0, 256, 1, p8)), (mb("RIV"), S("UP"))])
+            act(blk("MK", 1), P(5), AF.Abs, kcol, -1.0); act(blk("MK", 0), blk("MK", 1), AF.Relu, 1.0, -1.0)
+            new = ([(mb("R23"), S("UP"))], [(mb("R6"), S("UP")), (mb("RKB"), own), (mb("I64"), blk("HI", 2))], [(mb("R01"), S("UP"))], [(S("I32"), blk("AB", 2))])
+            for f in (1, 0, 3, 2)[:4 if t == 0 else 3]:
+                z = (5, 4)[f % 2]
+                old, out = (blk("LG", t), blk("LG", t + 2)) if f == 3 else (FX(b, f), FX(b, f))
+                mms(P(z, 256, 512), [(mf("I"), old), (mb("NB"), blk("MK", 0))])
+                act(blk("TT", f), P(z, 256, 512)) if FXA else cp(blk("TT", f), P(z, 256, 512))
+                mms(P(z), new[f] + [(mb("NB"), blk("MK", 1))])
+                tt(out, P(z), blk("TT", f), O.max)
+            ts(blk("cB", b), FX(b, 1), -1.0, O.add); ts(blk("cA", b), FX(b, 0), float(CD), O.add)
+    tag[0] = "end"
+    mms(P(3, 0, 128), [(Y("23", a), S("PH", a, E, 16)) for a in range(16)]); ts(S("uY"), P(3, 0, 128), float(CD), O.add)
     for j in range(4):
-        o, w = S("YA", 512 * j, 512 * j + 512), I(S("AW", 0, FB[0]), S("uY", 32 * j, 32 * j + 32))
-        ts(o, w, -1.0, O.mult, 15.0, O.add) if j % 2 == 0 else act(o, w, AF.Identity, 15.0, -1.0)
+        o, w = S("RG", 4096 + 512 * j, 4608 + 512 * j), I(S("AW", 0, FB[0]), S("uY", 32 * j, 32 * j + 32))
+        cp(o, w) if j % 2 == 0 else act(o, w)
         dma("SA"[j % 2], T["ya"][:, 512 * j:512 * j + 512], o)
-    op("S", None, None, [], 0.0, ("end", 0), False, 0.0, [i for i, o in enumerate(ops) if o["dma"]])
+    op(None, None, None, [], 0.0, ("end", 0), False, 0.0, [i for i, o in enumerate(ops) if o["dma"]])
     ops = [o for o in arrange(ops) if o["f"] is not None or o["q"] is None]
     emit(g, T, ops)

@@ -8,11 +8,11 @@ I0, LB, ILN = 16, 2832, 4896
 LO = (0, 256, 768)
 BIG = 16384.0
 CH = (0, 64, 128, 192, 256)
-KCUT = (0, 16, 32, 64, 96, 128, 160, 192, 224, 256)
-MODE = ("aaaaaaaaa",) + ("bbbbbbbbb",) * 4
+KCUT = (0, 32, 64, 128, 192, 256)
+MODE = ("aaaaa",) + ("bbbbb",) * 4
 LAM = 256
 WHO0, WHO1, XV, GKA, FXA, PROD, PASSES, PSK = "VAVAVAVA", "AAAAAAAA", "VVV", True, True, "scan", 200, True
-CY, PEC, GAT, SCA, FIX, HOP, LDMA, RDMA, ISS, DISS, FIRST = 0.95e-3, 0.485e-3, 1.56, 3.8, 0.05, 0.22, 2.1, 2.6, 0.3, 0.15, 2.0
+CY, PEC, GAT, SCA, FIX, HOP, LDMA, RDMA, ISS, DISS, FIRST = 0.95e-3, 0.485e-3, 1.56, 3.8, 0.05, 0.22, 2.1, 2.3, 0.3, 0.15, 2.0
 
 SCRATCH = {}
 for _n, _w, _d in (
@@ -20,7 +20,7 @@ for _n, _w, _d in (
         ("PR", 4 * 4096, "bfloat16"), ("A0", 2816, "bfloat16"), ("RG", 8192, "float32"), ("ST", 4096, "float32"),
         ("YL", 1280, "float32"), ("XR", 768, "bfloat16"), ("XT", 768, "bfloat16"), ("LND", 1536, "bfloat16"),
         ("XD", 768, "bfloat16"), ("G1", 768, "bfloat16"), ("G2", 768, "bfloat16"), ("IM", 768, "bfloat16"),
-        ("U", 1280, "bfloat16"), ("AUX", 1280, "bfloat16"), ("OH", 512, "bfloat16"), ("C7", 512, "bfloat16"),
+        ("U", 1280, "bfloat16"), ("AUX", 1280, "bfloat16"), ("CL", 512, "bfloat16"), ("OH", 512, "bfloat16"), ("C7", 512, "bfloat16"),
         ("FX0", 768, "float16"), ("FX1", 768, "float16"), ("CUM", 256, "float32"), ("D32", 128, "float32"), ("L32", 128, "float32"), ("KD", 512, "bfloat16"), ("TK", 2048, "bfloat16"), ("T1", 256, "float32"),
         ("HIT", 256, "bfloat16"), ("SEL", 768, "float16"), ("REP", 512, "float16"), ("VL", 96, "float32"), ("SD", 768, "float32"),
         ("TN", 128, "float32"), ("TI", 16, "int32"), ("MB", 16, "bfloat16"), ("M8", 256, "bfloat16"), ("MK", 512, "bfloat16"), ("TT", 1024, "float32"),
@@ -33,7 +33,7 @@ for _n, _w, _d in (
         ("KI", 2, "int32"), ("KC", 32, "float32"), ("KH", 48, "float32"), ("M16", 16, "float32"), ("M2", 8, "float32"), ("I256", 256, "float32"),
         ("B256", 256, "bfloat16"), ("LG", 1280, "float16"), ("DC", 16, "float32"),
         ("CM", 256, "bfloat16"), ("RS", 256, "float32"), ("RM", 256, "float32"), ("DU", 32, "float32"), ("G8", 128, "float32"),
-        ("YB", 5 * 144, "bfloat16"), ("Y16", 144, "float16"), ("MBF", 29 * 128, "bfloat16"), ("MF", 3 * 128, "float16"), ("DK", 16 * 128, "float16")):
+        ("YB", 5 * 144, "bfloat16"), ("Y16", 144, "float16"), ("MBF", 28 * 128, "bfloat16"), ("MF", 3 * 128, "float16"), ("DK", 16 * 128, "float16")):
     SCRATCH[_n] = ("sbuf", [128, _w], _d)
 SCRATCH["EQ"] = ("sbuf", [128, 32, 256], "bfloat16")
 for _n in range(8):
@@ -42,13 +42,16 @@ NDMA = 40
 DBG = []
 ORDER = []
 DBG2 = []
-SEED, SWAPS, HEAT, BYTE, JOGS, WARM = 5, 1500, 0.3, 6e-4, 2000, 0.5
-GUESS = ((1.0, 1.0, 0.24, 0.0), (0.95, 1.2, 0.16, 0.0), (1.35, 0.75, 0.2, 0.0), (1.3, 1.6, 0.25, 0.0))
+SEED, SWAPS, HEAT, BYTE, JOGS, WARM = 9, 9000, 0.25, 6e-4, 1000, 0.5
+GUESS = ((1.0, 1.0, 0.21, 0.0, 1.15, 0.0), (0.92, 1.2, 0.16, -0.4, 1.05, -0.5), (1.35, 0.75, 0.2, 0.4, 1.5, 0.4), (1.3, 1.6, 0.26, 0.0, 1.45, 0.0))
 SEQ = ("PR", "AG", "KG", "EQ")
-XPW = "VVV"
-LEAD = {}
+XPW = "VAA"
+LEAD = {"exp": -200.0, "lam": -200.0, "cand": -100.0}
+MILE, GCP, SAME, GVA, PAIR, UDMA, VF = 1.0, "A", 1.0, True, False, True, 0.03
+FCUT, PHV, XO, TKG = (0, 64, 128, 192, 256), 5, (0, 1, 2), 15
+YCUT = (0, 512, 1024, 1536, 2048)
 KB, EB, KVL, TOT = 1, (6, 7), "V", 192
-SEMAPHORES = ["eV", "eA", "eP", "eG"] + ["d%d" % _n for _n in range(NDMA)] + [_a + str(_n) for _a in ("a", "x", "n", "m", "la", "lx", "ln", "lm") for _n in range(3)]
+SEMAPHORES = ["eV", "eA", "eP", "eG", "rCL", "rU"] + ["d%d" % _n for _n in range(NDMA)] + [_a + str(_n) for _a in ("a", "x", "n", "m", "la", "lx", "ln", "lm") for _n in range(3)]
 
 
 def S(name, c0=0, c1=None, step=1, p=(0, 128, 1)):
@@ -75,7 +78,7 @@ def hazards(ops, pe_chain):
                 same = ops[j]["q"] == o["q"]
                 if same and o["q"] == "P":
                     if pe_chain and ps: dep.add(j)
-                elif (ps and not same) or ((wr or w2) and (m2 & pm) and a < d[3] and d[2] < b and not (s2 == d[4] > 1 and (a - d[2]) % s2 and d[0] == "RG")):
+                elif (ps and not same) or ((wr or w2) and (m2 & pm) and a < d[3] and d[2] < b and not (d[0] == "RG" and (a - d[2]) % min(s2, d[4]))):
                     dep.add(j)
         for d, wr, pm in acc:
             l = recs.setdefault(d[0], [])
@@ -98,17 +101,28 @@ def arrange(ops):
         assert len(ORDER) == n and all(at[j] < at[i] for i in range(n) for j in pre[i])
         return [ops[i] for i in ORDER]
 
-    def graph(fc, fg, hop, far):
-        c = [o["c"] * (1.0 if o["dma"] or o["lat"] else fg if o["ind"] else fc) for o in ops]
-        lt = [o["lat"] + (far if o["lat"] and not o["dma"] else 0.0) for o in ops]
+    anc = []
+    for i in range(n):
+        m = 0
+        for j in pre[i] | set(ops[i]["after"]):
+            m |= anc[j]
+        pre[i] = set(j for j in pre[i] if ops[j]["lat"] or not m >> j & 1)
+        for j in pre[i] | set(ops[i]["after"]):
+            m |= 1 << j
+        anc.append(m)
+
+    def graph(fc, fg, hop, far, fp, near):
+        c = [o["c"] * (1.0 if o["dma"] or o["lat"] else fg if o["ind"] else fp if o["q"] == "P" else fc) for o in ops]
+        lt = [o["lat"] + (near if o["dma"] else far if o["lat"] else 0.0) for o in ops]
         ed = []
         for i in range(n):
             e = {j: c[j] + (lt[j] if qs[i] is None else 0.0) for j in ops[i]["after"]}
             for j in pre[i]:
-                e[j] = c[j] + (0.0 if qs[i] == qs[j] == "P" else lt[j] + hop)
+                e[j] = c[j] + (0.0 if qs[i] == qs[j] == "P" else lt[j] + hop * (SAME if qs[i] == qs[j] and not lt[j] else 1.0))
             ed.append(list(e.items()))
         return c, ed
     guess = [graph(*x) for x in GUESS]
+    far = [i for i in range(n) if ops[i]["lat"] and not ops[i]["dma"]]
     c, edges = guess[0]
     back = [[] for _ in range(n)]
     for i in range(n):
@@ -154,7 +168,7 @@ def arrange(ops):
                     if s[j] + l > t: t = s[j] + l
                 s[i] = t
                 if qs[i] is not None: free[qs[i]] = t + cc[i]
-            tot += max(s) / (x[0] + x[1])
+            tot += (s[n - 1] + MILE * sum(s[i] for i in far) / len(far)) / (x[0] + x[1])
         return tot, seq
     pr = list(c)
     for i in range(n - 1, -1, -1):
@@ -198,14 +212,15 @@ def arrange(ops):
                     if s[j] + l >= t: t = s[j] + l; y = j
                 s[i] = t; by[i] = y
                 if qs[i] is not None: free[qs[i]] = (t + cc[i], i)
-            tot += s[n - 1] / (x[0] + x[1]); why.append(by)
+            tot += (s[n - 1] + MILE * sum(s[i] for i in far) / len(far)) / (x[0] + x[1]); why.append(by)
         return tot, why, seq
     cur = top = replay(best[1])
     for k in range(SWAPS):
-        by = cur[1][k % len(GUESS)]; v = n - 1; pairs = []
+        by = cur[1][k % len(GUESS)]; v = far[int(rng.integers(len(far)))] if k // len(GUESS) % 2 else n - 1; pairs = []
         while by[v] >= 0:
             if by[v] not in ps[v]: pairs.append((by[v], v))
             v = by[v]
+        if not pairs: continue
         u, v = pairs[int(rng.integers(len(pairs)))]
         seq = cur[2]; a, z = seq.index(u), seq.index(v); need, held, head, rest = set(ps[v]), set(), [], []
         for x in seq[z - 1:a:-1]:
@@ -214,7 +229,10 @@ def arrange(ops):
             else:
                 rest.append(x)
         if u in need or qs[u] in held: continue
-        new = replay(seq[:a] + head[::-1] + [v, u] + rest[::-1] + seq[z + 1:])
+        tail = rest[::-1] + seq[z + 1:]; r = (0, 0, 1, 2, 4, 8)[int(rng.integers(6))]; m = 0
+        while r and u not in ps[tail[m]]:
+            r -= qs[tail[m]] == qs[u]; m += 1
+        new = replay(seq[:a] + head[::-1] + [v] + tail[:m] + [u] + tail[m:])
         if new[0] < cur[0] + HEAT * (1 - k / SWAPS) * rng.random():
             cur = new
             if cur[0] < top[0]: top = cur
@@ -308,7 +326,7 @@ def rank_program(g, core, T, topo):
         if ins[0][0] == "ind": return FIX + w * GAT * CY
         if q == "A": return FIX + max(64, w) * CY
         if mul == 1.0 and all(SCRATCH[d[0]][2] in ("bfloat16", "float16", "uint16") for d in [out] + ins): mul = 0.5
-        return max(64, w * mul) * CY
+        return VF + max(64, w * mul) * CY
 
     def op(q, f, out, ins, c, tok=None, dma=False, lat=0.0, after=()):
         r, w = [], []
@@ -372,12 +390,17 @@ def rank_program(g, core, T, topo):
     def diag(out, a, v, shift):
         op("G", lambda q: q.affine_select(ap(out), ap(a), [[1, 128]], O.not_equal, v, -shift, -1), out, [a], 0.17 + 256 * CY)
 
+    def gcopy(out, a):
+        if GCP == "A": return act(out, a)
+        op("G", lambda q: q.affine_select(ap(out), ap(a), [[0, width(a)]], O.is_ge, 0.0, 0, 0), out, [a], 0.17 + 2 * width(a) * CY)
+
     def rowsel(out, a, v, r):
         op("G", lambda q: q.affine_select(ap(out), ap(a), [[-16, 8], [0, 16]], O.not_equal, v, -r, 1), out, [a], 0.17 + 256 * CY)
 
-    def dma(q, out, a, more=0.0, wait=()):
-        nd[0] += 1
-        op(q, lambda e: e.dma_start(ap(out), ap(a)), out, [a] + list(wait), DISS, ("d%d" % (nd[0] - 1), 16), True, LDMA + more)
+    def dma(q, out, a, more=0.0, wait=(), part=None):
+        if not part: nd[0] += 1
+        tok = ("d%d" % (nd[0] - 1), 16) if part is None else ("r" + out[0], 16 * part + 16)
+        op(q, lambda e: e.dma_start(ap(out), ap(a)), out, [a] + list(wait), DISS, tok, True, LDMA + more, [len(ops) - 2] if part else ())
 
     def send(peer, dst, src, rs, ls, more=0.0):
         c = T.cores[peer]; rid, pid, _ = topo.addr(c)
@@ -386,14 +409,35 @@ def rank_program(g, core, T, topo):
            ISS + (0 if sends else FIRST), (ls, rc[ls]), False, RDMA + width(src) * BYTE + more, sends[-1:])
         sends.append(len(ops) - 1); sent[rs] = len(ops) - 1
 
+    def halves(src, dst):
+        el = topo.engines(src, dst)
+        return el[1::2], el[0::2]
+
+    def pair(trs, ls, more):
+        l = []
+        for h, (peer, dst, src, rs) in enumerate(trs):
+            c = T.cores[peer]; rid, pid, _ = topo.addr(c); el = halves(core, c)[h]
+            l.append((DstId(rid=rid, pnc=pid), sum(1 << e for e in el), rs, src, dst)); rc[ls] = rc.get(ls, 0) + len(el); sent[rs] = len(ops)
+        op("G", lambda q: q.remote_dma_fused([RemoteDMATransfer(dst_ids=[x[0]], dma_engine_mask=x[1], remote_sem=T.sem[x[2]], src=ap(x[3]), dst=ap(x[4])) for x in l],
+                                             local_sem=T.sem[ls]), None, [x[3] for x in l], ISS, (ls, rc[ls]), False, RDMA + 2 * width(l[0][3]) * BYTE + more, sends[-1:])
+        sends.append(len(ops) - 1)
+
+    def swap(peers, dst, src, s):
+        if PAIR:
+            pair([(peers[2], sub(dst[2], (0, 512)), sub(src[2], (0, 512)), s + "2"), (peers[1], dst[1], src[1], s + "1")], "l" + s + "1", 0.0)
+            pair([(peers[2], sub(dst[2], (512, 768)), sub(src[2], (512, 768)), s + "2"), (peers[0], dst[0], src[0], s + "0")], "l" + s + "0", 0.3)
+        else:
+            for i in (2, 1, 0) if s == "a" else XO:
+                send(peers[i], dst[i], src[i], s + str(i), "l" + s + str(i), (0.15, 0.15, 0.0)[i] if s == "a" or XO[0] else 0.0)
+
     def recv(peer, dst, rs):
-        rc[rs] = rc.get(rs, 0) + len(topo.engines(T.cores[peer], core))
+        rc[rs] = rc.get(rs, 0) + len(topo.engines(T.cores[peer], core)) // (2 if PAIR and rs in ("a0", "a1", "x0", "x1") else 1)
         op(None, None, dst, [], 0.0, (rs, rc[rs]), False, 0.0, [sent[rs]])
 
     def P(b, c0=0, c1=256, step=1, p=(0, 128, 1)): return S("P%d" % b, c0, c1, step, p)
     def col(name, j): return S(name, j, j + 1)
-    names = ["I", "ROT", "ROTM", "ROT23", "RINV", "NRI", "N3", "N2", "N1", "I64", "NB", "D01", "R01", "R23", "R45", "NR45", "R6", "RKB", "RIV", "RB", "RC", "RU",
-             "WD", "WF", "DF", "GT", "WE", "RZ", "I16"]
+    names = ["I", "ROT", "ROTM", "ROT23", "RINV", "NRI", "N3", "N2", "N1", "I64", "NB", "D01", "R01", "R23", "R45", "NR45", "R6", "RKB", "RIV", "RB",
+             "WD", "WF", "DF", "GT", "WE", "I16", "RC", "RU"]
     def mb(x): return S("MBF", 128 * names.index(x), 128 * names.index(x) + 128)
     n16 = ["I", "BK", "B15"]
     def mf(x): return S("MF", 128 * n16.index(x), 128 * n16.index(x) + 128)
@@ -407,6 +451,7 @@ def rank_program(g, core, T, topo):
     def fw(i): return S("AW", FB[i], FB[i] + 256 * (i + 1))
     def il(c0, w): return S("IL", I0 + c0, I0 + c0 + w)
     def kc(j): return col("KC", j)
+    def tk(k): return S("TK", 128 * k, 128 * k + 128) if k else S("BK")
     def m16(j): return col("M16", j)
     def m2(j): return col("M2", j)
     kcol = kc(0); io = S("IO", 0, 128); p8 = (0, 8, 1); Y1 = S("YB", 0, 144)
@@ -414,9 +459,12 @@ def rank_program(g, core, T, topo):
 
     dma("S", S("SN"), T["snd"][:], -0.5); dma("A", S("DI", 0, 128), T["ti"][:], -0.4); dma("S", S("DI", 288, 416), T["kd"][:], -0.3); dma("S", S("A0", 0, E), T["a0"][:], 1.3)
     ops[2]["after"], ops[3]["after"] = [0], [2]
-    dma("S", S("KW", 0, E), T["k0"][:], 2.0, [S("SN")]); dma("S", S("CA"), T["ca"][:], 0.5, [S("A0", 0, E)]); dma("S", S("BE", 0, 1), T["be"][:], 0.0, [S("CA")])
+    dma("S", S("CA"), T["ca"][:], 2.0); dma("S", S("BE", 0, 1), T["be"][:], 2.0)
     for c0, c1, x in ((128, 160, "bg"), (416, 448, "cl"), (448, 528, "us"), (160, 288, "lp")):
-        dma("S", S("DI", c0, c1), T[x][:], 0.0, [S("CA")])
+        dma("S", S("DI", c0, c1), T[x][:], 2.0)
+    dma("S", S("KW", 0, E), T["k0"][:], 2.0, [S("SN")])
+    for k in range(4, 11):
+        ops[k]["after"] = [k - 1]
     iota(col("KI", 0), [[1, 1]], 0, 1); iota(S("I256"), [[1, 256]], 0, 0); iota(S("IO"), [[1, 144]], 0, -1)
     ms(S("Z"), 0.0)
     diag(mb("ROT"), S("Z"), 1.0, 16); diag(mb("ROT"), mb("ROT"), 1.0, -112)
@@ -434,8 +482,9 @@ def rank_program(g, core, T, topo):
     for j in range(4):
         ts(S("PH", 128 * j, 128 * j + 128), S("B256", 0, 256, 2), col("KH", 16 + j), O.add)
     for j in range(2, 8):
-        ts(blk("PH", j), S("B256"), col("KH", 18 + j), O.add)
-    ms(S("IL", 0, I0 + E), 1.0)
+        ts(blk("PH", j), S("B256"), col("KH", 18 + j), O.add) if j < PHV else act(blk("PH", j), S("B256"), AF.Identity, col("KH", 18 + j))
+    for j in range(6):
+        ms(S("IL", 344 * j, 344 * j + 344), 1.0)
     ts(S("DB", 816, 944), S("Z"), kcol, O.add, 128.0, O.mult); cp(S("DB", 944, 1072), S("I256", 0, 128))
     tt(kc(2), m2(0), m2(1), O.add); ts(kc(4), kc(2), -1.0, O.mult, 1.0, O.add)
     for i in range(3):
@@ -450,16 +499,18 @@ def rank_program(g, core, T, topo):
     ts(kc(10), m16(8), -1408.0, O.mult, m2(0), O.add); ts(kc(13), m2(2), -1.0, O.mult)
     for x, c in (("RKB", kc(9)), ("NR45", kc(13)), ("R01", kc(10))):
         act(mb(x), S("BK"), scale=c)
-    for x, v, rows in (("R23", 1.0, (2, 3)), ("R45", 1.0, (4, 5)), ("R6", 1.0, (6,)), ("RB", 1.0, (10, 11)), ("RC", 1.0, (12,)),
-                       ("RU", 1.0, (13,)), ("WE", -BIG, (15,)), ("RZ", -2.0 ** 17, (8,))):
+    for x, v, rows in (("R23", 1.0, (2, 3)), ("R45", 1.0, (4, 5)), ("R6", 1.0, (6,)), ("RB", 1.0, (10, 11)), ("WE", -BIG, (15,))):
         for j, r in enumerate(rows):
             rowsel(mb(x), mb(x) if j else S("Z"), v, r)
     rowsel(mb("RIV"), S("Z"), -100.0, 7); rowsel(mb("RIV"), mb("RIV"), 100.0, 8)
     act(mb("WF"), S("BK"), scale=BIG); act(S("I32"), mb("I"))
     cp(S("Y16"), Y1); cp(mf("I"), mb("I")); cp(mf("BK"), S("BK")); ts(mf("B15"), S("BK"), m16(15), O.mult)
     iota(b2(5), [[0, 8], [1, 16]], 1, 0); tt(b2(2), b2(5), S("BK"), O.mult)
-    for k in range(16):
-        ts(S("TK", 128 * k, 128 * k + 128), b2(2), k + 0.5, O.is_gt)
+    for k in range(1, 16):
+        if k <= TKG:
+            op("G", lambda q, k=k: q.affine_select(ap(tk(k)), ap(S("BK")), [[0, 8], [1, 16]], O.is_ge, 0.0, -k, 0), tk(k), [S("BK")], 0.17 + 256 * CY)
+        else:
+            ts(tk(k), b2(2), k + 0.5, O.is_gt)
     ts(b2(3), io, 1.0, O.is_ge, BIG, O.mult); tt(mb("WD"), b2(3), S("BK"), O.mult)
     ts(kc(12), m16(15), -1.0, O.mult, 1.0, O.add); act(b2(1), b2(0), scale=kc(12)); diag(mb("DF"), b2(1), 1.0, 0)
     act(S("D32"), mb("DF")); act(S("L32"), S("BK"), scale=m16(15))
@@ -470,20 +521,20 @@ def rank_program(g, core, T, topo):
     GT = mb("GT")[:1] + (p8,) + mb("GT")[2:]
     ts(GT, S("G8", 0, 128, 1, p8), 0.0, O.is_equal)
     tt(kc(14), m16(8), m16(0), O.subtract); cp(col("IL", I0 - 1), kc(14))
-    fill(S("IL", LB, ILN), 0); cp(col("IL", LB + E), kc(14))
-    fill(S("AW", 0, 1024), 0); fill(S("AW", 2560, XB), 0); fill(S("AW", FB[0], AWN), 0); fill(S("KW", E, E + 256), 0)
+    ms(S("IL", LB + E, ILN), 0.0); cp(col("IL", LB + E), kc(14))
+    fill(S("AW", 2560, XB), 0); fill(S("AW", FB[0], FB[2] + 768), 0)
     iota(blk("TT", 0), [[0, 16], [1, 16]], 0, 0); iota(blk("TT", 1), [[1, 256]], E + 1 - int(BIG), 0); iota(S("DU"), [[16, 32]], 1408, 0)
     ts(S("CM"), blk("TT", 0), kcol, O.subtract, 2.0 ** 26, O.mult); act(blk("TT", 2), S("CM"), AF.Abs); tt(S("RS"), blk("TT", 1), blk("TT", 2), O.subtract)
     ms(S("RM"), -0.0625); ms(S("RM", 0, 256, 16), 2.0 ** 20); ts(S("DU"), S("DU"), kcol, O.add)
     act(col("BE", 1), col("BE", 0), scale=-1.0)
+    fill(S("RG", 0, 8192, 16), 0)
     for i in range(3):
         cp(S("uS", 16 * i, 16 * i + 16), S("SN", 16 * (dto[i] - 1), 16 * dto[i]))
     for a, z in ((0, 128), (128, 288)):
         cp(S("DB", a, z), S("DI", a, z)); tt(S("DB", 288 + a, 288 + z), S("DI", a, z), S("DB", a, z), O.subtract)
-    cp(S("DB", 576, 704), S("DI", 288, 416)); cp(S("DB", 704, 816), S("DI", 416, 528))
-    ms(S("AUX"), 0.0)
-    for q, x, r, at, c0, w in (("A", "IL", 0, I0, 816, 128), ("A", "IL", 1, I0, 944, 128), ("S", "IL", 4, I0, 0, 128), ("A", "IL", 5, I0, 288, 128), ("S", "IL", 6, I0, 576, 128), ("S", "AUX", 10, 0, 128, 32), ("S", "AUX", 11, 0, 416, 32),
-                               ("S", "AUX", 12, 0, 704, 32), ("S", "AUX", 13, 0, 736, 80), ("S", "IL", 0, LB, 160, 128), ("S", "IL", 1, LB, 448, 128)):
+    cp(S("DB", 576, 704), S("DI", 288, 416)); cp(S("DB", 704, 736), S("DI", 416, 448)); ts(S("DB", 736, 816), S("DI", 448, 528), 2.0 ** -8, O.mult)
+    fill(S("AUX", 0, 512), 0) if UDMA else ms(S("AUX"), 0.0)
+    for q, x, r, at, c0, w in (("A", "IL", 0, I0, 816, 128), ("A", "IL", 1, I0, 944, 128), ("S", "IL", 4, I0, 0, 128), ("S", "IL", 5, I0, 288, 128), ("S", "IL", 6, I0, 576, 128), ("S", "AUX", 10, 0, 128, 32), ("S", "AUX", 11, 0, 416, 32)):
         dma(q, row(x, r, at, 16 * w), S("DB", c0, c0 + w), 0.3 if w == 128 else 0.0)
     for i in range(3):
         act(blk("G1", i), I(il(0, E), S("uS", 16 * i, 16 * i + 16)))
@@ -494,7 +545,6 @@ def rank_program(g, core, T, topo):
         mm(P(i), mb("ROT"), xp(i), True, True)
         act(blk("XR", i), P(i))
         send(to[i], blk("A0", 7 + dto[i]), blk("XR", i), "m%d" % i, "lm%d" % i)
-    act(S("AW", 0, 1024, 2), S("A0", 0, 512))
     for i in (2, 1, 0):
         cp(I(S("PH"), S("uS", 16 * i, 16 * i + 16)), blk("XD", i))
     for i in range(3):
@@ -508,10 +558,10 @@ def rank_program(g, core, T, topo):
         d = (rank - fr[i]) % n
         recv(fr[i], blk("A0", 7 + d), "m%d" % i); recv(fr[i], il(E + 256 * (d - 1), 256), "n%d" % i)
     dma("S", S("AW", 1024, 2560), T["a0"][:, 512:E], 1.0, [il(E, 768)])
-    for c0, w in ((0, 512), (512, 512), (1024, 256)):
-        mm(P(3, 0, w), mb("RU"), S("AUX", c0, c0 + w), True, True); act(S("U", c0, c0 + w), P(3, 0, w), scale=2.0 ** -8)
-    mm(P(4, 0, 512), mb("RC"), S("AUX", 0, 512), True, True); ts(S("OH"), P(4, 0, 512), kcol, O.is_equal)
-    if not GKA: act(S("C7"), S("OH"), AF.Identity, 7.0, -1.0)
+    dma("S", S("AW", 0, 1024), T["a0"][:, 0:1024], 1.5, [il(E, 768)]); dma("S", S("AW", FB[2] + 768, AWN), T["a0"][:, 0:AWN - FB[2] - 768], 1.5, [il(E, 768)])
+    dma("S", S("KW", E, E + 256), T["k0"][:, 0:256], 1.5, [il(E, 768)]); dma("S", S("IL", LB, LB + E), T["k0"][:], 2.5, [il(E, 768)])
+    act(S("AW", 0, 1024, 2), S("A0", 0, 512))
+    dma("S", row("IL", 0, LB, E), S("DB", 160, 288), 0.3); dma("S", row("IL", 1, LB, E), S("DB", 448, 576), 0.3)
 
     def floor32(ps, j, c=(0, 256)):
         act(sub(blk("AB", j), c), ps, AF.Abs); act(sub(blk("HI", j), c), sub(blk("AB", j), c), AF.Identity, 159.515625, 0.03125)
@@ -531,10 +581,27 @@ def rank_program(g, core, T, topo):
         ts(sub(FX(b, 0), c), P(bk[2], 0, w), 1.5 * 2 ** 23, O.add, 1.5 * 2 ** 23, O.subtract)
         tt(sub(blk("KD", b), c), P(bk[2], 0, w), sub(FX(b, 0), c), O.subtract); mm(P(bk[1], 0, w), mb("I16"), sub(blk("KD", b), c), False, False)
         floor32(P(bk[0], 0, w), b, c); mm(P(bk[1], 0, w), mb("I64"), sub(blk("HI", b), c), False, True)
-        cp(sub(FX(b, 1), c), P(bk[1], 0, w)); cp(sub(blk("LG", b), c), sub(blk("AB", b), c))
-        ts(sub(blk("cB", b), c), sub(FX(b, 1), c), -1.0, O.add)
+        if b == 0: ts(sub(blk("cB", b), c), P(bk[1], 0, w), -1.0, O.add)
+        cp(sub(FX(b, 1), c), P(bk[1], 0, w))
+        if b: ts(sub(blk("cB", b), c), sub(FX(b, 1), c), -1.0, O.add)
+        if c[1] == 256: cp(blk("LG", b), blk("AB", b))
 
-    facts(0, WHO0, (0, 1, 2), (0, 128)); facts(0, WHO0, (5, 6, 7), (128, 256))
+    tag[0] = "first"
+    for j, (a, z) in enumerate(zip(FCUT[:-1], FCUT[1:])):
+        facts(0, WHO0, ((2, 3, 4), (5, 6, 7))[j % 2], (a, z))
+    tag[0] = "draws"
+    if UDMA:
+        for r in range(16):
+            dma("S", row("CL", r, 0, 512), S("DB", 704, 736), 0.0, (), r); dma("S", row("U", r, 0, 1280), S("DB", 736, 816), 0.0, (), r)
+        ts(S("OH"), S("CL"), kcol, O.is_equal)
+    else:
+        dma("S", row("AUX", 12, 0, 512), S("DB", 704, 736)); dma("S", row("AUX", 13, 0, 1280), S("DB", 736, 816))
+        rowsel(mb("RC"), S("Z"), 1.0, 12); rowsel(mb("RU"), S("Z"), 1.0, 13)
+        for c0, w in ((0, 512), (512, 512), (1024, 256)):
+            mm(P(3, 0, w), mb("RU"), S("AUX", c0, c0 + w), True, True); act(S("U", c0, c0 + w), P(3, 0, w))
+        mm(P(4, 0, 512), mb("RC"), S("AUX", 0, 512), True, True); ts(S("OH"), P(4, 0, 512), kcol, O.is_equal)
+    if not GKA: act(S("C7"), S("OH"), AF.Identity, 7.0, -1.0)
+    if not GVA: act(S("XT", 0, 512), S("OH"), AF.Identity, 15.0, -1.0)
     tag[0] = "facts"; facts(1, WHO1, (5, 6, 7), (0, 256))
     ts(blk("cA", 1), FX(1, 0), float(CD), O.add)
 
@@ -548,8 +615,11 @@ def rank_program(g, core, T, topo):
         scan(blk("SD", k), S("RS"), P(bank), -2.0 ** 26, O.max, O.min)
         ts(u, S("SD", 256 * k + 15, 256 * k + 256, 16), add + BIG, O.add)
 
+    def listed(ps, f):
+        mms(ps, [(S("Y16", 15 - a, 143 - a), S("SEL", 256 * f + a, 256 * f + 256, 16)) for a in range(16)])
+
     def raised(name, win, u, b, cap, ps):
-        act(blk(name, 0), I(win, u)); mms(ps, [(mb("I"), blk("OH", b)), (mb("I"), blk(name, 0))])
+        act(blk(name, 0), I(win, u)); mms(ps, [(mb("I"), blk("OH", b)), (mb("I"), blk(name, 0))], False)
         act(blk(name, 1), ps, AF.Relu, cap, -1.0); act(blk(name, 2), blk(name, 1), AF.Identity, cap, -1.0)
 
     def capped(out, ps, j, who):
@@ -570,9 +640,11 @@ def rank_program(g, core, T, topo):
         def ut(j): return S("uT", 128 * b + 16 * j, 128 * b + 16 * j + 16)
 
         tag[0] = "exp%d" % t
-        for k in range(8):
+        mm(P(EB[0]), S("DK", 1024, 1152), blk("LG", t), True, True); act(S("RG", rg + 8, rg + 4096, 16), P(EB[0]), AF.Exp, None, col("BE", 0))
+        for k in range(1, 8):
             for h in range(2):
-                mm(P(EB[k % 2], h, 512, 2), *((S("DK", 128 * (k + 8 * h), 128 * (k + 8 * h + 1)), blk("LG", t)) if k + h else (mb("RZ"), il(0, 256))), True, True)
+                mm(P(EB[k % 2], h, 512, 2), S("DK", 128 * (k + 8 * h), 128 * (k + 8 * h + 1)), blk("LG", t), True, True)
+            unit(2); ops[-1]["w"] = [P(EB[k % 2], 0, 512)]
             act(S("RG", rg + k, rg + 4096, 8), P(EB[k % 2], 0, 512), AF.Exp, None, col("BE", 0))
         if t: last_factor(t - 1)
         tag[0] = "chain%d" % t
@@ -586,45 +658,45 @@ def rank_program(g, core, T, topo):
                         act(ag, ia); tt(o, ik, ag, O.mult)
                     elif md == "b":
                         act(kg, ik); tt(o, ia, kg, O.mult)
+                    elif md == "p":
+                        ps = P((4, 3, 2)[MODE[t][:KCUT.index(c0)].count("p")], 0, 16 * (c1 - c0))
+                        act(kg, ik); mm(ps, mb("I"), kg, True, True); act(ag, ia); tt(o, ps, ag, O.mult)
                     elif PROD == "tt":
                         act(kg, ik); act(ag, ia); tt(o, ag, kg, O.mult)
                     else:
                         act(kg, ik, scale=-1.0); act(ag, ia, scale=-1.0); scan(o, ag, kg, 0.0, O.min, O.mult)
             if z > TOT:
                 mms(P(0, j, z), [(mb("RB"), S("AUX", lo + j, lo + z))] + [(S("BK"), S("PR", pr + 16 * j + k, pr + 16 * z, 16)) for k in range(16)])
-            mms(P(1, j, z), [(S("TK", 128 * k, 128 * k + 128), S("PR", pr + 16 * j + k, pr + 16 * z, 16)) for k in range(16)])
+            mms(P(1, j, z), [(tk(k), S("PR", pr + 16 * j + k, pr + 16 * z, 16)) for k in range(16)])
             if z == TOT:
                 act(S("CUM", 0, z), P(1, 0, z)); mms(P(0, 0, z), [(mb("RB"), S("AUX", lo, lo + z)), (S("L32"), S("CUM", 0, z))])
         tt(S("T1"), P(0), blk("U", t), O.mult); tt(S("HIT"), P(1), S("T1"), O.is_gt)
         if t < R - 2: act(S("CUM", TOT, 256), P(1, TOT, 256))
         mm(P(2), mb("DF"), S("HIT"), True, True)
         nf = (3, 3, 3, 2, 1)[t]
-        tt(blk("SEL", 0), P(2), FX(b, 0), O.mult)
-        key, bn, cn = S("VL", v0, v0 + 16), S("VL", v0 + 16, v0 + 32), S("VL", v0 + 32, v0 + 48)
-        mm(P(2, 256, 512), mf("BK"), blk("SEL", 0), True, True); cp(blk("REP", 0), P(2, 256, 512))
-        for f in range(1, nf):
+        for f in range(nf):
+            tag[0] = ("chain%d", "k%d", "cand%d")[f] % t
             tt(blk("SEL", f), P(2), FX(b, f), O.mult)
-        mms(P(3, 0, 16), [(S("Y16", 15 - a, 143 - a), S("SEL", a, 256, 16)) for a in range(16)])
-        if not PSK: cp(key, P(3, 0, 16))
-        ts(ut(0), P(3, 0, 16) if PSK else key, float(CD), O.add)
-        raised("GV", S("AW"), ut(0), b, 15.0, P(2, 256, 512))
-        first_wins(0, P(3, 0, 16) if PSK else key, 0, ut(1), float(CD))
-        if PSK and t < R - 2: cp(key, P(3, 0, 16))
-        cp(I(S("AW"), ut(1)), blk("GV", 2))
+        tag[0] = "chain%d" % t
+        bn = S("VL", 16 * b, 16 * b + 16)
+        mm(P(4, 256, 512), mf("BK"), blk("SEL", 0), True, True); cp(blk("REP", 0), P(4, 256, 512))
+        listed(P(3, 0, 16), 0); ts(ut(0), P(3, 0, 16), float(CD), O.add)
+        if GVA:
+            raised("GV", S("AW"), ut(0), b, 15.0, P(2, 256, 512))
+        else:
+            tt(blk("GV", 0), I(S("AW"), ut(0)), blk("XT", b), O.min)
+        first_wins(0, P(3, 0, 16), 0, ut(1), float(CD))
+        cp(I(S("AW"), ut(1)), blk("GV", 2)) if GVA else tt(I(S("AW"), ut(1)), blk("GV", 0), blk("OH", b), O.add)
         if t < R - 1:
             tag[0] = "k%d" % t
-            mm(P(KB, 256, 512), mf("BK"), blk("SEL", 1), True, True)
-            mms(P(KB, 0, 16 * nf - 16), [(S("Y16", 15 - a, 143 - a), S("SEL", 256 + a, 256 * nf, 16)) for a in range(16)])
-            cp(blk("REP", 1), P(KB, 256, 512))
-            (cp if KVL == "V" else act)(S("VL", v0 + 16, v0 + 16 * nf), P(KB, 0, 16 * nf - 16))
-            ts(ut(2), bn, -1.0, O.add)
+            mm(P(4, 256, 512), mf("BK"), blk("SEL", 1), True, True); listed(P(4, 0, 16), 1)
+            cp(blk("REP", 1), P(4, 256, 512)); cp(bn, P(4, 0, 16)); ts(ut(2), P(4, 0, 16), -1.0, O.add)
             if GKA:
                 raised("GK", S("KW"), ut(2), b, 7.0, P(2, 256, 512))
             else:
                 tt(blk("GK", 0), I(S("KW"), ut(2)), blk("C7", b), O.min)
         tag[0] = "chain%d" % t
-        for i in (2, 1, 0):
-            send(fr[i], S("LND", LO[i], LO[i] + 256 * (i + 1)), fw(i), "a%d" % i, "la%d" % i, (0.15, 0.15, 0.0)[i])
+        swap(fr, [S("LND", LO[i], LO[i] + 256 * (i + 1)) for i in range(3)], [fw(i) for i in range(3)], "a")
         for i in range(3):
             recv(to[i], S("LND", LO[i], LO[i] + 256 * (i + 1)), "a%d" % i)
         for j in (2, 1, 0):
@@ -636,8 +708,7 @@ def rank_program(g, core, T, topo):
                 mms(P(j), [(mb("NRI"), blk("XR", j))] * (3 - j) + [(mb("I"), xp(j))] + [(mb("RINV"), x) for x in lnd], False)
                 capped(xp(j), P(j), j, XV[j])
         if t < R - 1:
-            for j in (2, 1, 0):
-                send(to[j], fw(j), S("XR", 0, 256 * j + 256), "x%d" % j, "lx%d" % j, (0.15, 0.15, 0.0)[j])
+            swap(to, [fw(j) for j in range(3)], [S("XR", 0, 256 * j + 256) for j in range(3)], "x")
             for j in (2, 1, 0):
                 mm(P(j, 256, 512), mb("RINV"), blk("XR", j), True, True)
                 act(xp(j), P(j, 256, 512)) if XPW[j] == "A" else cp(xp(j), P(j, 256, 512))
@@ -648,15 +719,15 @@ def rank_program(g, core, T, topo):
             cp(I(S("KW"), ut(3)), blk("GK", 2)) if GKA else tt(I(S("KW"), ut(3)), blk("GK", 0), blk("OH", b), O.add)
         tag[0] = "lam%d" % t
         for a in range(0, 4096, LAM):
-            scan(S("ST", a, a + LAM), S("RG", rg + a, rg + a + LAM), S("PR", pr + a, pr + a + LAM), 0.0, O.mult, O.add)
+            z = min(a + LAM, 4096)
+            scan(S("ST", a, z), S("RG", rg + a, rg + z), S("PR", pr + a, pr + z), 0.0, O.mult, O.add)
         if t == R - 1: last_factor(t)
         if t < R - 2:
             tag[0] = "cand%d" % t
-            ts(tn(0), key, 0.0, O.is_equal, 8192.0, O.mult); tt(tn(1), cn, tn(0), O.add); tt(tn(2), tn(1), S("DU", 16 * b, 16 * b + 16), O.min)
+            listed(P(5, 0, 16), 2)
+            ts(tn(0), bn, 0.0, O.is_equal, 8192.0, O.mult); tt(tn(1), P(5, 0, 16), tn(0), O.add); tt(tn(2), tn(1), S("DU", 16 * b, 16 * b + 16), O.min)
             ts(ut(4), tn(2), 1408.0, O.add); ts(ut(5), tn(1), 640.0, O.min, float(LB - I0 + 1408), O.add)
-            act(S("TMP"), I(il(0, ILN - I0), ut(4))); act(S("IL", LB + lo, LB + lo + 256), S("TMP")); act(S("UC"), I(il(0, ILN - I0), ut(5)))
-            mms(P(4, 0, 16), [(Y("01", a), S("UC", a, 256, 16)) for a in range(16)]); ts(ut(6), P(4, 0, 16), float(I0), O.add)
-            act(S("UP"), I(S("IL", 0, LB), ut(6)))
+            act(S("TMP"), I(il(0, ILN - I0), ut(4))); gcopy(S("IL", LB + lo, LB + lo + 256), S("TMP")); act(S("UC"), I(il(0, ILN - I0), ut(5)))
             for h in range(2):
                 mm(P(5, 128 * h, 128 * h + 128), S("CUM", 128 * h, 128 * h + 128), S("D32"), True, True)
             scan(blk("SD", 2), S("RM"), P(5), 0.0, O.add, O.min)
@@ -664,24 +735,28 @@ def rank_program(g, core, T, topo):
             for h in range(2):
                 mm(P(5, 128 * h, 128 * h + 128, 1, p8), S("MB", 8 * h, 8 * h + 8), mb("I"), True, True)
             act(S("M8", 0, 256, 1, p8), P(5, 0, 256, 1, p8))
-            mms(P(4), [(mb("R45"), S("UP")), (mb("NR45"), own)]); floor32(P(4), 2)
-            mms(P(5), [(GT, S("M8", 0, 256, 1, p8)), (mb("RIV"), S("UP"))])
-            act(blk("MK", 1), P(5), AF.Abs, kcol, -1.0); act(blk("MK", 0), blk("MK", 1), AF.Relu, 1.0, -1.0)
+            mms(P(5, 0, 16), [(Y("01", a), S("UC", a, 256, 16)) for a in range(16)]); ts(ut(6), P(5, 0, 16), float(I0), O.add)
+            act(S("UP"), I(S("IL", 0, LB), ut(6)))
+            mms(P(5), [(GT, S("M8", 0, 256, 1, p8)), (mb("RIV"), S("UP"))]); mms(P(5, 256, 512), [(mb("R45"), S("UP")), (mb("NR45"), own)])
+            act(blk("MK", 1), P(5), AF.Abs, kcol, -1.0); floor32(P(5, 256, 512), 2); act(blk("MK", 0), blk("MK", 1), AF.Relu, 1.0, -1.0)
             new = ([(mb("R23"), S("UP"))], [(mb("R6"), S("UP")), (mb("RKB"), own), (mb("I64"), blk("HI", 2))], [(mb("R01"), S("UP"))], [(S("I32"), blk("AB", 2))])
-            for f in (1, 0, 3, 2)[:4 if t == 0 else 3]:
-                z = (5, 4)[f % 2]
-                old, out = (blk("LG", t), blk("LG", t + 2)) if f == 3 else (FX(b, f), FX(b, f))
-                mms(P(z, 256, 512), [(mf("I"), old), (mb("NB"), blk("MK", 0))])
-                act(blk("TT", f), P(z, 256, 512)) if FXA else cp(blk("TT", f), P(z, 256, 512))
-                mms(P(z), new[f] + [(mb("NB"), blk("MK", 1))])
-                tt(out, P(z), blk("TT", f), O.max)
+            old = [FX(b, 0), FX(b, 1), FX(b, 2), blk("LG", t)]; out = old[:3] + [blk("LG", t + 2)]
+            for fs in ((0, 1), (2, 3) if t == 0 else (3,)):
+                w = 256 * len(fs); keep = S("TT", 256 * fs[0], 256 * fs[0] + w)
+                for j, f in enumerate(fs):
+                    mms(P(5, 256 * j, 256 * j + 256), [(mf("I"), old[f]), (mb("NB"), blk("MK", 0))])
+                act(keep, P(5, 0, w)) if FXA else cp(keep, P(5, 0, w))
+                for j, f in enumerate(fs):
+                    mms(P(5, 256 * j, 256 * j + 256), new[f] + [(mb("NB"), blk("MK", 1))])
+                for j, f in enumerate(fs):
+                    tt(out[f], P(5, 256 * j, 256 * j + 256), blk("TT", f), O.max)
             ts(blk("cB", b), FX(b, 1), -1.0, O.add); ts(blk("cA", b), FX(b, 0), float(CD), O.add)
     tag[0] = "end"
     mms(P(3, 0, 128), [(Y("23", a), S("PH", a, E, 16)) for a in range(16)]); ts(S("uY"), P(3, 0, 128), float(CD), O.add)
-    for j in range(4):
-        o, w = S("RG", 4096 + 512 * j, 4608 + 512 * j), I(S("AW", 0, FB[0]), S("uY", 32 * j, 32 * j + 32))
+    for j, (a, z) in enumerate(zip(YCUT[:-1], YCUT[1:])):
+        o, w = S("RG", 4096 + a, 4096 + z), I(S("AW", 0, FB[0]), S("uY", a // 16, z // 16))
         cp(o, w) if j % 2 == 0 else act(o, w)
-        dma("SA"[j % 2], T["ya"][:, 512 * j:512 * j + 512], o)
+        dma("S", T["ya"][:, a:z], o, (z - a) * 1e-3)
     op(None, None, None, [], 0.0, ("end", 0), False, 0.0, [i for i, o in enumerate(ops) if o["dma"]])
     ops = [o for o in arrange(ops) if o["f"] is not None or o["q"] is None]
     emit(g, T, ops)

import numpy
from concourse.bass import DstId, RemoteDMATransfer
from concourse.mybir import AluOpType as O, ActivationFunctionType as AF

E, M, R = 2048, 256, 5
CD, XB, FB, AWN = 3072, 3136, (3904, 2560, 4160), 5392
I0, LB, ILN = 16, 2832, 4896
LO = (0, 256, 768)
BIG = 16384.0
CH = (0, 64, 128, 192, 256)
KCUT = (0, 32, 64, 128, 192, 256)
MODE = ("aaaaa",) + ("bbbbb",) * 4
LAM = 256
WHO0, WHO1, XV, GKA, FXA, PROD, PASSES, PSK = "VAVAVAVA", "AAAAAAAA", "VVV", True, True, "scan", 200, True
CY, PEC, GAT, SCA, FIX, HOP, LDMA, RDMA, ISS, DISS, FIRST = 0.95e-3, 0.485e-3, 1.56, 3.8, 0.05, 0.22, 2.1, 2.3, 0.3, 0.15, 2.0

SCRATCH = {}
for _n, _w, _d in (
        ("AW", AWN, "bfloat16"), ("KW", 2304, "bfloat16"), ("IL", ILN, "bfloat16"), ("PH", E, "bfloat16"), ("AG", 4096, "bfloat16"), ("KG", 4096, "bfloat16"),
        ("PR", 4 * 4096, "bfloat16"), ("A0", 2816, "bfloat16"), ("RG", 8192, "float32"), ("ST", 4096, "float32"),
        ("YL", 1280, "float32"), ("XR", 768, "bfloat16"), ("XT", 768, "bfloat16"), ("LND", 1536, "bfloat16"),
        ("XD", 768, "bfloat16"), ("G1", 768, "bfloat16"), ("G2", 768, "bfloat16"), ("IM", 768, "bfloat16"),
        ("U", 1280, "bfloat16"), ("AUX", 1280, "bfloat16"), ("CL", 512, "bfloat16"), ("OH", 512, "bfloat16"), ("C7", 512, "bfloat16"),
        ("FX0", 768, "float16"), ("FX1", 768, "float16"), ("CUM", 256, "float32"), ("D32", 128, "float32"), ("L32", 128, "float32"), ("KD", 512, "bfloat16"), ("TK", 2048, "bfloat16"), ("T1", 256, "float32"),
        ("HIT", 256, "bfloat16"), ("SEL", 768, "float16"), ("REP", 512, "float16"), ("VL", 96, "float32"), ("SD", 768, "float32"),
        ("TN", 128, "float32"), ("TI", 16, "int32"), ("MB", 16, "bfloat16"), ("M8", 256, "bfloat16"), ("MK", 512, "bfloat16"), ("TT", 1024, "float32"),
        ("GV", 768, "bfloat16"), ("GK", 768, "bfloat16"), ("TMP", 256, "bfloat16"), ("UC", 256, "bfloat16"), ("UP", 256, "bfloat16"),
        ("AB", 768, "float32"), ("HI", 768, "bfloat16"),
        ("cI", 512, "uint16"), ("cA", 512, "uint16"), ("cB", 512, "uint16"), ("uS", 48, "uint16"), ("uT", 256, "uint16"),
        ("uY", 128, "uint16"), ("CA", 512, "int32"), ("SN", 48, "int32"), ("BE", 2, "float32"),
        ("DI", 528, "int32"), ("DB", 1072, "bfloat16"), ("Z", 128, "bfloat16"),
        ("IO", 144, "float32"), ("J", 144, "float32"), ("BK", 128, "bfloat16"), ("B2", 768, "bfloat16"), ("I32", 128, "float32"),
        ("KI", 2, "int32"), ("KC", 32, "float32"), ("KH", 48, "float32"), ("M16", 16, "float32"), ("M2", 8, "float32"), ("I256", 256, "float32"),
        ("B256", 256, "bfloat16"), ("LG", 1280, "float16"), ("DC", 16, "float32"),
        ("CM", 256, "bfloat16"), ("RS", 256, "float32"), ("RM", 256, "float32"), ("DU", 32, "float32"), ("G8", 128, "float32"),
        ("YB", 5 * 144, "bfloat16"), ("Y16", 144, "float16"), ("MBF", 28 * 128, "bfloat16"), ("MF", 3 * 128, "float16"), ("DK", 16 * 128, "float16")):
    SCRATCH[_n] = ("sbuf", [128, _w], _d)
SCRATCH["EQ"] = ("sbuf", [128, 32, 256], "bfloat16")
for _n in range(8):
    SCRATCH["P%d" % _n] = ("psum", [128, 512], "float32")
NDMA = 40
DBG = []
ORDER = []
DBG2 = []
SEED, SWAPS, HEAT, BYTE, JOGS, WARM = 9, 9000, 0.25, 6e-4, 1000, 0.5
GUESS = ((1.0, 1.0, 0.21, 0.0, 1.15, 0.0), (0.92, 1.2, 0.16, -0.4, 1.05, -0.5), (1.35, 0.75, 0.2, 0.4, 1.5, 0.4), (1.3, 1.6, 0.26, 0.0, 1.45, 0.0))
SEQ = ("PR", "AG", "KG", "EQ")
XPW = "VAA"
LEAD = {"exp": -200.0, "lam": -200.0, "cand": -100.0}
MILE, GCP, SAME, GVA, PAIR, UDMA, VF = 1.0, "A", 1.0, True, False, True, 0.03
FCUT, PHV, XO, TKG = (0, 64, 128, 192, 256), 5, (0, 1, 2), 15
YCUT = (0, 512, 1024, 1536, 2048)
KB, EB, KVL, TOT = 1, (6, 7), "V", 192
SEMAPHORES = ["eV", "eA", "eP", "eG", "rCL", "rU"] + ["d%d" % _n for _n in range(NDMA)] + [_a + str(_n) for _a in ("a", "x", "n", "m", "la", "lx", "ln", "lm") for _n in range(3)]


def S(name, c0=0, c1=None, step=1, p=(0, 128, 1)):
    return (name, p, c0, SCRATCH[name][1][1] if c1 is None else c1, step)


def orders(T, topo):
    n = len(T.cores)
    return [sorted([(q + d) % n for d in range(1, n)], key=lambda r: (topo.die(T.cores[r]) == topo.die(T.cores[q]), (r - q) % n != 2, (r - q) % n)) for q in range(n)]


def hazards(ops, pe_chain):
    recs, out = {}, []
    for i, o in enumerate(ops):
        dep = set()
        acc = []
        for d, wr in [(d, False) for d in o["r"]] + [(d, True) for d in o["w"]]:
            pm = 0
            for x in range(*d[1]):
                pm |= 1 << x
            acc.append((d, wr, pm))
            ps = SCRATCH[d[0]][0] == "psum"
            for (m2, a, b, j, w2, s2) in recs.get(d[0], []):
                same = ops[j]["q"] == o["q"]
                if same and o["q"] == "P":
                    if pe_chain and ps: dep.add(j)
                elif (ps and not same) or ((wr or w2) and (m2 & pm) and a < d[3] and d[2] < b and not (d[0] == "RG" and (a - d[2]) % min(s2, d[4]))):
                    dep.add(j)
        for d, wr, pm in acc:
            l = recs.setdefault(d[0], [])
            if SCRATCH[d[0]][0] == "psum":
                if l and ops[l[-1][3]]["q"] != o["q"]:
                    l[:] = [e for e in l if ops[e[3]]["q"] == ops[l[-1][3]]["q"]]
                elif l and o["q"] == "P":
                    l.pop()
            elif wr:
                l[:] = [e for e in l if not ((e[0] & ~pm) == 0 and e[1] >= d[2] and e[2] <= d[3] and (d[4] == 1 or (e[5] == d[4] and (e[1] - d[2]) % d[4] == 0)))]
            l.append((pm, d[2], d[3], i, wr, d[4]))
        out.append(dep)
    return out


def arrange(ops):
    n = len(ops); pre = hazards(ops, True); qs = [o["q"] for o in ops]
    if ORDER:
        at = {i: k for k, i in enumerate(ORDER)}
        assert len(ORDER) == n and all(at[j] < at[i] for i in range(n) for j in pre[i])
        return [ops[i] for i in ORDER]

    anc = []
    for i in range(n):
        m = 0
        for j in pre[i] | set(ops[i]["after"]):
            m |= anc[j]
        pre[i] = set(j for j in pre[i] if ops[j]["lat"] or not m >> j & 1)
        for j in pre[i] | set(ops[i]["after"]):
            m |= 1 << j
        anc.append(m)

    def graph(fc, fg, hop, far, fp, near):
        c = [o["c"] * (1.0 if o["dma"] or o["lat"] else fg if o["ind"] else fp if o["q"] == "P" else fc) for o in ops]
        lt = [o["lat"] + (near if o["dma"] else far if o["lat"] else 0.0) for o in ops]
        ed = []
        for i in range(n):
            e = {j: c[j] + (lt[j] if qs[i] is None else 0.0) for j in ops[i]["after"]}
            for j in pre[i]:
                e[j] = c[j] + (0.0 if qs[i] == qs[j] == "P" else lt[j] + hop * (SAME if qs[i] == qs[j] and not lt[j] else 1.0))
            ed.append(list(e.items()))
        return c, ed
    guess = [graph(*x) for x in GUESS]
    far = [i for i in range(n) if ops[i]["lat"] and not ops[i]["dma"]]
    c, edges = guess[0]
    back = [[] for _ in range(n)]
    for i in range(n):
        for j, l in edges[i]:
            back[j].append((i, l - c[j] + c[i]))

    def place(key, ed, to):
        left = [len(e) for e in ed]; st, busy = [0.0] * n, {q: ([], []) for q in "VAPGS"}
        ready = sorted(((key[i], i) for i in range(n) if not left[i]), reverse=True)
        while ready:
            i = ready.pop()[1]; t = 0.0
            for j, l in ed[i]:
                if st[j] + l > t: t = st[j] + l
            if qs[i] is not None:
                a, z = busy[qs[i]]; lo, k, d = 0, len(a), c[i] - 1e-9
                while lo < k:
                    mid = (lo + k) // 2
                    if z[mid] <= t: lo = mid + 1
                    else: k = mid
                while k < len(a) and a[k] < t + d:
                    if z[k] > t: t = z[k]
                    k += 1
                a.insert(k, t); z.insert(k, t + c[i])
            st[i] = t
            for j, _ in to[i]:
                left[j] -= 1
                if not left[j]:
                    x = (key[j], j); lo, k = 0, len(ready)
                    while lo < k:
                        mid = (lo + k) // 2
                        if ready[mid] > x: lo = mid + 1
                        else: k = mid
                    ready.insert(lo, x)
        return st

    def worth(st):
        seq = sorted(range(n), key=lambda i: (st[i], i)); tot = 0.0
        for (cc, ed), x in zip(guess, GUESS):
            s, free = [0.0] * n, {}
            for i in seq:
                t = free.get(qs[i], 0.0)
                for j, l in ed[i]:
                    if s[j] + l > t: t = s[j] + l
                s[i] = t
                if qs[i] is not None: free[qs[i]] = t + cc[i]
            tot += (s[n - 1] + MILE * sum(s[i] for i in far) / len(far)) / (x[0] + x[1])
        return tot, seq
    pr = list(c)
    for i in range(n - 1, -1, -1):
        for j, l in edges[i]:
            pr[j] = max(pr[j], l + pr[i])
    tags = sorted(set(o["tag"] for o in ops)); tg = [tags.index(o["tag"]) for o in ops]
    rng = numpy.random.default_rng(SEED); best = None; lead = (0.0, [LEAD.get(x[:-1], 0.0) for x in tags])
    for k in range(PASSES):
        x = list(lead[1])
        for _ in range(k and 2):
            x[int(rng.integers(len(x)))] += float(rng.normal()) * (1.0, 4.0, 10.0)[k % 3]
        st = place([-pr[i] - x[tg[i]] for i in range(n)], edges, back)
        w = worth(st) + (st,)
        if k == 0 or w[0] < lead[0] + 0.1: lead = (w[0], x)
        best = min(best or w, w)
    cur = best
    for k in range(JOGS):
        st = cur[2]; t0 = rng.random() * max(st); t1 = t0 + 3.0 + 12.0 * rng.random()
        near = [i for i in range(n) if t0 <= st[i] < t1]; key = list(st)
        if k % 2:
            x = tg[near[int(rng.integers(len(near)))]]; d = float(rng.normal()) * (1.0, 3.0)[k // 2 % 2]
            for i in near:
                if tg[i] == x: key[i] += d
        else:
            for i, d in zip(near, (rng.random(len(near)) * (0.3, 1.0)[k // 2 % 2]).tolist()):
                key[i] += d
        if k % 16 == 0:
            sb = place([-key[i] - c[i] for i in range(n)], back, edges); key = [-sb[i] - c[i] for i in range(n)]
        st = place(key, edges, back); w = worth(st) + (st,)
        if w[0] < cur[0] + WARM * (1 - k / JOGS) * rng.random(): cur = w
        best = min(best, w)
    ps = [set(j for j, _ in e) for e in edges]

    def replay(seq):
        tot, why = 0.0, []
        for (cc, ed), x in zip(guess, GUESS):
            s, by, free = [0.0] * n, [-1] * n, {}
            for i in seq:
                t, y = free.get(qs[i], (0.0, -1))
                for j, l in ed[i]:
                    if s[j] + l >= t: t = s[j] + l; y = j
                s[i] = t; by[i] = y
                if qs[i] is not None: free[qs[i]] = (t + cc[i], i)
            tot += (s[n - 1] + MILE * sum(s[i] for i in far) / len(far)) / (x[0] + x[1]); why.append(by)
        return tot, why, seq
    cur = top = replay(best[1])
    for k in range(SWAPS):
        by = cur[1][k % len(GUESS)]; v = far[int(rng.integers(len(far)))] if k // len(GUESS) % 2 else n - 1; pairs = []
        while by[v] >= 0:
            if by[v] not in ps[v]: pairs.append((by[v], v))
            v = by[v]
        if not pairs: continue
        u, v = pairs[int(rng.integers(len(pairs)))]
        seq = cur[2]; a, z = seq.index(u), seq.index(v); need, held, head, rest = set(ps[v]), set(), [], []
        for x in seq[z - 1:a:-1]:
            if x in need or qs[x] in held:
                head.append(x); need |= ps[x]; held.add(qs[x] or x)
            else:
                rest.append(x)
        if u in need or qs[u] in held: continue
        tail = rest[::-1] + seq[z + 1:]; r = (0, 0, 1, 2, 4, 8)[int(rng.integers(6))]; m = 0
        while r and u not in ps[tail[m]]:
            r -= qs[tail[m]] == qs[u]; m += 1
        new = replay(seq[:a] + head[::-1] + [v] + tail[:m] + [u] + tail[m:])
        if new[0] < cur[0] + HEAT * (1 - k / SWAPS) * rng.random():
            cur = new
            if cur[0] < top[0]: top = cur
    st, free = [0.0] * n, {}
    for i in top[2]:
        st[i] = max([free.get(qs[i], 0.0)] + [st[j] + l for j, l in edges[i]])
        if qs[i] is not None: free[qs[i]] = st[i] + c[i]
    DBG2[:] = [dict(zip(tags, lead[1])), best[0]]
    DBG[:] = [max(st), st, ops, [[(j, l - c[j]) for j, l in e] for e in edges], top[0]]
    ORDER.extend(top[2])
    return [ops[i] for i in ORDER]


def emit(g, T, ops):
    Q = {"V": g.vector, "A": g.scalar, "P": g.tensor, "G": g, "S": g.sync}
    pre = hazards(ops, False)
    known, clock, waits, need, cnt, last = {q: {} for q in Q}, {}, [], set(), {}, {}
    for o, dp in zip(ops, pre):
        q, tok = o["q"], o["tok"]
        if tok is None:
            cnt[q] = cnt.get(q, 0) + 1
            tok = o["tok"] = ("e" + q, cnt[q])
            o["eng"] = True
        dep, ws = {}, []
        for j in dp:
            s, v = ops[j]["tok"]
            dep[s] = max(dep.get(s, 0), v)
        if q is not None:
            for s, v in sorted(dep.items()):
                if known[q].get(s, 0) < v and not any(s2 != s and clock[(s2, v2)].get(s, 0) >= v for s2, v2 in dep.items()):
                    ws.append((s, v))
            for s, v in dep.items():
                for s2, v2 in clock[(s, v)].items():
                    known[q][s2] = max(known[q].get(s2, 0), v2)
            need.update(ws)
            clock[tok] = dict(known[q])
        else:
            clock[tok] = {}
        clock[tok][tok[0]] = tok[1]
        waits.append(ws)
        last[tok[0]] = max(tok[1], last.get(tok[0], 0))
    num, c = {}, {}
    for o in ops:
        if o.get("eng") and o["tok"] in need:
            c[o["tok"][0]] = c.get(o["tok"][0], 0) + 1
            num[o["tok"]] = c[o["tok"][0]]
    for o, ws in zip(ops, waits):
        if o["q"] is None:
            continue
        for w in ws:
            Q[o["q"]].wait_ge(T.sem[w[0]], num.get(w, w[1]))
        ins = o["f"](Q[o["q"]])
        if o["tok"] in num:
            ins.then_inc(T.sem[o["tok"][0]], 1)
        elif o["dma"]:
            ins.then_inc(T.sem[o["tok"][0]], 16)
    for s, v in sorted(last.items()):
        if s[0] != "e":
            g.wait_ge(T.sem[s], v)


def rank_program(g, core, T, topo):
    rank = T.rank_of(core)
    if rank is None:
        return
    n = len(T.cores)
    order = orders(T, topo)
    to = order[rank]
    fr = [[q for q in range(n) if q != rank and order[q][i] == rank][0] for i in range(3)]
    dto = [(r - rank) % n for r in to]
    ops, nd, rc, sends, sent, prev, tag = [], [0], {}, [], {}, {}, ["load"]

    def ap(d):
        if not isinstance(d, tuple):
            return d
        if d[0] == "ind":
            return ap(d[1]).indirect(ap(d[2]))
        if d[0] == "EQ":
            return T["EQ"][:, d[2] // 256:d[3] // 256, 0:16] if d[4] == 16 else T["EQ"][:, d[2] // 256, d[2] % 256:(d[3] - 1) % 256 + 1]
        return T[d[0]][d[1][0]:d[1][1]:d[1][2], d[2]:d[3]:d[4]] if (d[4] != 1 or d[1][2] != 1) else T[d[0]][d[1][0]:d[1][1], d[2]:d[3]]

    def I(win, off):
        return ("ind", win, off)

    def width(d):
        return 16 * width(d[2]) if d[0] == "ind" else len(range(d[2], d[3], d[4]))

    def cost(q, out, ins, mul=1.0):
        w = max(width(out), width(ins[0]))
        if out[0] == "ind": return FIX + w * SCA * CY
        if ins[0][0] == "ind": return FIX + w * GAT * CY
        if q == "A": return FIX + max(64, w) * CY
        if mul == 1.0 and all(SCRATCH[d[0]][2] in ("bfloat16", "float16", "uint16") for d in [out] + ins): mul = 0.5
        return VF + max(64, w * mul) * CY

    def op(q, f, out, ins, c, tok=None, dma=False, lat=0.0, after=()):
        r, w = [], []
        for d in ins:
            if isinstance(d, tuple):
                r += [d[1], d[2]] if d[0] == "ind" else [d]
        if isinstance(out, tuple):
            if out[0] == "ind":
                w.append(out[1]); r.append(out[2])
            else:
                w.append(out)
        ops.append({"q": q, "f": f, "r": r, "w": w, "tok": tok, "dma": dma, "c": c, "lat": lat, "after": list(after), "tag": tag[0],
                    "ind": any(isinstance(d, tuple) and d[0] == "ind" for d in [out] + ins)})
        if w and q in ("V", "A") and w[0][0] in SEQ:
            k = (q, w[0][0])
            if k in prev: ops[-1]["after"].append(prev[k])
            prev[k] = len(ops) - 1

    def tt(out, a, b, o):
        ps = a[0] != "ind" and "psum" in (SCRATCH[a[0]][0], SCRATCH[b[0]][0])
        op("V", lambda q: q.tensor_tensor(ap(out), ap(a), ap(b), o), out, [a, b], cost("V", out, [a], 1.001 if ps else 2.0))

    def ts(out, a, s1, o0, s2=None, o1=None):
        if o1 is None:
            op("V", lambda q: q.tensor_scalar(ap(out), ap(a), ap(s1), None, o0), out, [a, s1], cost("V", out, [a]))
        else:
            op("V", lambda q: q.tensor_scalar(ap(out), ap(a), ap(s1), ap(s2), o0, o1), out, [a, s1, s2], cost("V", out, [a]))

    def cp(out, a): op("V", lambda q: q.tensor_copy(ap(out), ap(a)), out, [a], cost("V", out, [a]))
    def ms(out, v): op("V", lambda q: q.memset(ap(out), v), out, [], cost("V", out, [out]))
    def scan(out, a, b, ini, o0, o1): op("V", lambda q: q.tensor_tensor_scan(ap(out), ap(a), ap(b), ini, o0, o1), out, [a, b], cost("V", out, [a, b]))

    def act(out, a, f=AF.Copy, bias=None, scale=None):
        k = {}
        if bias is not None: k["bias"] = ap(bias)
        if scale is not None: k["scale"] = ap(scale)
        op("A", lambda q: q.activation(ap(out), ap(a), f, **k), out, [a, bias, scale], cost("A", out, [a]))

    def mm(out, l, r, start, stop, w=None):
        op("P", lambda q: q.matmul(ap(out), ap(l), ap(r), start, stop), out, [l, r],
           max(min(64, width(l)), w or width(r)) * PEC * (4 if SCRATCH[l[0]][2] == "float32" else 1))

    def mms(out, terms, whole=True):
        for j, (l, r) in enumerate(terms):
            mm(out, l, r, j == 0, j == len(terms) - 1)
        if whole: unit(len(terms))

    def unit(k):
        l = ops[-k:]; del ops[-k:]
        op("P", lambda q: [o["f"](q) for o in l][-1], l[0]["w"][0], [d for o in l for d in o["r"]], sum(o["c"] for o in l))

    def iota(out, pat, base, cm):
        c = 0.13 + 2 * width(out) * CY
        if SCRATCH[out[0]][2] == "int32":
            op("G", lambda q: q.iota(ap(out), pat, base, cm), out, [], c)
        else:
            op("G", lambda q: q.iota(ap(out), pat, base, cm, allow_small_or_imprecise_dtypes=True), out, [], c)

    def fill(out, v): iota(out, [[0, width(out)]], v, 0)

    def diag(out, a, v, shift):
        op("G", lambda q: q.affine_select(ap(out), ap(a), [[1, 128]], O.not_equal, v, -shift, -1), out, [a], 0.17 + 256 * CY)

    def gcopy(out, a):
        if GCP == "A": return act(out, a)
        op("G", lambda q: q.affine_select(ap(out), ap(a), [[0, width(a)]], O.is_ge, 0.0, 0, 0), out, [a], 0.17 + 2 * width(a) * CY)

    def rowsel(out, a, v, r):
        op("G", lambda q: q.affine_select(ap(out), ap(a), [[-16, 8], [0, 16]], O.not_equal, v, -r, 1), out, [a], 0.17 + 256 * CY)

    def dma(q, out, a, more=0.0, wait=(), part=None):
        if not part: nd[0] += 1
        tok = ("d%d" % (nd[0] - 1), 16) if part is None else ("r" + out[0], 16 * part + 16)
        op(q, lambda e: e.dma_start(ap(out), ap(a)), out, [a] + list(wait), DISS, tok, True, LDMA + more, [len(ops) - 2] if part else ())

    def send(peer, dst, src, rs, ls, more=0.0):
        c = T.cores[peer]; rid, pid, _ = topo.addr(c)
        rc[ls] = rc.get(ls, 0) + len(topo.engines(core, c))
        op("G", lambda q: q.remote_dma(ap(dst), ap(src), T.sem[rs], T.sem[ls], pid, rid, topo.mask(core, c)), None, [src],
           ISS + (0 if sends else FIRST), (ls, rc[ls]), False, RDMA + width(src) * BYTE + more, sends[-1:])
        sends.append(len(ops) - 1); sent[rs] = len(ops) - 1

    def halves(src, dst):
        el = topo.engines(src, dst)
        return el[1::2], el[0::2]

    def pair(trs, ls, more):
        l = []
        for h, (peer, dst, src, rs) in enumerate(trs):
            c = T.cores[peer]; rid, pid, _ = topo.addr(c); el = halves(core, c)[h]
            l.append((DstId(rid=rid, pnc=pid), sum(1 << e for e in el), rs, src, dst)); rc[ls] = rc.get(ls, 0) + len(el); sent[rs] = len(ops)
        op("G", lambda q: q.remote_dma_fused([RemoteDMATransfer(dst_ids=[x[0]], dma_engine_mask=x[1], remote_sem=T.sem[x[2]], src=ap(x[3]), dst=ap(x[4])) for x in l],
                                             local_sem=T.sem[ls]), None, [x[3] for x in l], ISS, (ls, rc[ls]), False, RDMA + 2 * width(l[0][3]) * BYTE + more, sends[-1:])
        sends.append(len(ops) - 1)

    def swap(peers, dst, src, s):
        if PAIR:
            pair([(peers[2], sub(dst[2], (0, 512)), sub(src[2], (0, 512)), s + "2"), (peers[1], dst[1], src[1], s + "1")], "l" + s + "1", 0.0)
            pair([(peers[2], sub(dst[2], (512, 768)), sub(src[2], (512, 768)), s + "2"), (peers[0], dst[0], src[0], s + "0")], "l" + s + "0", 0.3)
        else:
            for i in (2, 1, 0) if s == "a" else XO:
                send(peers[i], dst[i], src[i], s + str(i), "l" + s + str(i), (0.15, 0.15, 0.0)[i] if s == "a" or XO[0] else 0.0)

    def recv(peer, dst, rs):
        rc[rs] = rc.get(rs, 0) + len(topo.engines(T.cores[peer], core)) // (2 if PAIR and rs in ("a0", "a1", "x0", "x1") else 1)
        op(None, None, dst, [], 0.0, (rs, rc[rs]), False, 0.0, [sent[rs]])

    def P(b, c0=0, c1=256, step=1, p=(0, 128, 1)): return S("P%d" % b, c0, c1, step, p)
    def col(name, j): return S(name, j, j + 1)
    names = ["I", "ROT", "ROTM", "ROT23", "RINV", "NRI", "N3", "N2", "N1", "I64", "NB", "D01", "R01", "R23", "R45", "NR45", "R6", "RKB", "RIV", "RB",
             "WD", "WF", "DF", "GT", "WE", "I16", "RC", "RU"]
    def mb(x): return S("MBF", 128 * names.index(x), 128 * names.index(x) + 128)
    n16 = ["I", "BK", "B15"]
    def mf(x): return S("MF", 128 * n16.index(x), 128 * n16.index(x) + 128)
    ny = ["1", "45", "236", "23", "01"]
    def Y(x, k): return S("YB", 144 * ny.index(x) + 15 - k, 144 * ny.index(x) + 143 - k)
    def row(name, r, c0, w): return S(name, c0, c0 + w, 1, (r, 128, 16))
    def b2(j): return S("B2", 128 * j, 128 * j + 128)
    def blk(name, j): return S(name, 256 * j, 256 * j + 256)
    def sub(d, c): return d[:2] + (d[2] + c[0], d[2] + c[1], 1)
    def xp(j): return S("AW", XB + 256 * j, XB + 256 * j + 256)
    def fw(i): return S("AW", FB[i], FB[i] + 256 * (i + 1))
    def il(c0, w): return S("IL", I0 + c0, I0 + c0 + w)
    def kc(j): return col("KC", j)
    def tk(k): return S("TK", 128 * k, 128 * k + 128) if k else S("BK")
    def m16(j): return col("M16", j)
    def m2(j): return col("M2", j)
    kcol = kc(0); io = S("IO", 0, 128); p8 = (0, 8, 1); Y1 = S("YB", 0, 144)
    def FX(b, f): return S("FX%d" % b, 256 * f, 256 * f + 256)

    dma("S", S("SN"), T["snd"][:], -0.5); dma("A", S("DI", 0, 128), T["ti"][:], -0.4); dma("S", S("DI", 288, 416), T["kd"][:], -0.3); dma("S", S("A0", 0, E), T["a0"][:], 1.3)
    ops[2]["after"], ops[3]["after"] = [0], [2]
    dma("S", S("CA"), T["ca"][:], 2.0); dma("S", S("BE", 0, 1), T["be"][:], 2.0)
    for c0, c1, x in ((128, 160, "bg"), (416, 448, "cl"), (448, 528, "us"), (160, 288, "lp")):
        dma("S", S("DI", c0, c1), T[x][:], 2.0)
    dma("S", S("KW", 0, E), T["k0"][:], 2.0, [S("SN")])
    for k in range(4, 11):
        ops[k]["after"] = [k - 1]
    iota(col("KI", 0), [[1, 1]], 0, 1); iota(S("I256"), [[1, 256]], 0, 0); iota(S("IO"), [[1, 144]], 0, -1)
    ms(S("Z"), 0.0)
    diag(mb("ROT"), S("Z"), 1.0, 16); diag(mb("ROT"), mb("ROT"), 1.0, -112)
    for x, v in (("I", 1.0), ("I64", 64.0), ("I16", 16.0), ("N3", -3.0), ("N2", -2.0), ("N1", -1.0), ("NB", -BIG)):
        diag(mb(x), S("Z"), v, 0)
    diag(mb("RINV"), S("Z"), 1.0, -16); diag(mb("RINV"), mb("RINV"), 1.0, 112); diag(mb("NRI"), S("Z"), -1.0, -16); diag(mb("NRI"), mb("NRI"), -1.0, 112)
    diag(b2(0), S("Z"), -1.0, 1)
    ts(col("KI", 1), col("KI", 0), 15, O.bitwise_and); cp(kcol, col("KI", 1))
    ts(S("M16"), S("I256", 0, 16), kcol, O.is_equal); tt(S("M2"), S("M16", 0, 16, 2), S("M16", 1, 16, 2), O.add)
    iota(S("KH", 0, 16), [[256, 16]], -CD, 0); ts(S("KH", 16, 32), S("KH", 0, 16), m16(2), O.mult)
    ts(S("KH", 32, 48), S("KH", 0, 16), float(XB), O.add, m16(2), O.mult)
    tt(kc(1), m16(1), m16(3), O.add); ts(S("B256"), S("I256"), kc(1), O.mult)
    for j in range(3):
        ts(blk("XD", j), S("B256"), col("KH", 32 + j), O.add)
    for j in range(4):
        ts(S("PH", 128 * j, 128 * j + 128), S("B256", 0, 256, 2), col("KH", 16 + j), O.add)
    for j in range(2, 8):
        ts(blk("PH", j), S("B256"), col("KH", 18 + j), O.add) if j < PHV else act(blk("PH", j), S("B256"), AF.Identity, col("KH", 18 + j))
    for j in range(6):
        ms(S("IL", 344 * j, 344 * j + 344), 1.0)
    ts(S("DB", 816, 944), S("Z"), kcol, O.add, 128.0, O.mult); cp(S("DB", 944, 1072), S("I256", 0, 128))
    tt(kc(2), m2(0), m2(1), O.add); ts(kc(4), kc(2), -1.0, O.mult, 1.0, O.add)
    for i in range(3):
        ts(kc(16 + i), m16(0), float(E + 256 * (dto[i] - 1)), O.mult); ts(kc(5 + i), m16(2), float(FB[i] - XB), O.mult, kc(16 + i), O.add)
    ts(S("J"), S("IO"), kcol, O.add); ts(Y1, S("J"), 15.0, O.is_equal)
    act(b2(4), S("J", 0, 128), AF.Abs, -7.5); ts(S("BK"), b2(4), 8.0, O.is_lt)
    act(mb("ROTM"), mb("ROT"), scale=kc(4)); act(mb("D01"), mb("I"), scale=m2(0)); act(mb("ROT23"), mb("ROT"), scale=m2(1))
    ts(kc(3), m16(6), 0.0625, O.mult, m2(1), O.add)
    for x, c in (("45", m2(2)), ("236", kc(3)), ("23", m2(1)), ("01", m2(0))):
        act(S("YB", 144 * ny.index(x), 144 * ny.index(x) + 144), Y1, scale=c)
    ts(kc(8), m16(8), -10240.0, O.mult, m16(9), O.add); ts(kc(9), m16(6), 8.0, O.mult, kc(8), O.add)
    ts(kc(10), m16(8), -1408.0, O.mult, m2(0), O.add); ts(kc(13), m2(2), -1.0, O.mult)
    for x, c in (("RKB", kc(9)), ("NR45", kc(13)), ("R01", kc(10))):
        act(mb(x), S("BK"), scale=c)
    for x, v, rows in (("R23", 1.0, (2, 3)), ("R45", 1.0, (4, 5)), ("R6", 1.0, (6,)), ("RB", 1.0, (10, 11)), ("WE", -BIG, (15,))):
        for j, r in enumerate(rows):
            rowsel(mb(x), mb(x) if j else S("Z"), v, r)
    rowsel(mb("RIV"), S("Z"), -100.0, 7); rowsel(mb("RIV"), mb("RIV"), 100.0, 8)
    act(mb("WF"), S("BK"), scale=BIG); act(S("I32"), mb("I"))
    cp(S("Y16"), Y1); cp(mf("I"), mb("I")); cp(mf("BK"), S("BK")); ts(mf("B15"), S("BK"), m16(15), O.mult)
    iota(b2(5), [[0, 8], [1, 16]], 1, 0); tt(b2(2), b2(5), S("BK"), O.mult)
    for k in range(1, 16):
        if k <= TKG:
            op("G", lambda q, k=k: q.affine_select(ap(tk(k)), ap(S("BK")), [[0, 8], [1, 16]], O.is_ge, 0.0, -k, 0), tk(k), [S("BK")], 0.17 + 256 * CY)
        else:
            ts(tk(k), b2(2), k + 0.5, O.is_gt)
    ts(b2(3), io, 1.0, O.is_ge, BIG, O.mult); tt(mb("WD"), b2(3), S("BK"), O.mult)
    ts(kc(12), m16(15), -1.0, O.mult, 1.0, O.add); act(b2(1), b2(0), scale=kc(12)); diag(mb("DF"), b2(1), 1.0, 0)
    act(S("D32"), mb("DF")); act(S("L32"), S("BK"), scale=m16(15))
    tt(S("DC", 1, 16), S("M16", 1, 16), S("M16", 0, 15), O.subtract)
    for k in range(1, 16):
        ts(S("DK", 128 * k, 128 * k + 128), S("BK"), col("DC", k), O.mult)
    iota(S("G8", 0, 128, 1, p8), [[1, 8], [0, 16]], 0, -1)
    GT = mb("GT")[:1] + (p8,) + mb("GT")[2:]
    ts(GT, S("G8", 0, 128, 1, p8), 0.0, O.is_equal)
    tt(kc(14), m16(8), m16(0), O.subtract); cp(col("IL", I0 - 1), kc(14))
    ms(S("IL", LB + E, ILN), 0.0); cp(col("IL", LB + E), kc(14))
    fill(S("AW", 2560, XB), 0); fill(S("AW", FB[0], FB[2] + 768), 0)
    iota(blk("TT", 0), [[0, 16], [1, 16]], 0, 0); iota(blk("TT", 1), [[1, 256]], E + 1 - int(BIG), 0); iota(S("DU"), [[16, 32]], 1408, 0)
    ts(S("CM"), blk("TT", 0), kcol, O.subtract, 2.0 ** 26, O.mult); act(blk("TT", 2), S("CM"), AF.Abs); tt(S("RS"), blk("TT", 1), blk("TT", 2), O.subtract)
    ms(S("RM"), -0.0625); ms(S("RM", 0, 256, 16), 2.0 ** 20); ts(S("DU"), S("DU"), kcol, O.add)
    act(col("BE", 1), col("BE", 0), scale=-1.0)
    fill(S("RG", 0, 8192, 16), 0)
    for i in range(3):
        cp(S("uS", 16 * i, 16 * i + 16), S("SN", 16 * (dto[i] - 1), 16 * dto[i]))
    for a, z in ((0, 128), (128, 288)):
        cp(S("DB", a, z), S("DI", a, z)); tt(S("DB", 288 + a, 288 + z), S("DI", a, z), S("DB", a, z), O.subtract)
    cp(S("DB", 576, 704), S("DI", 288, 416)); cp(S("DB", 704, 736), S("DI", 416, 448)); ts(S("DB", 736, 816), S("DI", 448, 528), 2.0 ** -8, O.mult)
    fill(S("AUX", 0, 512), 0) if UDMA else ms(S("AUX"), 0.0)
    for q, x, r, at, c0, w in (("A", "IL", 0, I0, 816, 128), ("A", "IL", 1, I0, 944, 128), ("S", "IL", 4, I0, 0, 128), ("S", "IL", 5, I0, 288, 128), ("S", "IL", 6, I0, 576, 128), ("S", "AUX", 10, 0, 128, 32), ("S", "AUX", 11, 0, 416, 32)):
        dma(q, row(x, r, at, 16 * w), S("DB", c0, c0 + w), 0.3 if w == 128 else 0.0)
    for i in range(3):
        act(blk("G1", i), I(il(0, E), S("uS", 16 * i, 16 * i + 16)))
    for b in range(2):
        cp(blk("cI", b), blk("CA", b)); ts(FX(b, 2), blk("cI", b), -1408.0, O.add)
    for i in range(3):
        act(xp(i), I(S("A0", 0, E), S("uS", 16 * i, 16 * i + 16)))
        mm(P(i), mb("ROT"), xp(i), True, True)
        act(blk("XR", i), P(i))
        send(to[i], blk("A0", 7 + dto[i]), blk("XR", i), "m%d" % i, "lm%d" % i)
    for i in (2, 1, 0):
        cp(I(S("PH"), S("uS", 16 * i, 16 * i + 16)), blk("XD", i))
    for i in range(3):
        if i: cp(blk("G2", i), I(S("PH"), S("uS", 16 * i, 16 * i + 16)))
        c0 = 256 * (dto[i] - 1)
        mms(P(5 + i), [(mb("D01"), blk("XD", 0)), (mb("ROTM"), blk("G1", i)), (mb("ROT23"), blk("G2" if i else "XD", i))], False)
        act(blk("IM", i), P(5 + i), AF.Identity, kc(5 + i))
        send(to[i], il(E + c0, 256), blk("IM", i), "n%d" % i, "ln%d" % i)
    dma("S", row("IL", 2, I0, E), row("PH", 2, 0, E), 0.3); dma("A", row("IL", 3, I0, E), row("PH", 3, 0, E), 0.3)
    for i in range(3):
        d = (rank - fr[i]) % n
        recv(fr[i], blk("A0", 7 + d), "m%d" % i); recv(fr[i], il(E + 256 * (d - 1), 256), "n%d" % i)
    dma("S", S("AW", 1024, 2560), T["a0"][:, 512:E], 1.0, [il(E, 768)])
    dma("S", S("AW", 0, 1024), T["a0"][:, 0:1024], 1.5, [il(E, 768)]); dma("S", S("AW", FB[2] + 768, AWN), T["a0"][:, 0:AWN - FB[2] - 768], 1.5, [il(E, 768)])
    dma("S", S("KW", E, E + 256), T["k0"][:, 0:256], 1.5, [il(E, 768)]); dma("S", S("IL", LB, LB + E), T["k0"][:], 2.5, [il(E, 768)])
    act(S("AW", 0, 1024, 2), S("A0", 0, 512))
    dma("S", row("IL", 0, LB, E), S("DB", 160, 288), 0.3); dma("S", row("IL", 1, LB, E), S("DB", 448, 576), 0.3)

    def floor32(ps, j, c=(0, 256)):
        act(sub(blk("AB", j), c), ps, AF.Abs); act(sub(blk("HI", j), c), sub(blk("AB", j), c), AF.Identity, 159.515625, 0.03125)

    def facts(b, who, bk, c):
        own = il(256 * b + c[0], c[1] - c[0]); g0 = 4096 * b; w = c[1] - c[0]
        for j in range(c[0] // 32, c[1] // 32):
            o, x = S("PR", g0 + 512 * j, g0 + 512 * j + 512), I(il(0, 2816), S("cI", 256 * b + 32 * j, 256 * b + 32 * j + 32))
            cp(o, x) if who[j] == "V" else act(o, x)
        mm(P(bk[0], 0, w), mb("NR45"), own, True, False); mm(P(bk[1], 0, w), mb("RKB"), own, True, False)
        for x, z in (("45", bk[0]), ("236", bk[2])):
            for j in range(c[0] // 64, c[1] // 64):
                for k in range(16):
                    mm(P(z, 64 * j - c[0], 64 * j + 64 - c[0]), Y(x, k), S("PR", g0 + 1024 * j + k, g0 + 1024 * j + 1024, 16),
                       x == "236" and k == 0, k == 15 and (x == "236" or j == c[1] // 64 - 1))
                unit(16)
        ts(sub(FX(b, 0), c), P(bk[2], 0, w), 1.5 * 2 ** 23, O.add, 1.5 * 2 ** 23, O.subtract)
        tt(sub(blk("KD", b), c), P(bk[2], 0, w), sub(FX(b, 0), c), O.subtract); mm(P(bk[1], 0, w), mb("I16"), sub(blk("KD", b), c), False, False)
        floor32(P(bk[0], 0, w), b, c); mm(P(bk[1], 0, w), mb("I64"), sub(blk("HI", b), c), False, True)
        if b == 0: ts(sub(blk("cB", b), c), P(bk[1], 0, w), -1.0, O.add)
        cp(sub(FX(b, 1), c), P(bk[1], 0, w))
        if b: ts(sub(blk("cB", b), c), sub(FX(b, 1), c), -1.0, O.add)
        if c[1] == 256: cp(blk("LG", b), blk("AB", b))

    tag[0] = "first"
    for j, (a, z) in enumerate(zip(FCUT[:-1], FCUT[1:])):
        facts(0, WHO0, ((2, 3, 4), (5, 6, 7))[j % 2], (a, z))
    tag[0] = "draws"
    if UDMA:
        for r in range(16):
            dma("S", row("CL", r, 0, 512), S("DB", 704, 736), 0.0, (), r); dma("S", row("U", r, 0, 1280), S("DB", 736, 816), 0.0, (), r)
        ts(S("OH"), S("CL"), kcol, O.is_equal)
    else:
        dma("S", row("AUX", 12, 0, 512), S("DB", 704, 736)); dma("S", row("AUX", 13, 0, 1280), S("DB", 736, 816))
        rowsel(mb("RC"), S("Z"), 1.0, 12); rowsel(mb("RU"), S("Z"), 1.0, 13)
        for c0, w in ((0, 512), (512, 512), (1024, 256)):
            mm(P(3, 0, w), mb("RU"), S("AUX", c0, c0 + w), True, True); act(S("U", c0, c0 + w), P(3, 0, w))
        mm(P(4, 0, 512), mb("RC"), S("AUX", 0, 512), True, True); ts(S("OH"), P(4, 0, 512), kcol, O.is_equal)
    if not GKA: act(S("C7"), S("OH"), AF.Identity, 7.0, -1.0)
    if not GVA: act(S("XT", 0, 512), S("OH"), AF.Identity, 15.0, -1.0)
    tag[0] = "facts"; facts(1, WHO1, (5, 6, 7), (0, 256))
    ts(blk("cA", 1), FX(1, 0), float(CD), O.add)

    def first_wins(k, key, bank, u, add):
        mm(P(bank), mb("I"), S("CM"), True, False); mm(P(bank), mb("WE"), S("HIT"), False, False); mm(P(bank), mf("BK"), blk("SEL", k), False, False)
        for b in range(16):
            w = 256 - 16 * b; off = 4096 * k + 256 * b
            ts(S("EQ", off, off + w), S("REP", 256 * k + 16 * b, 256 * k + 256), sub(key, (b, b + 1)), O.is_equal)
            if b < 15: mm(P(bank, 16 * b + 16, 256), mb("WF"), S("EQ", off + 16, off + w), False, False)
        mm(P(bank), mb("WD"), S("EQ", 4096 * k, 4096 * k + 4096, 16), False, True)
        scan(blk("SD", k), S("RS"), P(bank), -2.0 ** 26, O.max, O.min)
        ts(u, S("SD", 256 * k + 15, 256 * k + 256, 16), add + BIG, O.add)

    def listed(ps, f):
        mms(ps, [(S("Y16", 15 - a, 143 - a), S("SEL", 256 * f + a, 256 * f + 256, 16)) for a in range(16)])

    def raised(name, win, u, b, cap, ps):
        act(blk(name, 0), I(win, u)); mms(ps, [(mb("I"), blk("OH", b)), (mb("I"), blk(name, 0))], False)
        act(blk(name, 1), ps, AF.Relu, cap, -1.0); act(blk(name, 2), blk(name, 1), AF.Identity, cap, -1.0)

    def capped(out, ps, j, who):
        if who == "V":
            ts(out, ps, 15.0, O.min)
        else:
            act(blk("XT", j), ps, AF.Relu, 15.0, -1.0); act(out, blk("XT", j), AF.Identity, 15.0, -1.0)

    def last_factor(t):
        mm(P(EB[1]), mf("B15"), blk("LG", t), True, True); act(P(EB[1]), P(EB[1]), AF.Exp, None, col("BE", 1))
        tt(blk("YL", t), S("ST", 15, 4096, 16), P(EB[1]), O.mult)
        dma("S", T["yl"][:, 256 * t:256 * t + 256], blk("YL", t))

    for t in range(R):
        b = t % 2; lo = 256 * b; own = il(lo, 256); pr = 4096 * (t % 4); rg = 4096 * b; v0 = 48 * b

        def tn(j): return S("TN", 64 * b + 16 * j, 64 * b + 16 * j + 16)
        def ut(j): return S("uT", 128 * b + 16 * j, 128 * b + 16 * j + 16)

        tag[0] = "exp%d" % t
        mm(P(EB[0]), S("DK", 1024, 1152), blk("LG", t), True, True); act(S("RG", rg + 8, rg + 4096, 16), P(EB[0]), AF.Exp, None, col("BE", 0))
        for k in range(1, 8):
            for h in range(2):
                mm(P(EB[k % 2], h, 512, 2), S("DK", 128 * (k + 8 * h), 128 * (k + 8 * h + 1)), blk("LG", t), True, True)
            unit(2); ops[-1]["w"] = [P(EB[k % 2], 0, 512)]
            act(S("RG", rg + k, rg + 4096, 8), P(EB[k % 2], 0, 512), AF.Exp, None, col("BE", 0))
        if t: last_factor(t - 1)
        tag[0] = "chain%d" % t
        for j, z in zip(CH[:-1], CH[1:]):
            for md, c0, c1 in zip(MODE[t], KCUT[:-1], KCUT[1:]):
                if j <= c0 < z:
                    ia = I(S("AW", 0, FB[2] + 768), S("cA", lo + c0, lo + c1)) if t else I(S("A0"), S("cI", c0, c1))
                    ik = I(S("KW", 0, E), S("cB", lo + c0, lo + c1))
                    o, ag, kg = S("PR", pr + 16 * c0, pr + 16 * c1), S("AG", 16 * c0, 16 * c1), S("KG", 16 * c0, 16 * c1)
                    if md == "a":
                        act(ag, ia); tt(o, ik, ag, O.mult)
                    elif md == "b":
                        act(kg, ik); tt(o, ia, kg, O.mult)
                    elif md == "p":
                        ps = P((4, 3, 2)[MODE[t][:KCUT.index(c0)].count("p")], 0, 16 * (c1 - c0))
                        act(kg, ik); mm(ps, mb("I"), kg, True, True); act(ag, ia); tt(o, ps, ag, O.mult)
                    elif PROD == "tt":
                        act(kg, ik); act(ag, ia); tt(o, ag, kg, O.mult)
                    else:
                        act(kg, ik, scale=-1.0); act(ag, ia, scale=-1.0); scan(o, ag, kg, 0.0, O.min, O.mult)
            if z > TOT:
                mms(P(0, j, z), [(mb("RB"), S("AUX", lo + j, lo + z))] + [(S("BK"), S("PR", pr + 16 * j + k, pr + 16 * z, 16)) for k in range(16)])
            mms(P(1, j, z), [(tk(k), S("PR", pr + 16 * j + k, pr + 16 * z, 16)) for k in range(16)])
            if z == TOT:
                act(S("CUM", 0, z), P(1, 0, z)); mms(P(0, 0, z), [(mb("RB"), S("AUX", lo, lo + z)), (S("L32"), S("CUM", 0, z))])
        tt(S("T1"), P(0), blk("U", t), O.mult); tt(S("HIT"), P(1), S("T1"), O.is_gt)
        if t < R - 2: act(S("CUM", TOT, 256), P(1, TOT, 256))
        mm(P(2), mb("DF"), S("HIT"), True, True)
        nf = (3, 3, 3, 2, 1)[t]
        for f in range(nf):
            tag[0] = ("chain%d", "k%d", "cand%d")[f] % t
            tt(blk("SEL", f), P(2), FX(b, f), O.mult)
        tag[0] = "chain%d" % t
        bn = S("VL", 16 * b, 16 * b + 16)
        mm(P(4, 256, 512), mf("BK"), blk("SEL", 0), True, True); cp(blk("REP", 0), P(4, 256, 512))
        listed(P(3, 0, 16), 0); ts(ut(0), P(3, 0, 16), float(CD), O.add)
        if GVA:
            raised("GV", S("AW"), ut(0), b, 15.0, P(2, 256, 512))
        else:
            tt(blk("GV", 0), I(S("AW"), ut(0)), blk("XT", b), O.min)
        first_wins(0, P(3, 0, 16), 0, ut(1), float(CD))
        cp(I(S("AW"), ut(1)), blk("GV", 2)) if GVA else tt(I(S("AW"), ut(1)), blk("GV", 0), blk("OH", b), O.add)
        if t < R - 1:
            tag[0] = "k%d" % t
            mm(P(4, 256, 512), mf("BK"), blk("SEL", 1), True, True); listed(P(4, 0, 16), 1)
            cp(blk("REP", 1), P(4, 256, 512)); cp(bn, P(4, 0, 16)); ts(ut(2), P(4, 0, 16), -1.0, O.add)
            if GKA:
                raised("GK", S("KW"), ut(2), b, 7.0, P(2, 256, 512))
            else:
                tt(blk("GK", 0), I(S("KW"), ut(2)), blk("C7", b), O.min)
        tag[0] = "chain%d" % t
        swap(fr, [S("LND", LO[i], LO[i] + 256 * (i + 1)) for i in range(3)], [fw(i) for i in range(3)], "a")
        for i in range(3):
            recv(to[i], S("LND", LO[i], LO[i] + 256 * (i + 1)), "a%d" % i)
        for j in (2, 1, 0):
            lnd = [S("LND", LO[i] + 256 * j, LO[i] + 256 * j + 256) for i in (2, 1, 0) if i >= j]
            if t < R - 1:
                mms(P(j), [(mb("N%d" % (3 - j)), blk("XR", j))] * (t > 0) + [(mb("ROT"), xp(j))] + [(mb("I"), x) for x in lnd], False)
                capped(blk("XR", j), P(j), j, XV[j])
            else:
                mms(P(j), [(mb("NRI"), blk("XR", j))] * (3 - j) + [(mb("I"), xp(j))] + [(mb("RINV"), x) for x in lnd], False)
                capped(xp(j), P(j), j, XV[j])
        if t < R - 1:
            swap(to, [fw(j) for j in range(3)], [S("XR", 0, 256 * j + 256) for j in range(3)], "x")
            for j in (2, 1, 0):
                mm(P(j, 256, 512), mb("RINV"), blk("XR", j), True, True)
                act(xp(j), P(j, 256, 512)) if XPW[j] == "A" else cp(xp(j), P(j, 256, 512))
            for i in range(3):
                recv(fr[i], fw(i), "x%d" % i)
            tag[0] = "k%d" % t
            first_wins(1, bn, 3, ut(3), -1.0)
            cp(I(S("KW"), ut(3)), blk("GK", 2)) if GKA else tt(I(S("KW"), ut(3)), blk("GK", 0), blk("OH", b), O.add)
        tag[0] = "lam%d" % t
        for a in range(0, 4096, LAM):
            z = min(a + LAM, 4096)
            scan(S("ST", a, z), S("RG", rg + a, rg + z), S("PR", pr + a, pr + z), 0.0, O.mult, O.add)
        if t == R - 1: last_factor(t)
        if t < R - 2:
            tag[0] = "cand%d" % t
            listed(P(5, 0, 16), 2)
            ts(tn(0), bn, 0.0, O.is_equal, 8192.0, O.mult); tt(tn(1), P(5, 0, 16), tn(0), O.add); tt(tn(2), tn(1), S("DU", 16 * b, 16 * b + 16), O.min)
            ts(ut(4), tn(2), 1408.0, O.add); ts(ut(5), tn(1), 640.0, O.min, float(LB - I0 + 1408), O.add)
            act(S("TMP"), I(il(0, ILN - I0), ut(4))); gcopy(S("IL", LB + lo, LB + lo + 256), S("TMP")); act(S("UC"), I(il(0, ILN - I0), ut(5)))
            for h in range(2):
                mm(P(5, 128 * h, 128 * h + 128), S("CUM", 128 * h, 128 * h + 128), S("D32"), True, True)
            scan(blk("SD", 2), S("RM"), P(5), 0.0, O.add, O.min)
            ts(S("TI"), S("SD", 527, 768, 16), 16.0, O.mult, 15.0, O.add); ts(S("TI"), S("TI"), 15, O.bitwise_and); cp(S("MB"), S("TI"))
            for h in range(2):
                mm(P(5, 128 * h, 128 * h + 128, 1, p8), S("MB", 8 * h, 8 * h + 8), mb("I"), True, True)
            act(S("M8", 0, 256, 1, p8), P(5, 0, 256, 1, p8))
            mms(P(5, 0, 16), [(Y("01", a), S("UC", a, 256, 16)) for a in range(16)]); ts(ut(6), P(5, 0, 16), float(I0), O.add)
            act(S("UP"), I(S("IL", 0, LB), ut(6)))
            mms(P(5), [(GT, S("M8", 0, 256, 1, p8)), (mb("RIV"), S("UP"))]); mms(P(5, 256, 512), [(mb("R45"), S("UP")), (mb("NR45"), own)])
            act(blk("MK", 1), P(5), AF.Abs, kcol, -1.0); floor32(P(5, 256, 512), 2); act(blk("MK", 0), blk("MK", 1), AF.Relu, 1.0, -1.0)
            new = ([(mb("R23"), S("UP"))], [(mb("R6"), S("UP")), (mb("RKB"), own), (mb("I64"), blk("HI", 2))], [(mb("R01"), S("UP"))], [(S("I32"), blk("AB", 2))])
            old = [FX(b, 0), FX(b, 1), FX(b, 2), blk("LG", t)]; out = old[:3] + [blk("LG", t + 2)]
            for fs in ((0, 1), (2, 3) if t == 0 else (3,)):
                w = 256 * len(fs); keep = S("TT", 256 * fs[0], 256 * fs[0] + w)
                for j, f in enumerate(fs):
                    mms(P(5, 256 * j, 256 * j + 256), [(mf("I"), old[f]), (mb("NB"), blk("MK", 0))])
                act(keep, P(5, 0, w)) if FXA else cp(keep, P(5, 0, w))
                for j, f in enumerate(fs):
                    mms(P(5, 256 * j, 256 * j + 256), new[f] + [(mb("NB"), blk("MK", 1))])
                for j, f in enumerate(fs):
                    tt(out[f], P(5, 256 * j, 256 * j + 256), blk("TT", f), O.max)
            ts(blk("cB", b), FX(b, 1), -1.0, O.add); ts(blk("cA", b), FX(b, 0), float(CD), O.add)
    tag[0] = "end"
    mms(P(3, 0, 128), [(Y("23", a), S("PH", a, E, 16)) for a in range(16)]); ts(S("uY"), P(3, 0, 128), float(CD), O.add)
    for j, (a, z) in enumerate(zip(YCUT[:-1], YCUT[1:])):
        o, w = S("RG", 4096 + a, 4096 + z), I(S("AW", 0, FB[0]), S("uY", a // 16, z // 16))
        cp(o, w) if j % 2 == 0 else act(o, w)
        dma("S", T["ya"][:, a:z], o, (z - a) * 1e-3)
    op(None, None, None, [], 0.0, ("end", 0), False, 0.0, [i for i, o in enumerate(ops) if o["dma"]])
    ops = [o for o in arrange(ops) if o["f"] is not None or o["q"] is None]
    emit(g, T, ops)
